import numpy as np, ml_dtypes
CORES = [2,3,42,43,82,83,122,123]
N = 8
import mx_ref
BF = ml_dtypes.bfloat16
def gcols(t, e):
    v = np.concatenate([t.reshape(8, 16, -1, 4), np.zeros((8, 16, 1, 4), BF)], axis=2)
    return np.ascontiguousarray(np.stack([v[g][:, e[g]] for g in range(8)])).reshape(128, -1)
def tile(rs):
    return np.stack(rs, axis=2).reshape(128, -1).astype(BF)
def pick(q, e):
    c = np.concatenate([q[0].reshape(128, -1, 4), np.zeros((128, 1, 4), np.uint8)], axis=1); s = np.concatenate([q[1], np.ones((16, 1), np.uint8)], axis=1)
    return (np.ascontiguousarray(c[:, e].reshape(128, -1)), np.ascontiguousarray(s[:, e]))
def join(*qs):
    return (np.concatenate([q[0] for q in qs], axis=1), np.concatenate([q[1] for q in qs], axis=1))
def put(q, e, v):
    c, s = q[0].reshape(128, -1, 4).copy(), q[1].copy(); c[:, e] = v[0].reshape(128, -1, 4); s[:, e] = v[1]
    return (c.reshape(128, -1), s)
def pk(c, s):
    return (np.ascontiguousarray(c), mx_ref.live(s))
def emit(q):
    return q[0], q[1]
def packed(v, rng):
    q = [mx_ref.quantize(np.ascontiguousarray(v[r])) for r in range(N)]
    return np.stack([a for a, b in q]), np.stack([mx_ref.plane(b, rng) for a, b in q])
def values_of_codes():
    e, c = np.zeros((128, 128, 4), np.float32), np.zeros((128, 2, 4), np.uint8)
    e[np.arange(128), np.arange(128), 0] = 1
    c[:127, :, 0] = np.arange(256).reshape(2, 128).T[:127]
    return mx_ref.matmul(mx_ref.quantize(e.reshape(128, 512).astype(BF)), (c.reshape(128, 8), np.full((16, 2), 127, np.uint8))).T.reshape(-1).astype(np.float64)
CODE_VALUE, SCALE_VALUE = values_of_codes(), 2.0 ** (np.arange(256) - 127.0)
def decode(q):
    return (CODE_VALUE[q[0]].reshape(16, 8, -1, 4) * SCALE_VALUE[q[1]][:, None, :, None] + 0.0).reshape(128, -1).astype(np.float32)
def f(rng, *shape):
    return mx_ref.flush((rng.standard_normal(shape, dtype=np.float32) * np.exp2(rng.integers(-2, 3, shape[:-1] + (1,)))).astype(BF))
def wide(rng, *shape, cols=0):
    v = rng.standard_normal(shape, dtype=np.float32) * np.exp2(rng.integers(-12, 13, shape)).astype(np.float32)
    if cols: v *= np.repeat(np.exp2(rng.integers(-cols, cols + 1, shape[:-2] + (1, shape[-1] // 4))) * (rng.random(shape[:-2] + (1, shape[-1] // 4)) > 0.0625), 4, axis=-1).astype(np.float32)
    return mx_ref.flush(v.astype(BF))
C, A, R = 256, 64, 3
HOP = [1, 2, 3]
def lengths(p):
    z = p + np.float32(0.0)
    return 1 + (z[::16] > 0) + 2 * (z[1::16] > 0)
def walk(n):
    m, k, now = np.zeros((8, N * C + 4), bool), np.zeros((8, N * C), np.int64), np.full(8, -1)
    m[:, 0] = True
    for p in range(N * C):
        if p % C == 0: now = np.full(8, -1)
        now = now + m[:, p]
        k[:, p] = now
        m[np.arange(8), p + n[:, p]] |= m[:, p]
    return m[:, :N * C], k
def big(v):
    v = v.astype(np.float32)
    v[np.abs(v) < np.float32(2.0 ** -16)] = 0
    return v.astype(BF)
def numbers_of(rng):
    return {"x": big(f(rng, N, 128, 4 * C)), "u": np.array(f(rng, N, 128, 512)), "v": np.array(f(rng, N, 128, 512))}
def layers(rng):
    return big(f(rng, N, 128, 2048)).reshape(N, 8, 16, 4, 8, 16, 4)
def weights(rng, w):
    c, p = packed(w.reshape(N, 128, 2048), rng)
    return {"wc": c, "ws": p}
def setup_inputs(rng):
    return {**numbers_of(rng), **weights(rng, layers(rng))}
def setup_inputs_chains(rng):
    d = numbers_of(rng)
    k = rng.permutation(N) % 4
    unit = np.exp2(np.array([-28.0, -10.0, 0.0, 26.0])[k]).astype(np.float32)[:, None, None]
    by = np.exp2(np.array([-30.0, 0.0, 0.0, 30.0])[k]).astype(np.float32).astype(BF)
    o = rng.permutation(8)
    n = np.array([4, 4, 4, 3, 3, 2, 2, 1])[o]
    e = np.zeros((2, N, 8, C), np.float32)
    e[0] = np.where(n % 2 == 0, 8, -8)[None, :, None]
    e[1] = np.where(n > 2, 8, -8)[None, :, None]
    e[0, 0, :, 0] = np.where(o % 2 == 1, -1.0, -0.5)
    e[1, 0, :, 0] = np.where(o == 2, 1.0, 1.5)
    e[1, 1, o == 1, 3] = -8
    e[1, 2, o == 1, 1] = -8
    x = d["x"].reshape(N, 8, 16, C, 4)
    x[:, :, :8] = 0
    x[:, :, 0, :, 0] = (e[0] * unit).astype(BF)
    x[:, :, 1, :, 0] = (e[1] * unit).astype(BF)
    x[:, :, 2, :, 0] = unit.astype(BF)
    u = d["u"].reshape(N, 128, 128, 4)
    u[:, :, ::16] = 0
    u[:, :, 1::16] = 0
    w = layers(rng)
    w[:, :, :8] = 0
    w[:, :, :, :, :, :8] = 0
    for g in range(8):
        u[:, 16 * g, 16 * g, 0] = by
        u[:, 16 * g + 1, 16 * g + 1, 0] = by
        w[:, g, 2, 0, g, 0, 0] = 32
        w[:, g, 2, 0, g, 1, 0] = -32
    return {"x": x.reshape(N, 128, 4 * C), "u": u.reshape(N, 128, 512), "v": d["v"], **weights(rng, w)}
def setup_inputs_copies(rng):
    d = numbers_of(rng)
    o = rng.permutation(N)
    x = d["x"].reshape(N, 8, 16, C, 4)
    for r in range(N):
        k = rng.permutation(C) % 2 if r == o[1] else np.zeros(C, int)
        a = x[r][:, :8, :2].copy()
        x[r][:, :8] = a[:, :, k]
    x[o[0], :, :8] = 0
    u = d["u"].reshape(N, 8, 16, 128, 4)
    u[:, :, 8:, ::16] = 0
    u[:, :, 8:, 1::16] = 0
    w = layers(rng)
    w[:, :, 8:, :, :, :8] = 0
    return {"x": x.reshape(N, 128, 4 * C), "u": u.reshape(N, 128, 512), "v": d["v"], **weights(rng, w)}
def setup_inputs_spread(rng):
    d = setup_inputs(rng)
    d["x"] = big(wide(rng, N, 128, 4 * C, cols=6))
    return d
def check_inputs(d):
    b = []
    for k in ("x", "u", "v"):
        a = np.abs(d[k].astype(np.float32))
        if not (np.isfinite(a).all() and ((a == 0) | (a >= 2.0 ** -30) & (a <= 2.0 ** 30)).all()): b.append("a value of " + k)
    if ((d["wc"] & 127) == 127).any(): b.append("a code of wc is no number")
    for r in range(N):
        a = np.max(np.abs(CODE_VALUE[d["wc"][r]]).reshape(16, 8, 512, 4), axis=(1, 3)) * SCALE_VALUE[mx_ref.live(d["ws"][r])]
        if not ((a == 0) | (a >= 0.875 * 2.0 ** -30) & (a <= 1.125 * 2.0 ** 30)).all(): b.append("the largest size of a block of W")
    return b
def reference(x, u, v, wc, ws):
    qu = [mx_ref.quantize(u[r]) for r in range(N)]
    lay = [pk(wc[r], ws[r]) for r in range(N)]
    now = [x[r] for r in range(N)]
    first = [None] * N
    for t in range(R):
        q = [mx_ref.quantize(now[r]) for r in range(N)]
        n = np.concatenate([lengths(mx_ref.matmul(qu[r], q[r])) for r in range(N)], axis=1)
        mark, body = walk(n)
        for r in range(N):
            own = slice(C * r, C * r + C)
            s = np.argsort(~mark[:, own], axis=1, kind="stable")[:, :A]
            last = np.minimum(s + np.take_along_axis(n[:, own], s, axis=1) - 1, C - 1)
            val = decode(q[r]).astype(BF)
            pack = ((gcols(val, s).astype(np.float32) + gcols(val, last).astype(np.float32)) * np.float32(0.5)).astype(BF)
            sent = mx_ref.quantize(pack)
            w = lay[(r + HOP[t]) % N]
            h = tile([mx_ref.matmul(pick(w, np.arange(128 * b, 128 * b + 128)), sent) * np.float32(0.03125) for b in range(4)])
            came = decode(mx_ref.quantize(h)).astype(BF)
            k = body[:, own]
            now[r] = (now[r].astype(np.float32) + gcols(came, np.where(k < 0, -1, k % A)).astype(np.float32)).astype(BF)
            first[r] = s
    y, ol = np.zeros((N, 128, C), np.float32), np.zeros((N, 8, A), np.float32)
    oc, osc = np.zeros((N, 128, 4 * C), np.uint8), np.zeros((N, 16, C), np.uint8)
    for r in range(N):
        q = mx_ref.quantize(now[r])
        y[r] = mx_ref.matmul(mx_ref.quantize(v[r]), q)
        ol[r] = first[r]
        oc[r], osc[r] = emit(q)
    return {"y": y, "ol": ol, "oc": oc, "osc": osc}

@@ -1,0 +1,548 @@
+from concourse.bass import DstId, RemoteDMATransfer
+from concourse.mybir import dt, AluOpType, AxisListType, ActivationFunctionType
+
+N, C, A, R = 8, 256, 64, 3
+HOP = [1, 2, 3]
+LENT = HOP[1]
+X4, U8, BF, F32, I32, U16 = "float8_e4m3fn_x4", "uint8", "bfloat16", "float32", "int32", "uint16"
+BIG = float(2 ** 24)
+
+
+def _sb(n, d):
+    return ("sbuf", [128, n], d)
+
+
+SCRATCH = {
+    "Tt": _sb(1024, BF), "ut": _sb(512, BF), "vt": _sb(512, BF),
+    "uq": _sb(128, X4), "us": _sb(128, U8), "Uq": _sb(256, X4), "Us": _sb(256, U8),
+    "vq": _sb(128, X4), "vs": _sb(128, U8),
+    "Wq": _sb(512, X4), "Ws": _sb(512, U8), "Wl": _sb(512, X4), "Wm": _sb(512, U8),
+    "Sq": _sb(1792, X4), "Ss": _sb(1792, U8), "Lq": _sb(1536, X4), "Ls": _sb(1536, U8),
+    "Eq": _sb(512, X4), "Es": _sb(512, U8), "Z": _sb(528, BF), "ones": _sb(528, BF),
+    "Vh": _sb(1024, BF), "Vg": _sb(1024, BF), "G": _sb(1024, BF), "Ft": _sb(512, BF), "Ht": _sb(512, BF),
+    "Hd": _sb(320, BF), "ys": _sb(256, F32),
+    "pi": _sb(4, I32), "sc": _sb(32, F32), "pos": _sb(48, F32), "pos4": _sb(16, F32), "tmp": _sb(512, F32),
+    "PU": _sb(512, BF), "PA": _sb(256, BF), "PB": _sb(64, BF), "PC": _sb(256, BF), "PD": _sb(256, BF),
+    "Tab": _sb(1024, BF), "Flg": _sb(1024, BF), "c1": _sb(256, BF), "cE": _sb(48, BF), "cB": _sb(64, BF),
+    "rowa": _sb(16, F32), "rowb": _sb(16, F32), "rowc": _sb(16, F32), "lc": _sb(16, F32),
+    "ul": _sb(16, U16), "El": _sb(12, U16), "Fl": _sb(4, U16), "Pl": _sb(2, U16), "z0": _sb(2, U16),
+    "bits": _sb(512, BF), "su": _sb(512, F32), "cod": _sb(16, U16), "N1": _sb(256, BF), "X1": _sb(256, BF),
+    "s1": _sb(192, F32), "W1": _sb(12, U16), "Rb": _sb(192, BF), "s2": _sb(48, F32), "W2": _sb(6, U16),
+    "Qb": _sb(32, BF), "Pb": _sb(64, BF), "s3": _sb(16, F32), "W3": _sb(2, U16), "mp": _sb(48, F32),
+    "ML": _sb(96, F32), "ch": _sb(144, U16),
+    "AB": _sb(384, BF), "T12": _sb(64, BF), "BB": _sb(96, BF), "T2": _sb(16, BF), "Pp": _sb(16, BF),
+    "s4": _sb(16, F32), "D1": _sb(4, U16), "BC": _sb(64, BF), "s5": _sb(64, F32), "D2": _sb(16, U16),
+    "Pre": _sb(256, BF), "s6": _sb(256, F32), "nr": _sb(256, BF), "s7": _sb(256, F32), "s8": _sb(256, F32),
+    "ck": _sb(16, F32), "lf": _sb(16, F32), "ll": _sb(16, U16), "Kw": _sb(64, F32), "key": _sb(16, U16),
+    "m": _sb(256, BF), "K1": _sb(256, BF), "le": _sb(192, BF), "junk": _sb(368, BF), "sa": _sb(4, F32),
+    "sl": _sb(4, U16), "sf": _sb(4, F32), "s9": _sb(256, F32), "ka": _sb(16, I32), "kb": _sb(16, I32),
+    "kc": _sb(16, I32), "kl": _sb(16, U16),
+    "ps": ("psum", [128, 4096], F32),
+}
+SEMAPHORES = ["ev", "es", "et", "eg", "dx", "du", "dv", "dwa", "dwb", "dwc", "oy", "oz", "sent",
+              "map0", "map1", "map2", "fa0", "fa1", "ha0", "ha1", "wa"]
+
+
+def rank_program(g, core, T, topo):
+    r = T.rank_of(core)
+    if r is None:
+        return
+    AL, AF = AluOpType, ActivationFunctionType
+    cores = T.cores
+    queue = {"v": g.vector, "s": g.scalar, "t": g.tensor, "g": g, "y": g.sync}
+    own = {"v": "ev", "s": "es", "t": "et", "g": "eg"}
+    total, seen, clock = {}, {}, {e: {} for e in queue}
+
+    def V(name, lo, hi, step=1):
+        m = (1 << hi) - (1 << lo) if step == 1 else sum(1 << c for c in range(lo, hi, step))
+        ap = T[name][:, lo:hi] if step == 1 else T[name][:, lo:hi:step]
+        return (ap, [(name, m)])
+
+    def bank(k, n):
+        return (T.ps[:, 512 * k:512 * k + n], [("ps%d" % k, 1)])
+
+    def ind(win, off):
+        return (win[0].indirect(off[0]), win[1] + off[1])
+
+    def col(k):
+        return V("sc", k, k + 1)
+
+    def wait_for(e, reads, writes):
+        need = {}
+        for regs, wr in ((reads, False), (writes, True)):
+            for name, m in regs:
+                for am, aw, sem, val, snap, ae in seen.get(name, []):
+                    if not am & m:
+                        continue
+                    if name.startswith("ps"):
+                        if ae == e:
+                            continue
+                    elif not (aw or wr):
+                        continue
+                    if val > need.get(sem, (0, None))[0]:
+                        need[sem] = (val, snap)
+        for sem in list(need):
+            if any(o != sem and need[o][1].get(sem, 0) >= need[sem][0] for o in need):
+                del need[sem]
+        for sem, (val, snap) in need.items():
+            if clock[e].get(sem, 0) < val:
+                queue[e].wait_ge(T.sem[sem], val)
+            for k, x in snap.items():
+                clock[e][k] = max(clock[e].get(k, 0), x)
+
+    def note(e, reads, writes, sem, val):
+        snap = dict(clock[e]) if e else {}
+        snap[sem] = val
+        for name, m in writes:
+            seen[name] = [a for a in seen.get(name, []) if a[0] & ~m] + [(m, True, sem, val, snap, e)]
+        for name, m in reads:
+            seen.setdefault(name, []).append((m, False, sem, val, snap, e))
+
+    def issue(e, make, outs, ins, sem=None):
+        reads = [x for a in ins if isinstance(a, tuple) for x in a[1]]
+        writes = [x for a in outs for x in a[1]]
+        wait_for(e, reads, writes)
+        inc = 16 if sem else 1
+        sem = sem or own[e]
+        total[sem] = total.get(sem, 0) + inc
+        make().then_inc(T.sem[sem], inc)
+        note(e, reads, writes, sem, total[sem])
+
+    def ap(a):
+        return a[0] if isinstance(a, tuple) else a
+
+    def ts(out, in0, s1, op0, s2=None, op1=None):
+        if op1 is None:
+            issue("v", lambda: g.vector.tensor_scalar(out[0], in0[0], ap(s1), None, op0), [out], [in0, s1])
+        else:
+            issue("v", lambda: g.vector.tensor_scalar(out[0], in0[0], ap(s1), ap(s2), op0, op1), [out], [in0, s1, s2])
+
+    def tt(out, a, b, op):
+        issue("v", lambda: g.vector.tensor_tensor(out[0], a[0], b[0], op), [out], [a, b])
+
+    def cp(out, a, e="v", scale=None):
+        if e == "v" and scale is None:
+            issue("v", lambda: g.vector.tensor_copy(out[0], a[0]), [out], [a])
+        elif e == "v":
+            ts(out, a, scale, AL.mult)
+        elif scale is None:
+            issue("s", lambda: g.scalar.activation(out[0], a[0], AF.Copy), [out], [a])
+        else:
+            issue("s", lambda: g.scalar.activation(out[0], a[0], AF.Copy, scale=scale), [out], [a])
+
+    def affine(out, a, scale, bias):
+        issue("s", lambda: g.scalar.activation(out[0], a[0], AF.Identity, bias=ap(bias), scale=scale), [out], [a, bias])
+
+    def fill(out, x):
+        issue("v", lambda: g.vector.memset(out[0], x), [out], [])
+
+    def sfill(name, lo, hi, step, x):
+        cp(V(name, lo, hi, step), V("ones", 0, len(range(lo, hi, step))), "s", float(x))
+
+    def scan(out, d0, d1, op0, op1):
+        issue("v", lambda: g.vector.tensor_tensor_scan(out[0], d0[0], d1[0], 0.0, op0, op1), [out], [d0, d1])
+
+    def pickup(out, pat, row):
+        scan(out, pat, row, AL.add, AL.min)
+
+    def quant(q, s, lo, n, tile):
+        a, b = V(q, lo, lo + n), V(s, lo, lo + n)
+        issue("v", lambda: g.vector.quantize_mx(a[0], b[0], tile[0]), [a, b], [tile])
+
+    def mm(k, n, wq, ws, wlo, xq, xs, xlo):
+        o, a, b = bank(k, n), V(wq, wlo, wlo + 128), V(ws, wlo, wlo + 128)
+        c, d = V(xq, xlo, xlo + n), V(xs, xlo, xlo + n)
+        issue("t", lambda: g.tensor.matmul_mx(o[0], a[0], b[0], c[0], d[0], True, True), [o], [a, b, c, d])
+
+    def iota(out, pattern, base=0, cm=0, whole=False):
+        if whole:
+            issue("g", lambda: g.iota(out[0], pattern, base, cm), [out], [])
+        else:
+            issue("g", lambda: g.iota(out[0], pattern, base, cm, allow_small_or_imprecise_dtypes=True), [out], [])
+
+    def dma(e, out, in_, sem):
+        issue(e, lambda: queue[e].dma_start(ap(out), ap(in_)), [out] if isinstance(out, tuple) else [], [in_], sem)
+
+    def u8(a):
+        return (a[0].bitcast(dt.uint8), a[1])
+
+    def double(name, n, upto):
+        while n < upto:
+            cp(V(name, n, 2 * n), V(name, 0, n), "s")
+            n *= 2
+
+    def near(a, b):
+        return topo.chip(cores[a]) == topo.chip(cores[b])
+
+    def far_engines(a):
+        es = None
+        for b in range(N):
+            if b != a:
+                es = [e for e in topo.engines(cores[a], cores[b]) if es is None or e in es]
+        return es
+
+    def lanes(a, b):
+        return topo.engines(cores[a], cores[b])
+
+    def dst_id(c):
+        rid, pid, _ = topo.addr(c)
+        return DstId(rid=rid, pnc=pid)
+
+    def push(parts):
+        wait_for("g", [x for p in parts for x in p[0][1]], [])
+        g.remote_dma_fused([RemoteDMATransfer(dst_ids=[dst_id(cores[q]) for q in to],
+                                              dma_engine_mask=sum(1 << e for e in es),
+                                              remote_sem=T.sem[sem], src=src[0], dsts=[land[0] for q in to])
+                            for src, to, land, es, sem in parts], local_sem=T.sem.sent)
+        total["sent"] = total.get("sent", 0) + sum(len(p[3]) for p in parts)
+
+    def map_plan(q, t):
+        later = list(range(N - 1, q, -1))
+        here = [p for p in later if near(p, q)] if t else []
+        plan = [([p for p in later if p not in here], far_engines(q))]
+        plan += [([p], [e for e in lanes(q, p) if e not in far_engines(q)]) for p in here]
+        return [x for x in plan if x[0]]
+
+    def holder(q, t):
+        w = (q + HOP[t]) % N
+        for p in ((w - LENT) % N, w):
+            if p == q or near(p, q):
+                return p
+        return w
+
+    def arrives(sem, n, views):
+        total[sem] = n
+        note(None, [], [x for a in views for x in a[1]], sem, n)
+
+    def send_tile(base, to, stage, sem):
+        x, es = 384 * stage + 192, lanes(r, to)
+        push([(u8(V("Sq", base, base + 64)), [to], u8(V("Lq", x, x + 64)), es[:len(es) // 2], sem),
+              (V("Ss", base - 192, base + 64), [to], V("Ls", x - 192, x + 64), es[len(es) // 2:], sem)])
+
+    def landed(sem, stage, frm):
+        x = 384 * stage + 192
+        arrives(sem, len(lanes(frm, r)), [V("Lq", x, x + 64), V("Ls", x - 192, x + 64)])
+
+    for t in range(R):
+        n = sum(len(es) for q in range(r) for to, es in map_plan(q, t) if r in to)
+        if n:
+            arrives("map%d" % t, n, [V("ML", 32 * t, 32 * t + 4 * r)])
+    away = [t for t in range(R) if holder(r, t) != r]
+    guest = {t: [q for q in range(N) if holder(q, t) == r][0] for t in range(R)}
+    for k, t in enumerate(away):
+        landed("fa%d" % k, 2 * k, guest[t])
+        landed("ha%d" % k, 2 * k + 1, holder(r, t))
+    arrives("wa", 2 * len(far_engines((r + LENT) % N)), [V("Wl", 0, 512), V("Wm", 0, 512)])
+    wto, far = (r - LENT) % N, far_engines(r)
+    soon = (guest[0] + HOP[0]) % N == r and holder((r - HOP[0]) % N, 0) == r
+
+    dma("y", V("Tt", 0, 1024), T.x[:], "dx")
+    dma("s", V("ut", 0, 512), T.u[:], "du")
+    dma("y", V("Ws", 0, 512), T.ws[:], "dwa")
+    dma("y", u8(V("Wq", 0, 128)), T.wc[:, 0:512], "dwb")
+    dma("y", u8(V("Wq", 128, 512)), T.wc[:, 512:2048], "dwc")
+    dma("y", V("vt", 0, 512), T.v[:], "dv")
+
+    cI, cLO, cHI, cSW, cL8, cAA, cMU, cAU, cM3 = range(9)
+    cH4, cH1, cAC, cW, cA1, cA2, cAK, cSE, cS4, cK1, cK2, cK3, cT0, cT1, cT2 = range(9, 24)
+    iota(V("pi", 0, 1), [[0, 1]], 0, 1, True)
+    iota(V("pos", 0, 48), [[1, 48]], -8)
+    iota(V("rowa", 0, 16), [[1, 2], [16, 8]])
+    iota(V("Tab", 768, 1024), [[0, 64], [4, 4]])
+    iota(V("Tab", 512, 768), [[0, 16], [4, 4], [0, 4]], -4)
+    iota(V("pos4", 0, 16), [[0, 4], [1, 4]])
+    iota(V("rowb", 0, 12), [[1, 3], [64, 4]])
+    fill(V("ones", 0, 528), 1.0)
+    ts(V("pi", 1, 2), V("pi", 0, 1), 15, AL.bitwise_and)
+    ts(V("pi", 2, 3), V("pi", 0, 1), 3, AL.bitwise_and)
+    ts(V("pi", 3, 4), V("pi", 0, 1), 2, AL.arith_shift_right, 3, AL.bitwise_and)
+    fill(V("Ft", 256, 512), 0.0)
+    cp(V("sc", 0, 3), V("pi", 1, 4))
+    iota(V("c1", 3, 256, 4), [[1, 4], [0, 16]])
+    iota(V("c1", 0, 256, 4), [[16, 4], [1, 4], [0, 4]])
+    iota(V("c1", 1, 256, 4), [[16, 4], [1, 4], [0, 4]])
+    iota(V("c1", 2, 256, 4), [[16, 16], [0, 4]], 3)
+    iota(V("AB", 0, 64), [[0, 4], [4, 4], [0, 4]])
+    iota(V("rowc", 0, 16), [[16, 16]], -1)
+    iota(V("BB", 0, 16), [[0, 4], [4, 4]])
+    iota(V("Pb", 0, 16), [[0, 4], [4, 4]])
+    iota(V("cE", 0, 16), [[1, 4], [0, 4]])
+    iota(V("cE", 16, 32), [[0, 4], [1, 4]])
+    iota(V("cE", 32, 48), [[0, 4], [16, 4]], 3)
+    ts(col(cL8), col(cLO), 8.0, AL.mult)
+    ts(col(cSW), col(cLO), 4.0, AL.mult, col(cHI), AL.add)
+    ts(col(cH4), col(cHI), 4.0, AL.mult)
+    ts(col(cAA), col(cI), 15.0, AL.is_lt, 256.0, AL.mult)
+    ts(col(cAC), col(cHI), 3.0, AL.is_lt, 256.0, AL.mult)
+    ts(col(cT0), col(cLO), 2.0, AL.is_ge, 2.0, AL.mult)
+    ts(col(cMU), col(cLO), 3.0, AL.is_equal, 1.0 / BIG, AL.max)
+    ts(col(cM3), col(cHI), 3.0, AL.is_lt, 0.25, AL.mult)
+    ts(col(cAU), col(cHI), 256.0, AL.mult, -85.0, AL.add)
+    ts(col(cH1), col(cHI), 1.0, AL.add)
+    cp(V("ul", 0, 16), V("rowa", 0, 16))
+    cp(col(cS4), col(cSW), "s", 4.0)
+    affine(col(cW), col(cLO), 1.0, col(cT0))
+    affine(col(cT1), col(cLO), 1.0, col(cAC))
+    affine(col(cT2), col(cI), 1.0, col(cAA))
+    affine(col(cA1), col(cW), 16.0, col(cAC))
+    affine(col(cA2), col(cW), 64.0, col(cAC))
+
+    def horner(name, n, start, fours, stop, o):
+        ts(V("tmp", o, o + 48), V("pos", 0, 48), start, AL.is_equal)
+        at = lambda k: V("tmp", o + 8 - k, o + 8 - k + n)
+        acc, top = V("tmp", o + 64, o + 64 + n), V("tmp", o + 96, o + 96 + n)
+        ts(top, at(stop), BIG, AL.mult)
+        tt(acc, at(fours[0]), at(fours[1]), AL.add)
+        for k in fours[2:]:
+            tt(acc, acc, at(k), AL.add)
+        ts(acc, acc, 3.0, AL.mult, 1.0, AL.add)
+        tt(acc, acc, at(0), AL.subtract)
+        tt(V(name, 0, n), acc, top, AL.max)
+
+    def marks(name, a, sa, b, sb, at):
+        ts(V("tmp", at, at + 16), a, sa, AL.is_equal, 512.0, AL.mult)
+        ts(V("tmp", at + 16, at + 32), b, sb, AL.is_equal, 256.0, AL.mult)
+        tt(V(name, 0, 16), V("tmp", at, at + 16), V("tmp", at + 16, at + 32), AL.subtract)
+
+    horner("PU", 32, col(cL8), [2, 4, 6], 8, 0)
+    marks("PB", V("pos", 8, 24), col(cSW), V("pos", 7, 23), col(cSW), 256)
+    marks("PA", V("pos", 8, 24), col(cI), V("pos", 7, 23), col(cI), 288)
+    marks("PC", V("pos4", 0, 16), col(cHI), V("pos4", 0, 16), col(cH1), 320)
+    sfill("Tab", 288, 304, 1, 0)
+    sfill("Tab", 304, 320, 1, 4)
+    sfill("Tab", 192, 256, 1, 0)
+    cp(V("Tab", 272, 288), V("Tab", 768, 784), "s")
+    cp(V("Tab", 128, 192), V("Tab", 768, 832), "s")
+    double("PU", 32, 512)
+    for k in range(4):
+        sfill("Tab", 512 + k, 768, 16, 4 * k)
+    ts(V("El", 0, 12), V("rowb", 0, 12), col(cS4), AL.add)
+    quant("uq", "us", 0, 128, V("ut", 0, 512))
+    a, b, o = V("Uq", 0, 256), V("uq", 0, 128), V("ul", 0, 16)
+    issue("v", lambda: g.vector.tensor_copy(a[0].bitcast(dt.uint32), b[0].bitcast(dt.uint32).indirect(o[0])), [a], [b, o])
+    cp(V("Us", 0, 256), ind(V("us", 0, 128), V("ul", 0, 16)), "s")
+    cp(V("Tab", 256, 272), V("Tab", 512, 528), "s")
+    cp(V("Tab", 64, 128), V("Tab", 512, 576), "s")
+    cp(V("Tab", 0, 64), V("Tab", 256, 320), "s")
+    cp(V("Tab", 320, 384), V("Tab", 256, 320), "s")
+    for z in range(4):
+        sfill("c1", 64 * z + 35, 64 * z + 48, 4, 16 * z + 3)
+        sfill("c1", 64 * z + 51, 64 * z + 64, 4, 16 * (z + 1) if z < 3 else 16 * (r + 1))
+    cp(V("Tab", 384, 512), V("Tab", 256, 384), "s")
+    double("PB", 16, 64)
+    h = len(far) // 2
+    push([(V("Ws", 0, 512), [wto], V("Wm", 0, 512), far[:h], "wa"),
+          (u8(V("Wq", 0, 128)), [wto], u8(V("Wl", 0, 128)), far[h:], "wa")])
+    issue("g", lambda: g.affine_select(T.Z[:, 0:516], T.ones[:, 0:516], [[1, 516]], AL.is_equal, 0.0, -3, -4),
+          [V("Z", 0, 516)], [V("ones", 0, 516)])
+    iota(V("cB", 0, 64), [[0, 4], [16, 4], [1, 4]])
+
+    def rest_of_w():
+        push([(u8(V("Wq", 128, 512)), [wto], u8(V("Wl", 128, 512)), far, "wa")])
+
+    def flag_table():
+        def one(e, t, lo, hi, step=1):
+            sfill("Flg", 16 * lo + 4 * e + t, 16 * (hi - 1) + 4 * e + t + 1, 16 * step, 1)
+        sfill("Flg", 0, 512, 1, 0)
+        sfill("Flg", 512, 1024, 1, 0)
+        for e in range(4):
+            one(e, e, 0, 64)
+        one(0, 1, 0, 16)
+        one(2, 3, 0, 64, 4)
+        one(0, 2, 16, 32)
+        one(0, 2, 0, 4)
+        one(1, 3, 0, 64, 16)
+        one(0, 3, 32, 48)
+        one(0, 3, 16, 32, 4)
+        one(0, 3, 4, 8)
+        one(0, 3, 0, 1)
+        for k in range(4):
+            one(1, 2, k, 64, 16)
+            one(1, 3, 4 + k, 64, 16)
+
+    for t in range(R):
+        qt, qf, qh = 512 * t, 512 * t + 256, 512 * t + 384
+        for h in range(2):
+            quant("Sq", "Ss", qt + 128 * h, 128, V("Tt", 512 * h, 512 * h + 512))
+            mm(6 * h + 1, 128, "Uq", "Us", 128, "Sq", "Ss", qt + 128 * h)
+            mm(6 * h, 128, "Uq", "Us", 0, "Sq", "Ss", qt + 128 * h)
+        for h in range(2):
+            ts(V("bits", 256 * h, 256 * h + 256, 2), bank(6 * h + 1, 128), 0.0, AL.is_gt, 2.0, AL.mult)
+            ts(V("bits", 256 * h + 1, 256 * h + 256, 2), bank(6 * h, 128), 0.0, AL.is_gt, 1.0, AL.add)
+
+        def unpack(e):
+            for b in range(4):
+                if e == "t":
+                    mm(2 + b, 256, "Eq", "Es", 128 * b, "Sq", "Ss", qt)
+                else:
+                    cp(V("Vh", 256 * b, 256 * b + 256), bank(2 + b, 256), "s", 0.5)
+                    cp(V("Vg", 256 * b, 256 * b + 256), bank(2 + b, 256), "s", 0.5)
+        if t:
+            unpack("t")
+        else:
+            double("PA", 16, 256)
+        scan(V("su", 0, 512), V("PU", 0, 512), V("bits", 0, 512), AL.mult, AL.add)
+        ts(V("cod", 0, 16), V("su", 31, 512, 32), col(cMU), AL.mult, col(cAU), AL.add)
+        tt(V("N1", 0, 256), ind(V("Tab", 0, 1024), V("cod", 0, 16)), V("c1", 0, 256), AL.add)
+        cp(V("X1", 0, 256), ind(V("Tab", 0, 1024), V("cod", 0, 16)), "s")
+        cp(V("AB", 64, 256), ind(V("X1", 0, 256), V("El", 0, 12)), "s")
+        for u in (2, 1, 0):
+            pickup(V("s1", 64 * u, 64 * u + 64), V("PB", 0, 64), V("N1", u, 256, 4))
+        ts(V("W1", 0, 12), V("s1", 15, 192, 16), col(cAA), AL.add)
+        cp(V("Rb", 0, 64), ind(V("N1", 0, 256), V("W1", 8, 12)))
+        cp(V("Rb", 64, 128), ind(V("Rb", 0, 64), V("W1", 4, 8)))
+        cp(V("Rb", 128, 192), ind(V("Rb", 64, 128), V("W1", 0, 4)))
+        cp(V("T12", 0, 64), ind(V("AB", 192, 256), V("W1", 4, 8)), "s")
+        cp(V("AB", 256, 320), ind(V("AB", 128, 192), V("W1", 0, 4)), "s")
+        cp(V("AB", 320, 384), ind(V("T12", 0, 64), V("W1", 0, 4)), "s")
+        if t == 0:
+            double("PC", 16, 256)
+            affine(V("lc", 0, 16), V("rowc", 0, 16), 1.0, col(cT2))
+            flag_table()
+        else:
+            unpack("s")
+        for v in (2, 1, 0):
+            pickup(V("s2", 16 * v, 16 * v + 16), V("PB" if v else "PA", 0, 16), V("Rb", 128 + v, 192, 4))
+        ts(V("W2", 0, 6, 2), V("s2", 15, 48, 16), col(cAA), AL.add)
+        cp(V("Qb", 0, 16), ind(V("Rb", 128, 192), V("W2", 4, 5)))
+        cp(V("Qb", 16, 32), ind(V("Qb", 0, 16), V("W2", 2, 3)))
+        cp(V("Pb", 16, 32), ind(V("Qb", 16, 32), V("W2", 0, 1)))
+        pickup(V("s3", 0, 16), V("PA", 0, 16), V("Pb", 16, 32))
+        ts(V("W3", 0, 1), V("s3", 15, 16), col(cAA), AL.add, col(cM3), AL.mult)
+        cp(V("Pb", 32, 48), ind(V("Pb", 16, 32), V("W3", 0, 1)))
+        cp(V("Pb", 48, 64), ind(V("Pb", 32, 48), V("W3", 0, 1)))
+        if r < N - 1:
+            cp(V("mp", 16 * t, 16 * t + 16), ind(V("Pb", 48, 64), V("W3", 0, 1)))
+            push([(V("mp", 16 * t, 16 * t + 4), to, V("ML", 32 * t + 4 * r, 32 * t + 4 * r + 4), es, "map%d" % t)
+                  for to, es in map_plan(r, t)])
+        if t == 0:
+            if not soon:
+                rest_of_w()
+            for b in range(4):
+                quant("Eq", "Es", 128 * b, 128, V("Z", 3 - b, 515 - b))
+            unpack("t")
+            horner("PD", 16, col(cH4), [1, 2], 3, 128)
+            double("PD", 16, 256)
+            unpack("s")
+            ts(V("Fl", 0, 1), col(cI), 4.0, AL.mult)
+            ts(V("Fl", 1, 2), col(cSW), 4.0, AL.mult, 1.0, AL.add)
+            ts(V("Fl", 2, 3), col(cSW), 4.0, AL.mult, 2.0, AL.add)
+            ts(V("Pl", 0, 1), col(cLO), 16.0, AL.mult, col(cHI), AL.add)
+            ts(col(cAK), col(cT1), -336.0, AL.add)
+        tt(V("nr", 0, 256), V("bits", 0, 512, 2), V("bits", 1, 512, 2), AL.add)
+        tt(V("BB", 16, 64), ind(V("Rb", 128, 192), V("Fl", 0, 3)), V("cE", 0, 48), AL.subtract)
+        ts(V("Pp", 0, 16), ind(V("Pb", 0, 64), V("Pl", 0, 1)), 0.25, AL.mult)
+        pickup(V("s7", 0, 256), V("PA", 0, 256), V("nr", 0, 256))
+        cp(V("T2", 0, 16), ind(V("BB", 48, 64), V("W2", 2, 3)))
+        cp(V("BB", 64, 80), ind(V("BB", 32, 48), V("W2", 0, 1)))
+        pickup(V("s4", 0, 16), V("PC", 0, 16), V("Pp", 0, 16))
+        tt(V("lf", 0, 16), V("s7", 15, 256, 16), V("lc", 0, 16), AL.add)
+        cp(V("BB", 80, 96), ind(V("T2", 0, 16), V("W2", 0, 1)))
+        ts(V("D1", 0, 4), V("s4", 3, 16, 4), col(cA1), AL.add)
+        ts(V("ll", 0, 16), V("lf", 0, 16), 255.0, AL.min)
+        tt(V("BC", 0, 64), ind(V("BB", 0, 96), V("D1", 0, 4)), V("cB", 0, 64), AL.add)
+        scan(V("s8", 0, 256), V("PD", 0, 256), V("nr", 0, 256), AL.mult, AL.add)
+        pickup(V("s5", 0, 64), V("PC", 0, 64), V("BC", 0, 64))
+        ts(V("ck", 0, 16), V("s8", 15, 256, 16), 16.0 / BIG, AL.mult, col(cAK), AL.add)
+        ts(V("D2", 0, 16), V("s5", 3, 64, 4), col(cA2), AL.add)
+        cp(V("Pre", 0, 256), ind(V("AB", 0, 384), V("D2", 0, 16)), "s")
+        if t == 0:
+            ts(col(cSE), col(cI), -64.0 * r, AL.add)
+            ts(col(cK1), col(cI), 16.0, AL.add)
+            ts(col(cK2), col(cI), 32.5, AL.add)
+            ts(col(cK3), col(cI), 48.5, AL.add)
+            fill(V("z0", 0, 2), 0)
+            if r == 0:
+                cp(V("ch", 128, 129), col(cI))
+        for b in range(4):
+            tt(V("G", 256 * b, 256 * b + 256), ind(V("Vh", 256 * b, 256 * b + 256), V("ll", 0, 16)),
+               V("Vg", 256 * b, 256 * b + 256), AL.add)
+            if b == 1:
+                pickup(V("s6", 0, 256), V("PC", 0, 256), V("Pre", 0, 256))
+            if b == 2:
+                for e in range(4):
+                    tt(V("Kw", 16 * e, 16 * e + 16), V("s6", 64 * e + 3, 64 * e + 64, 4), V("ck", 0, 16), AL.add)
+        for q in range(r):
+            src = ind(V("ML", 32 * t, 32 * t + 4 * r), V("ch", 16 * q - 16, 16 * q - 15) if q else V("z0", 0, 1))
+            if q < r - 1:
+                ts(V("ch", 16 * q, 16 * q + 16), src, 0.25, AL.mult)
+            else:
+                ts(V("ch", 128, 144), src, 4.0, AL.mult, col(cSE), AL.add)
+        cp(V("key", 0, 16), ind(V("Kw", 0, 64), V("ch", 128, 129)))
+        cp(V("m", 0, 256), ind(V("Flg", 0, 1024), V("key", 0, 16)))
+        scan(V("K1", 0, 256), V("ones", 0, 256), V("m", 0, 256), AL.mult, AL.add)
+        for c, lo, hi, at in ((3, 48, 256, 0), (2, 32, 192, 208)):
+            o, s, k, bias = V("junk", at, at + hi - lo), V("sa", c, c + 1), V("K1", lo, hi), col(cK3 if c == 3 else cK2)
+            issue("s", lambda: g.scalar.activation(o[0], k[0], AF.Sign, bias=bias[0], scale=-1.0, accum_out=s[0]),
+                  [o, s], [k, bias])
+        ts(V("le", 64, 192), V("K1", 0, 128), col(cK1), AL.is_le)
+        ts(V("le", 0, 64), V("K1", 0, 64), col(cI), AL.is_le)
+        for c, lo, hi in ((1, 64, 192), (0, 0, 64)):
+            o, k = V("sa", c, c + 1), V("le", lo, hi)
+            issue("v", lambda: g.vector.tensor_reduce(o[0], k[0], AxisListType.X, AL.add), [o], [k])
+        ts(V("sl", 3, 4), V("sa", 3, 4), 0.5, AL.mult, 152.0, AL.add)
+        cp(V("sl", 0, 2), V("sa", 0, 2))
+        ts(V("sl", 2, 3), V("sa", 2, 3), 0.5, AL.mult, 112.0, AL.add)
+        for b in range(4):
+            cp(V("Ft", b, 256, 4), ind(V("G", 256 * b, 256 * b + 256), V("sl", 0, 4)), "vs"[b % 2])
+        quant("Sq", "Ss", qf, 128, V("Ft", 0, 512))
+        k = away.index(t) if t in away else None
+        if k is not None:
+            send_tile(qf, holder(r, t), 2 * k, "fa%d" % k)
+        if t == 0:
+            fill(V("Ht", 0, 512), 0.0)
+            for st in range(4):
+                quant("Lq", "Ls", 384 * st + 256, 128, V("Ht", 0, 512))
+            fill(V("Hd", 0, 320, 80), 0.0)
+            quant("vq", "vs", 0, 128, V("vt", 0, 512))
+        if t == R - 1:
+            cp(V("sf", 0, 4), V("sl", 0, 4))
+            for c in range(4):
+                dma("y", T.ol[:, 16 * c:16 * c + 16], V("sf", c, c + 1), "oy")
+        wq, ws = ("Wq", "Ws") if (guest[t] + HOP[t]) % N == r else ("Wl", "Wm")
+        for b in range(4):
+            if k is None:
+                mm(2 + b, 128, wq, ws, 128 * b, "Sq", "Ss", qf)
+            else:
+                mm(2 + b, 128, wq, ws, 128 * b, "Lq", "Ls", 768 * k + 192)
+        steps = [lambda: pickup(V("s9", 0, 256), V("PA", 0, 256), V("K1", 0, 256)),
+                 lambda: ts(V("ka", 0, 16), V("s9", 15, 256, 16), col(cAA), AL.add, -1.0, AL.add),
+                 lambda: ts(V("kb", 0, 16), V("ka", 0, 16), 63, AL.bitwise_and),
+                 lambda: tt(V("kc", 0, 16), V("ka", 0, 16), V("kb", 0, 16), AL.min),
+                 lambda: ts(V("kl", 0, 16), V("kc", 0, 16), 1.0, AL.add)]
+        cut = 1 if k is None else 5
+        for s in steps[:cut]:
+            s()
+        for b in range(4):
+            cp(V("Ht", b, 256, 4), bank(2 + b, 64), "sv"[b % 2], 0.03125)
+        quant("Sq", "Ss", qh, 128, V("Ht", 0, 512))
+        if k is not None:
+            send_tile(qh, guest[t], 2 * k + 1, "ha%d" % k)
+        if t == 0 and soon:
+            rest_of_w()
+        banks = (0, 1, 6, 7)
+        for b in range(4):
+            if k is None:
+                mm(banks[b], 128, "Eq", "Es", 128 * b, "Sq", "Ss", qh)
+            else:
+                mm(banks[b], 128, "Eq", "Es", 128 * b, "Lq", "Ls", 768 * k + 576)
+        for s in steps[cut:]:
+            s()
+        for b in range(4):
+            cp(V("Hd", 80 * b + 1, 80 * b + 65), bank(banks[b], 64), "s" if b or k is None else "v")
+        for b in range(4):
+            w = V("Tt", b, 1024, 4)
+            tt(w, ind(V("Hd", 80 * b, 80 * b + 65), V("kl", 0, 16)), w, AL.add)
+    qt = 512 * R
+    for h in range(2):
+        quant("Sq", "Ss", qt + 128 * h, 128, V("Tt", 512 * h, 512 * h + 512))
+        mm(2 + h, 128, "vq", "vs", 0, "Sq", "Ss", qt + 128 * h)
+    dma("y", T.oc[:], u8(V("Sq", qt, qt + 256)), "oy")
+    for h in range(2):
+        cp(V("ys", 128 * h, 128 * h + 128), bank(2 + h, 128))
+    for k in range(4):
+        src = (T.Ss[32 * k:32 * k + 4, qt:qt + 256], V("Ss", qt, qt + 256)[1])
+        dma("s", T.osc[4 * k:4 * k + 4, :], src, "oz")
+    dma("y", T.y[:], V("ys", 0, 256), "oy")
+    for sem, n in total.items():
+        g.wait_ge(T.sem[sem], n)

@@ -6,6 +6,7 @@ HOP = [1, 2, 3]
 LENT = HOP[1]
 X4, U8, BF, F32, I32, U16 = "float8_e4m3fn_x4", "uint8", "bfloat16", "float32", "int32", "uint16"
 BIG = float(2 ** 24)
+WAIT, FLIGHT, LOAD, SLACK = 0.2, 3.5, 2.5, 0.08
 
 
 def _sb(n, d):
@@ -20,7 +21,7 @@ SCRATCH = {
     "Sq": _sb(1792, X4), "Ss": _sb(1792, U8), "Lq": _sb(1536, X4), "Ls": _sb(1536, U8),
     "Eq": _sb(512, X4), "Es": _sb(512, U8), "Z": _sb(528, BF), "ones": _sb(528, BF),
     "Vh": _sb(1024, BF), "Vg": _sb(1024, BF), "G": _sb(1024, BF), "Ft": _sb(512, BF), "Ht": _sb(512, BF),
-    "Hd": _sb(320, BF), "ys": _sb(256, F32),
+    "Hd": _sb(320, BF), "ys": _sb(256, F32), "zt": _sb(512, BF),
     "pi": _sb(4, I32), "sc": _sb(32, F32), "pos": _sb(48, F32), "pos4": _sb(16, F32), "tmp": _sb(512, F32),
     "PU": _sb(512, BF), "PA": _sb(256, BF), "PB": _sb(64, BF), "PC": _sb(256, BF), "PD": _sb(256, BF),
     "Tab": _sb(1024, BF), "Flg": _sb(1024, BF), "c1": _sb(256, BF), "cE": _sb(48, BF), "cB": _sb(64, BF),
@@ -39,8 +40,8 @@ SCRATCH = {
     "kc": _sb(16, I32), "kl": _sb(16, U16),
     "ps": ("psum", [128, 4096], F32),
 }
-SEMAPHORES = ["ev", "es", "et", "eg", "dx", "du", "dv", "dwa", "dwb", "dwc", "oy", "oz", "sent",
-              "map0", "map1", "map2", "fa0", "fa1", "ha0", "ha1", "wa"]
+SEMAPHORES = ["ev", "es", "et", "eg", "dx", "du", "dv", "dwa", "dwb", "oy", "oz", "sent",
+              "fa0", "fa1", "ha0", "ha1", "wa"] + ["map%d_%d" % (t, q) for t in range(R) for q in range(N - 1)]
 
 
 def rank_program(g, core, T, topo):
@@ -52,17 +53,18 @@ def rank_program(g, core, T, topo):
     queue = {"v": g.vector, "s": g.scalar, "t": g.tensor, "g": g, "y": g.sync}
     own = {"v": "ev", "s": "es", "t": "et", "g": "eg"}
     total, seen, clock = {}, {}, {e: {} for e in queue}
+    ops, touched, landing, anchor, chain = [], {}, [], {}, {}
 
     def V(name, lo, hi, step=1):
         m = (1 << hi) - (1 << lo) if step == 1 else sum(1 << c for c in range(lo, hi, step))
         ap = T[name][:, lo:hi] if step == 1 else T[name][:, lo:hi:step]
-        return (ap, [(name, m)])
+        return (ap, [(name, m)], len(range(lo, hi, step)), 0)
 
     def bank(k, n):
-        return (T.ps[:, 512 * k:512 * k + n], [("ps%d" % k, 1)])
+        return (T.ps[:, 512 * k:512 * k + n], [("ps%d" % k, 1)], n, 0)
 
     def ind(win, off):
-        return (win[0].indirect(off[0]), win[1] + off[1])
+        return (win[0].indirect(off[0]), win[1] + off[1], 16 * off[2], 1)
 
     def col(k):
         return V("sc", k, k + 1)
@@ -98,15 +100,76 @@ def rank_program(g, core, T, topo):
         for name, m in reads:
             seen.setdefault(name, []).append((m, False, sem, val, snap, e))
 
-    def issue(e, make, outs, ins, sem=None):
-        reads = [x for a in ins if isinstance(a, tuple) for x in a[1]]
-        writes = [x for a in outs for x in a[1]]
+    def issue(e, make, outs, ins, sem=None, cost=None, f=1.0, late=0.0, line=None):
+        ins = [a for a in ins if isinstance(a, tuple)]
+        reads, writes = [x for a in ins for x in a[1]], [x for a in outs for x in a[1]]
+        if cost is None:
+            n = max(a[2] for a in outs + ins[:1])
+            cost = 0.05 + 0.0013 * n if any(a[3] for a in ins) else max(64, n * f) * 0.00083
+        me, pre = len(ops), {}
+        for regs, wr in ((reads, False), (writes, True)):
+            for name, m in regs:
+                for am, aw, j in touched.get(name, []):
+                    if am & m and (aw or wr or name.startswith("ps")):
+                        pre[j] = WAIT + ops[j][6]
+        for name, m in reads:
+            for ln, lm, key, lat in landing:
+                if ln == name and lm & m and key in anchor:
+                    pre[anchor[key]] = max(pre.get(anchor[key], 0), lat)
+        if line:
+            if line in chain:
+                pre.setdefault(chain[line], 0.0)
+            chain[line] = me
+        ops.append((e, make, reads, writes, sem, cost, late, pre))
+        for name, m in writes:
+            touched[name] = [a for a in touched.get(name, []) if a[0] & ~m] + [(m, True, me)]
+        for name, m in reads:
+            touched.setdefault(name, []).append((m, False, me))
+        return me
+
+    def emit(i):
+        e, make, reads, writes, sem = ops[i][:5]
         wait_for(e, reads, writes)
+        if sem == "sent":
+            return make()
         inc = 16 if sem else 1
         sem = sem or own[e]
         total[sem] = total.get(sem, 0) + inc
         make().then_inc(T.sem[sem], inc)
         note(e, reads, writes, sem, total[sem])
+
+    def run():
+        n = len(ops)
+        rest, after, left = [0.0] * n, [[] for _ in ops], [len(o[7]) for o in ops]
+        for i in range(n - 1, -1, -1):
+            rest[i] += ops[i][5]
+            for j, lat in ops[i][7].items():
+                after[j].append(i)
+                rest[j] = max(rest[j], rest[i] + lat)
+        free, end, can = {e: 0.0 for e in queue}, [0.0] * n, [0.0] * n
+        ready = {e: [i for i in range(n) if ops[i][0] == e and not left[i]] for e in queue}
+        for _ in range(n):
+            pick = None
+            for e, l in ready.items():
+                if not l:
+                    continue
+                top = max(l, key=lambda i: (rest[i], -i))
+                at = max(free[e], can[top])
+                fits = [i for i in l if max(free[e], can[i]) + ops[i][5] <= at + SLACK and can[i] < at]
+                i = max(fits, key=lambda i: (rest[i], -i)) if fits else top
+                s = max(free[e], can[i])
+                if pick is None or s < pick[0]:
+                    pick = (s, i)
+            s, i = pick
+            e = ops[i][0]
+            ready[e].remove(i)
+            free[e] = end[i] = s + ops[i][5]
+            emit(i)
+            for k in after[i]:
+                can[k] = max(can[k], end[i] + ops[k][7][i])
+                left[k] -= 1
+                if not left[k]:
+                    ready[ops[k][0]].append(k)
 
     def ap(a):
         return a[0] if isinstance(a, tuple) else a
@@ -118,11 +181,11 @@ def rank_program(g, core, T, topo):
             issue("v", lambda: g.vector.tensor_scalar(out[0], in0[0], ap(s1), ap(s2), op0, op1), [out], [in0, s1, s2])
 
     def tt(out, a, b, op):
-        issue("v", lambda: g.vector.tensor_tensor(out[0], a[0], b[0], op), [out], [a, b])
+        issue("v", lambda: g.vector.tensor_tensor(out[0], a[0], b[0], op), [out], [a, b], f=2.0)
 
     def cp(out, a, e="v", scale=None):
         if e == "v" and scale is None:
-            issue("v", lambda: g.vector.tensor_copy(out[0], a[0]), [out], [a])
+            return issue("v", lambda: g.vector.tensor_copy(out[0], a[0]), [out], [a])
         elif e == "v":
             ts(out, a, scale, AL.mult)
         elif scale is None:
@@ -134,37 +197,39 @@ def rank_program(g, core, T, topo):
         issue("s", lambda: g.scalar.activation(out[0], a[0], AF.Identity, bias=ap(bias), scale=scale), [out], [a, bias])
 
     def fill(out, x):
-        issue("v", lambda: g.vector.memset(out[0], x), [out], [])
+        issue("v", lambda: g.vector.memset(out[0], x), [out], [], f=0.5)
 
     def sfill(name, lo, hi, step, x):
         cp(V(name, lo, hi, step), V("ones", 0, len(range(lo, hi, step))), "s", float(x))
 
-    def scan(out, d0, d1, op0, op1):
-        issue("v", lambda: g.vector.tensor_tensor_scan(out[0], d0[0], d1[0], 0.0, op0, op1), [out], [d0, d1])
+    def scan(out, d0, d1, op0, op1, f=1.0):
+        issue("v", lambda: g.vector.tensor_tensor_scan(out[0], d0[0], d1[0], 0.0, op0, op1), [out], [d0, d1], f=f)
 
     def pickup(out, pat, row):
         scan(out, pat, row, AL.add, AL.min)
 
     def quant(q, s, lo, n, tile):
         a, b = V(q, lo, lo + n), V(s, lo, lo + n)
-        issue("v", lambda: g.vector.quantize_mx(a[0], b[0], tile[0]), [a, b], [tile])
+        issue("v", lambda: g.vector.quantize_mx(a[0], b[0], tile[0]), [a, b], [tile], cost=0.012 + 0.00088 * n)
 
     def mm(k, n, wq, ws, wlo, xq, xs, xlo):
         o, a, b = bank(k, n), V(wq, wlo, wlo + 128), V(ws, wlo, wlo + 128)
         c, d = V(xq, xlo, xlo + n), V(xs, xlo, xlo + n)
-        issue("t", lambda: g.tensor.matmul_mx(o[0], a[0], b[0], c[0], d[0], True, True), [o], [a, b, c, d])
+        issue("t", lambda: g.tensor.matmul_mx(o[0], a[0], b[0], c[0], d[0], True, True), [o], [a, b, c, d], cost=0.0007 * (n + 16))
 
     def iota(out, pattern, base=0, cm=0, whole=False):
+        cost = 0.13 + 0.0017 * out[2]
         if whole:
-            issue("g", lambda: g.iota(out[0], pattern, base, cm), [out], [])
+            issue("g", lambda: g.iota(out[0], pattern, base, cm), [out], [], cost=cost)
         else:
-            issue("g", lambda: g.iota(out[0], pattern, base, cm, allow_small_or_imprecise_dtypes=True), [out], [])
+            issue("g", lambda: g.iota(out[0], pattern, base, cm, allow_small_or_imprecise_dtypes=True), [out], [], cost=cost)
 
     def dma(e, out, in_, sem):
-        issue(e, lambda: queue[e].dma_start(ap(out), ap(in_)), [out] if isinstance(out, tuple) else [], [in_], sem)
+        issue(e, lambda: queue[e].dma_start(ap(out), ap(in_)), [out] if isinstance(out, tuple) else [], [in_], sem,
+              cost=0.1, late=LOAD, line=e)
 
     def u8(a):
-        return (a[0].bitcast(dt.uint8), a[1])
+        return (a[0].bitcast(dt.uint8), a[1], a[2], 0)
 
     def double(name, n, upto):
         while n < upto:
@@ -188,16 +253,17 @@ def rank_program(g, core, T, topo):
         rid, pid, _ = topo.addr(c)
         return DstId(rid=rid, pnc=pid)
 
-    def push(parts):
-        wait_for("g", [x for p in parts for x in p[0][1]], [])
-        g.remote_dma_fused([RemoteDMATransfer(dst_ids=[dst_id(cores[q]) for q in to],
-                                              dma_engine_mask=sum(1 << e for e in es),
-                                              remote_sem=T.sem[sem], src=src[0], dsts=[land[0] for q in to])
-                            for src, to, land, es, sem in parts], local_sem=T.sem.sent)
+    def push(parts, key):
+        def make():
+            g.remote_dma_fused([RemoteDMATransfer(dst_ids=[dst_id(cores[q]) for q in to],
+                                                  dma_engine_mask=sum(1 << e for e in es),
+                                                  remote_sem=T.sem[sem], src=src[0], dsts=[land[0] for q in to])
+                                for src, to, land, es, sem in parts], local_sem=T.sem.sent)
+        anchor[key] = issue("g", make, [], [p[0] for p in parts], "sent", cost=0.5, line="g")
         total["sent"] = total.get("sent", 0) + sum(len(p[3]) for p in parts)
 
     def map_plan(q, t):
-        later = list(range(N - 1, q, -1))
+        later = list(range(q + 1, N))
         here = [p for p in later if near(p, q)] if t else []
         plan = [([p for p in later if p not in here], far_engines(q))]
         plan += [([p], [e for e in lanes(q, p) if e not in far_engines(q)]) for p in here]
@@ -210,37 +276,38 @@ def rank_program(g, core, T, topo):
                 return p
         return w
 
-    def arrives(sem, n, views):
+    def arrives(sem, n, views, key, lat):
         total[sem] = n
         note(None, [], [x for a in views for x in a[1]], sem, n)
+        landing.extend((name, m, key, lat) for a in views for name, m in a[1])
 
     def send_tile(base, to, stage, sem):
         x, es = 384 * stage + 192, lanes(r, to)
         push([(u8(V("Sq", base, base + 64)), [to], u8(V("Lq", x, x + 64)), es[:len(es) // 2], sem),
-              (V("Ss", base - 192, base + 64), [to], V("Ls", x - 192, x + 64), es[len(es) // 2:], sem)])
+              (V("Ss", base - 192, base + 64), [to], V("Ls", x - 192, x + 64), es[len(es) // 2:], sem)], sem)
 
     def landed(sem, stage, frm):
         x = 384 * stage + 192
-        arrives(sem, len(lanes(frm, r)), [V("Lq", x, x + 64), V("Ls", x - 192, x + 64)])
+        arrives(sem, len(lanes(frm, r)), [V("Lq", x, x + 64), V("Ls", x - 192, x + 64)], sem, FLIGHT)
 
     for t in range(R):
-        n = sum(len(es) for q in range(r) for to, es in map_plan(q, t) if r in to)
-        if n:
-            arrives("map%d" % t, n, [V("ML", 32 * t, 32 * t + 4 * r)])
+        for q in range(r):
+            n = sum(len(es) for to, es in map_plan(q, t) if r in to)
+            arrives("map%d_%d" % (t, q), n, [V("ML", 32 * t + 4 * q, 32 * t + 4 * q + 4)], "map%d" % t,
+                    FLIGHT / 2 if t and q < r - 3 else FLIGHT)
     away = [t for t in range(R) if holder(r, t) != r]
     guest = {t: [q for q in range(N) if holder(q, t) == r][0] for t in range(R)}
     for k, t in enumerate(away):
         landed("fa%d" % k, 2 * k, guest[t])
         landed("ha%d" % k, 2 * k + 1, holder(r, t))
-    arrives("wa", 2 * len(far_engines((r + LENT) % N)), [V("Wl", 0, 512), V("Wm", 0, 512)])
+    arrives("wa", 2 * len(far_engines((r + LENT) % N)), [V("Wl", 0, 512), V("Wm", 0, 512)], "none", 0.0)
     wto, far = (r - LENT) % N, far_engines(r)
     soon = (guest[0] + HOP[0]) % N == r and holder((r - HOP[0]) % N, 0) == r
 
     dma("y", V("Tt", 0, 1024), T.x[:], "dx")
     dma("s", V("ut", 0, 512), T.u[:], "du")
     dma("y", V("Ws", 0, 512), T.ws[:], "dwa")
-    dma("y", u8(V("Wq", 0, 128)), T.wc[:, 0:512], "dwb")
-    dma("y", u8(V("Wq", 128, 512)), T.wc[:, 512:2048], "dwc")
+    dma("y", u8(V("Wq", 0, 512)), T.wc[:], "dwb")
     dma("y", V("vt", 0, 512), T.v[:], "dv")
 
     cI, cLO, cHI, cSW, cL8, cAA, cMU, cAU, cM3 = range(9)
@@ -256,31 +323,34 @@ def rank_program(g, core, T, topo):
     ts(V("pi", 1, 2), V("pi", 0, 1), 15, AL.bitwise_and)
     ts(V("pi", 2, 3), V("pi", 0, 1), 3, AL.bitwise_and)
     ts(V("pi", 3, 4), V("pi", 0, 1), 2, AL.arith_shift_right, 3, AL.bitwise_and)
-    fill(V("Ft", 256, 512), 0.0)
     cp(V("sc", 0, 3), V("pi", 1, 4))
     iota(V("c1", 3, 256, 4), [[1, 4], [0, 16]])
     iota(V("c1", 0, 256, 4), [[16, 4], [1, 4], [0, 4]])
     iota(V("c1", 1, 256, 4), [[16, 4], [1, 4], [0, 4]])
     iota(V("c1", 2, 256, 4), [[16, 16], [0, 4]], 3)
-    iota(V("AB", 0, 64), [[0, 4], [4, 4], [0, 4]])
+    push([(V("Ws", 0, 512), [wto], V("Wm", 0, 512), far, "wa")], "w0")
+    iota(V("Pb", 0, 16), [[0, 4], [4, 4]])
     iota(V("rowc", 0, 16), [[16, 16]], -1)
     iota(V("BB", 0, 16), [[0, 4], [4, 4]])
-    iota(V("Pb", 0, 16), [[0, 4], [4, 4]])
     iota(V("cE", 0, 16), [[1, 4], [0, 4]])
     iota(V("cE", 16, 32), [[0, 4], [1, 4]])
     iota(V("cE", 32, 48), [[0, 4], [16, 4]], 3)
+    iota(V("cB", 0, 64), [[0, 4], [16, 4], [1, 4]])
+    iota(V("AB", 0, 64), [[0, 4], [4, 4], [0, 4]])
+    issue("g", lambda: g.affine_select(T.Z[:, 0:516], T.ones[:, 0:516], [[1, 516]], AL.is_equal, 0.0, -3, -4),
+          [V("Z", 0, 516)], [V("ones", 0, 516)], cost=1.05)
     ts(col(cL8), col(cLO), 8.0, AL.mult)
     ts(col(cSW), col(cLO), 4.0, AL.mult, col(cHI), AL.add)
-    ts(col(cH4), col(cHI), 4.0, AL.mult)
+    ts(col(cH1), col(cHI), 1.0, AL.add)
     ts(col(cAA), col(cI), 15.0, AL.is_lt, 256.0, AL.mult)
     ts(col(cAC), col(cHI), 3.0, AL.is_lt, 256.0, AL.mult)
     ts(col(cT0), col(cLO), 2.0, AL.is_ge, 2.0, AL.mult)
     ts(col(cMU), col(cLO), 3.0, AL.is_equal, 1.0 / BIG, AL.max)
     ts(col(cM3), col(cHI), 3.0, AL.is_lt, 0.25, AL.mult)
     ts(col(cAU), col(cHI), 256.0, AL.mult, -85.0, AL.add)
-    ts(col(cH1), col(cHI), 1.0, AL.add)
     cp(V("ul", 0, 16), V("rowa", 0, 16))
     cp(col(cS4), col(cSW), "s", 4.0)
+    cp(col(cH4), col(cHI), "s", 4.0)
     affine(col(cW), col(cLO), 1.0, col(cT0))
     affine(col(cT1), col(cLO), 1.0, col(cAC))
     affine(col(cT2), col(cI), 1.0, col(cAA))
@@ -305,60 +375,84 @@ def rank_program(g, core, T, topo):
         tt(V(name, 0, 16), V("tmp", at, at + 16), V("tmp", at + 16, at + 32), AL.subtract)
 
     horner("PU", 32, col(cL8), [2, 4, 6], 8, 0)
+    horner("PD", 16, col(cH4), [1, 2], 3, 128)
     marks("PB", V("pos", 8, 24), col(cSW), V("pos", 7, 23), col(cSW), 256)
     marks("PA", V("pos", 8, 24), col(cI), V("pos", 7, 23), col(cI), 288)
     marks("PC", V("pos4", 0, 16), col(cHI), V("pos4", 0, 16), col(cH1), 320)
+    for name, n, upto in (("PU", 32, 512), ("PB", 16, 64), ("PA", 16, 256), ("PC", 16, 256), ("PD", 16, 256)):
+        double(name, n, upto)
     sfill("Tab", 288, 304, 1, 0)
     sfill("Tab", 304, 320, 1, 4)
     sfill("Tab", 192, 256, 1, 0)
     cp(V("Tab", 272, 288), V("Tab", 768, 784), "s")
     cp(V("Tab", 128, 192), V("Tab", 768, 832), "s")
-    double("PU", 32, 512)
     for k in range(4):
         sfill("Tab", 512 + k, 768, 16, 4 * k)
-    ts(V("El", 0, 12), V("rowb", 0, 12), col(cS4), AL.add)
-    quant("uq", "us", 0, 128, V("ut", 0, 512))
-    a, b, o = V("Uq", 0, 256), V("uq", 0, 128), V("ul", 0, 16)
-    issue("v", lambda: g.vector.tensor_copy(a[0].bitcast(dt.uint32), b[0].bitcast(dt.uint32).indirect(o[0])), [a], [b, o])
-    cp(V("Us", 0, 256), ind(V("us", 0, 128), V("ul", 0, 16)), "s")
     cp(V("Tab", 256, 272), V("Tab", 512, 528), "s")
     cp(V("Tab", 64, 128), V("Tab", 512, 576), "s")
     cp(V("Tab", 0, 64), V("Tab", 256, 320), "s")
     cp(V("Tab", 320, 384), V("Tab", 256, 320), "s")
+    cp(V("Tab", 384, 512), V("Tab", 256, 384), "s")
     for z in range(4):
         sfill("c1", 64 * z + 35, 64 * z + 48, 4, 16 * z + 3)
         sfill("c1", 64 * z + 51, 64 * z + 64, 4, 16 * (z + 1) if z < 3 else 16 * (r + 1))
-    cp(V("Tab", 384, 512), V("Tab", 256, 384), "s")
-    double("PB", 16, 64)
-    h = len(far) // 2
-    push([(V("Ws", 0, 512), [wto], V("Wm", 0, 512), far[:h], "wa"),
-          (u8(V("Wq", 0, 128)), [wto], u8(V("Wl", 0, 128)), far[h:], "wa")])
-    issue("g", lambda: g.affine_select(T.Z[:, 0:516], T.ones[:, 0:516], [[1, 516]], AL.is_equal, 0.0, -3, -4),
-          [V("Z", 0, 516)], [V("ones", 0, 516)])
-    iota(V("cB", 0, 64), [[0, 4], [16, 4], [1, 4]])
+    quant("uq", "us", 0, 128, V("ut", 0, 512))
+    pa, pb, po = V("Uq", 0, 256), V("uq", 0, 128), V("ul", 0, 16)
+    issue("v", lambda: g.vector.tensor_copy(pa[0].bitcast(dt.uint32), pb[0].bitcast(dt.uint32).indirect(po[0])),
+          [pa], [pb, po], cost=0.38)
+    cp(V("Us", 0, 256), ind(V("us", 0, 128), V("ul", 0, 16)), "s")
+    ts(V("El", 0, 12), V("rowb", 0, 12), col(cS4), AL.add)
+    affine(V("lc", 0, 16), V("rowc", 0, 16), 1.0, col(cT2))
+    for b in range(4):
+        quant("Eq", "Es", 128 * b, 128, V("Z", 3 - b, 515 - b))
+    ts(V("Fl", 0, 1), col(cI), 4.0, AL.mult)
+    ts(V("Fl", 1, 2), col(cSW), 4.0, AL.mult, 1.0, AL.add)
+    ts(V("Fl", 2, 3), col(cSW), 4.0, AL.mult, 2.0, AL.add)
+    ts(V("Pl", 0, 1), col(cLO), 16.0, AL.mult, col(cHI), AL.add)
+    ts(col(cAK), col(cT1), -336.0, AL.add)
+    ts(col(cSE), col(cI), -64.0 * r, AL.add)
+    ts(col(cK1), col(cI), 16.0, AL.add)
+    ts(col(cK2), col(cI), 32.5, AL.add)
+    ts(col(cK3), col(cI), 48.5, AL.add)
+    fill(V("z0", 0, 2), 0)
+    fill(V("Ft", 256, 512), 0.0)
+    fill(V("Ht", 256, 512), 0.0)
+    fill(V("zt", 0, 512), 0.0)
+    fill(V("Hd", 0, 320, 80), 0.0)
+    if r == 0:
+        cp(V("ch", 128, 129), col(cI))
+    for st in range(4):
+        quant("Lq", "Ls", 384 * st + 256, 128, V("zt", 0, 512))
+    quant("vq", "vs", 0, 128, V("vt", 0, 512))
+
+    def one(e, t, lo, hi, step=1):
+        sfill("Flg", 16 * lo + 4 * e + t, 16 * (hi - 1) + 4 * e + t + 1, 16 * step, 1)
+    for k in range(4):
+        sfill("Flg", 256 * k, 256 * k + 256, 1, 0)
+    for e in range(4):
+        one(e, e, 0, 64)
+    for args in ((0, 1, 0, 16), (2, 3, 0, 64, 4), (0, 2, 16, 32), (0, 2, 0, 4), (1, 3, 0, 64, 16), (0, 3, 32, 48),
+                 (0, 3, 16, 32, 4), (0, 3, 4, 8), (0, 3, 0, 1)):
+        one(*args)
+    for k in range(4):
+        one(1, 2, k, 64, 16)
+        one(1, 3, 4 + k, 64, 16)
 
     def rest_of_w():
-        push([(u8(V("Wq", 128, 512)), [wto], u8(V("Wl", 128, 512)), far, "wa")])
+        push([(u8(V("Wq", 0, 512)), [wto], u8(V("Wl", 0, 512)), far, "wa")], "w1")
 
-    def flag_table():
-        def one(e, t, lo, hi, step=1):
-            sfill("Flg", 16 * lo + 4 * e + t, 16 * (hi - 1) + 4 * e + t + 1, 16 * step, 1)
-        sfill("Flg", 0, 512, 1, 0)
-        sfill("Flg", 512, 1024, 1, 0)
-        for e in range(4):
-            one(e, e, 0, 64)
-        one(0, 1, 0, 16)
-        one(2, 3, 0, 64, 4)
-        one(0, 2, 16, 32)
-        one(0, 2, 0, 4)
-        one(1, 3, 0, 64, 16)
-        one(0, 3, 32, 48)
-        one(0, 3, 16, 32, 4)
-        one(0, 3, 4, 8)
-        one(0, 3, 0, 1)
-        for k in range(4):
-            one(1, 2, k, 64, 16)
-            one(1, 3, 4 + k, 64, 16)
+    def count(c, lo, hi, at):
+        o, s, k, bias = V("junk", at, at + hi - lo), V("sa", c, c + 1), V("K1", lo, hi), col(cK3 if c == 3 else cK2)
+        issue("s", lambda: g.scalar.activation(o[0], k[0], AF.Sign, bias=bias[0], scale=-1.0, accum_out=s[0]), [o, s], [k, bias])
+
+    def reduce(c, lo, hi):
+        o, k = V("sa", c, c + 1), V("le", lo, hi)
+        issue("v", lambda: g.vector.tensor_reduce(o[0], k[0], AxisListType.X, AL.add), [o], [k])
+
+    def update(lo, hi):
+        for b in range(4):
+            w = V("Tt", 64 * lo + b, 64 * hi, 4)
+            tt(w, ind(V("Hd", 80 * b, 80 * b + 65), V("kl", lo, hi)), w, AL.add)
 
     for t in range(R):
         qt, qf, qh = 512 * t, 512 * t + 256, 512 * t + 384
@@ -369,18 +463,10 @@ def rank_program(g, core, T, topo):
         for h in range(2):
             ts(V("bits", 256 * h, 256 * h + 256, 2), bank(6 * h + 1, 128), 0.0, AL.is_gt, 2.0, AL.mult)
             ts(V("bits", 256 * h + 1, 256 * h + 256, 2), bank(6 * h, 128), 0.0, AL.is_gt, 1.0, AL.add)
-
-        def unpack(e):
-            for b in range(4):
-                if e == "t":
-                    mm(2 + b, 256, "Eq", "Es", 128 * b, "Sq", "Ss", qt)
-                else:
-                    cp(V("Vh", 256 * b, 256 * b + 256), bank(2 + b, 256), "s", 0.5)
-                    cp(V("Vg", 256 * b, 256 * b + 256), bank(2 + b, 256), "s", 0.5)
-        if t:
-            unpack("t")
-        else:
-            double("PA", 16, 256)
+        for b in range(4):
+            mm(2 + b, 256, "Eq", "Es", 128 * b, "Sq", "Ss", qt)
+            cp(V("Vh", 256 * b, 256 * b + 256), bank(2 + b, 256), "s", 0.5)
+            cp(V("Vg", 256 * b, 256 * b + 256), bank(2 + b, 256), "s", 0.5)
         scan(V("su", 0, 512), V("PU", 0, 512), V("bits", 0, 512), AL.mult, AL.add)
         ts(V("cod", 0, 16), V("su", 31, 512, 32), col(cMU), AL.mult, col(cAU), AL.add)
         tt(V("N1", 0, 256), ind(V("Tab", 0, 1024), V("cod", 0, 16)), V("c1", 0, 256), AL.add)
@@ -395,12 +481,6 @@ def rank_program(g, core, T, topo):
         cp(V("T12", 0, 64), ind(V("AB", 192, 256), V("W1", 4, 8)), "s")
         cp(V("AB", 256, 320), ind(V("AB", 128, 192), V("W1", 0, 4)), "s")
         cp(V("AB", 320, 384), ind(V("T12", 0, 64), V("W1", 0, 4)), "s")
-        if t == 0:
-            double("PC", 16, 256)
-            affine(V("lc", 0, 16), V("rowc", 0, 16), 1.0, col(cT2))
-            flag_table()
-        else:
-            unpack("s")
         for v in (2, 1, 0):
             pickup(V("s2", 16 * v, 16 * v + 16), V("PB" if v else "PA", 0, 16), V("Rb", 128 + v, 192, 4))
         ts(V("W2", 0, 6, 2), V("s2", 15, 48, 16), col(cAA), AL.add)
@@ -410,26 +490,15 @@ def rank_program(g, core, T, topo):
         pickup(V("s3", 0, 16), V("PA", 0, 16), V("Pb", 16, 32))
         ts(V("W3", 0, 1), V("s3", 15, 16), col(cAA), AL.add, col(cM3), AL.mult)
         cp(V("Pb", 32, 48), ind(V("Pb", 16, 32), V("W3", 0, 1)))
-        cp(V("Pb", 48, 64), ind(V("Pb", 32, 48), V("W3", 0, 1)))
+        anchor["map%d" % t] = cp(V("Pb", 48, 64), ind(V("Pb", 32, 48), V("W3", 0, 1)))
         if r < N - 1:
             cp(V("mp", 16 * t, 16 * t + 16), ind(V("Pb", 48, 64), V("W3", 0, 1)))
-            push([(V("mp", 16 * t, 16 * t + 4), to, V("ML", 32 * t + 4 * r, 32 * t + 4 * r + 4), es, "map%d" % t)
-                  for to, es in map_plan(r, t)])
-        if t == 0:
-            if not soon:
-                rest_of_w()
-            for b in range(4):
-                quant("Eq", "Es", 128 * b, 128, V("Z", 3 - b, 515 - b))
-            unpack("t")
-            horner("PD", 16, col(cH4), [1, 2], 3, 128)
-            double("PD", 16, 256)
-            unpack("s")
-            ts(V("Fl", 0, 1), col(cI), 4.0, AL.mult)
-            ts(V("Fl", 1, 2), col(cSW), 4.0, AL.mult, 1.0, AL.add)
-            ts(V("Fl", 2, 3), col(cSW), 4.0, AL.mult, 2.0, AL.add)
-            ts(V("Pl", 0, 1), col(cLO), 16.0, AL.mult, col(cHI), AL.add)
-            ts(col(cAK), col(cT1), -336.0, AL.add)
-        tt(V("nr", 0, 256), V("bits", 0, 512, 2), V("bits", 1, 512, 2), AL.add)
+            push([(V("mp", 16 * t, 16 * t + 4), to, V("ML", 32 * t + 4 * r, 32 * t + 4 * r + 4), es, "map%d_%d" % (t, r))
+                  for to, es in map_plan(r, t)], "map%d" % t)
+        if t == 0 and not soon:
+            rest_of_w()
+        for h in range(2):
+            tt(V("nr", 128 * h, 128 * h + 128), V("bits", 256 * h, 256 * h + 256, 2), V("bits", 256 * h + 1, 256 * h + 256, 2), AL.add)
         tt(V("BB", 16, 64), ind(V("Rb", 128, 192), V("Fl", 0, 3)), V("cE", 0, 48), AL.subtract)
         ts(V("Pp", 0, 16), ind(V("Pb", 0, 64), V("Pl", 0, 1)), 0.25, AL.mult)
         pickup(V("s7", 0, 256), V("PA", 0, 256), V("nr", 0, 256))
@@ -446,40 +515,28 @@ def rank_program(g, core, T, topo):
         ts(V("ck", 0, 16), V("s8", 15, 256, 16), 16.0 / BIG, AL.mult, col(cAK), AL.add)
         ts(V("D2", 0, 16), V("s5", 3, 64, 4), col(cA2), AL.add)
         cp(V("Pre", 0, 256), ind(V("AB", 0, 384), V("D2", 0, 16)), "s")
-        if t == 0:
-            ts(col(cSE), col(cI), -64.0 * r, AL.add)
-            ts(col(cK1), col(cI), 16.0, AL.add)
-            ts(col(cK2), col(cI), 32.5, AL.add)
-            ts(col(cK3), col(cI), 48.5, AL.add)
-            fill(V("z0", 0, 2), 0)
-            if r == 0:
-                cp(V("ch", 128, 129), col(cI))
         for b in range(4):
-            tt(V("G", 256 * b, 256 * b + 256), ind(V("Vh", 256 * b, 256 * b + 256), V("ll", 0, 16)),
-               V("Vg", 256 * b, 256 * b + 256), AL.add)
-            if b == 1:
-                pickup(V("s6", 0, 256), V("PC", 0, 256), V("Pre", 0, 256))
-            if b == 2:
-                for e in range(4):
-                    tt(V("Kw", 16 * e, 16 * e + 16), V("s6", 64 * e + 3, 64 * e + 64, 4), V("ck", 0, 16), AL.add)
+            for h in range(2):
+                lo = 256 * b + 128 * h
+                tt(V("G", lo, lo + 128), ind(V("Vh", 256 * b, 256 * b + 256), V("ll", 8 * h, 8 * h + 8)), V("Vg", lo, lo + 128), AL.add)
+        pickup(V("s6", 0, 256), V("PC", 0, 256), V("Pre", 0, 256))
+        for e in range(4):
+            tt(V("Kw", 16 * e, 16 * e + 16), V("s6", 64 * e + 3, 64 * e + 64, 4), V("ck", 0, 16), AL.add)
         for q in range(r):
-            src = ind(V("ML", 32 * t, 32 * t + 4 * r), V("ch", 16 * q - 16, 16 * q - 15) if q else V("z0", 0, 1))
+            src = ind(V("ML", 32 * t, 32 * t + 4 * q + 4), V("ch", 16 * q - 16, 16 * q - 15) if q else V("z0", 0, 1))
             if q < r - 1:
                 ts(V("ch", 16 * q, 16 * q + 16), src, 0.25, AL.mult)
             else:
                 ts(V("ch", 128, 144), src, 4.0, AL.mult, col(cSE), AL.add)
         cp(V("key", 0, 16), ind(V("Kw", 0, 64), V("ch", 128, 129)))
         cp(V("m", 0, 256), ind(V("Flg", 0, 1024), V("key", 0, 16)))
-        scan(V("K1", 0, 256), V("ones", 0, 256), V("m", 0, 256), AL.mult, AL.add)
-        for c, lo, hi, at in ((3, 48, 256, 0), (2, 32, 192, 208)):
-            o, s, k, bias = V("junk", at, at + hi - lo), V("sa", c, c + 1), V("K1", lo, hi), col(cK3 if c == 3 else cK2)
-            issue("s", lambda: g.scalar.activation(o[0], k[0], AF.Sign, bias=bias[0], scale=-1.0, accum_out=s[0]),
-                  [o, s], [k, bias])
+        scan(V("K1", 0, 256), V("ones", 0, 256), V("m", 0, 256), AL.mult, AL.add, 0.5)
+        count(3, 48, 256, 0)
+        count(2, 32, 192, 208)
         ts(V("le", 64, 192), V("K1", 0, 128), col(cK1), AL.is_le)
         ts(V("le", 0, 64), V("K1", 0, 64), col(cI), AL.is_le)
-        for c, lo, hi in ((1, 64, 192), (0, 0, 64)):
-            o, k = V("sa", c, c + 1), V("le", lo, hi)
-            issue("v", lambda: g.vector.tensor_reduce(o[0], k[0], AxisListType.X, AL.add), [o], [k])
+        reduce(1, 64, 192)
+        reduce(0, 0, 64)
         ts(V("sl", 3, 4), V("sa", 3, 4), 0.5, AL.mult, 152.0, AL.add)
         cp(V("sl", 0, 2), V("sa", 0, 2))
         ts(V("sl", 2, 3), V("sa", 2, 3), 0.5, AL.mult, 112.0, AL.add)
@@ -489,12 +546,6 @@ def rank_program(g, core, T, topo):
         k = away.index(t) if t in away else None
         if k is not None:
             send_tile(qf, holder(r, t), 2 * k, "fa%d" % k)
-        if t == 0:
-            fill(V("Ht", 0, 512), 0.0)
-            for st in range(4):
-                quant("Lq", "Ls", 384 * st + 256, 128, V("Ht", 0, 512))
-            fill(V("Hd", 0, 320, 80), 0.0)
-            quant("vq", "vs", 0, 128, V("vt", 0, 512))
         if t == R - 1:
             cp(V("sf", 0, 4), V("sl", 0, 4))
             for c in range(4):
@@ -505,14 +556,11 @@ def rank_program(g, core, T, topo):
                 mm(2 + b, 128, wq, ws, 128 * b, "Sq", "Ss", qf)
             else:
                 mm(2 + b, 128, wq, ws, 128 * b, "Lq", "Ls", 768 * k + 192)
-        steps = [lambda: pickup(V("s9", 0, 256), V("PA", 0, 256), V("K1", 0, 256)),
-                 lambda: ts(V("ka", 0, 16), V("s9", 15, 256, 16), col(cAA), AL.add, -1.0, AL.add),
-                 lambda: ts(V("kb", 0, 16), V("ka", 0, 16), 63, AL.bitwise_and),
-                 lambda: tt(V("kc", 0, 16), V("ka", 0, 16), V("kb", 0, 16), AL.min),
-                 lambda: ts(V("kl", 0, 16), V("kc", 0, 16), 1.0, AL.add)]
-        cut = 1 if k is None else 5
-        for s in steps[:cut]:
-            s()
+        pickup(V("s9", 0, 256), V("PA", 0, 256), V("K1", 0, 256))
+        ts(V("ka", 0, 16), V("s9", 15, 256, 16), col(cAA), AL.add, -1.0, AL.add)
+        ts(V("kb", 0, 16), V("ka", 0, 16), 63, AL.bitwise_and)
+        tt(V("kc", 0, 16), V("ka", 0, 16), V("kb", 0, 16), AL.min)
+        ts(V("kl", 0, 16), V("kc", 0, 16), 1.0, AL.add)
         for b in range(4):
             cp(V("Ht", b, 256, 4), bank(2 + b, 64), "sv"[b % 2], 0.03125)
         quant("Sq", "Ss", qh, 128, V("Ht", 0, 512))
@@ -526,23 +574,21 @@ def rank_program(g, core, T, topo):
                 mm(banks[b], 128, "Eq", "Es", 128 * b, "Sq", "Ss", qh)
             else:
                 mm(banks[b], 128, "Eq", "Es", 128 * b, "Lq", "Ls", 768 * k + 576)
-        for s in steps[cut:]:
-            s()
-        for b in range(4):
-            cp(V("Hd", 80 * b + 1, 80 * b + 65), bank(banks[b], 64), "s" if b or k is None else "v")
-        for b in range(4):
-            w = V("Tt", b, 1024, 4)
-            tt(w, ind(V("Hd", 80 * b, 80 * b + 65), V("kl", 0, 16)), w, AL.add)
+            cp(V("Hd", 80 * b + 1, 80 * b + 65), bank(banks[b], 64), "s" if b else "v")
+        update(0, 8)
+        update(8, 16)
     qt = 512 * R
     for h in range(2):
-        quant("Sq", "Ss", qt + 128 * h, 128, V("Tt", 512 * h, 512 * h + 512))
-        mm(2 + h, 128, "vq", "vs", 0, "Sq", "Ss", qt + 128 * h)
-    dma("y", T.oc[:], u8(V("Sq", qt, qt + 256)), "oy")
-    for h in range(2):
-        cp(V("ys", 128 * h, 128 * h + 128), bank(2 + h, 128))
-    for k in range(4):
-        src = (T.Ss[32 * k:32 * k + 4, qt:qt + 256], V("Ss", qt, qt + 256)[1])
-        dma("s", T.osc[4 * k:4 * k + 4, :], src, "oz")
-    dma("y", T.y[:], V("ys", 0, 256), "oy")
+        lo = qt + 128 * h
+        quant("Sq", "Ss", lo, 128, V("Tt", 512 * h, 512 * h + 512))
+        mm(2 + h, 128, "vq", "vs", 0, "Sq", "Ss", lo)
+        dma("y", T.oc[:, 512 * h:512 * h + 512], u8(V("Sq", lo, lo + 128)), "oy")
+        cp(V("ys", 128 * h, 128 * h + 128), bank(2 + h, 128), "sv"[h])
+        if h:
+            for k in range(4):
+                src = (T.Ss[32 * k:32 * k + 4, qt:qt + 256], V("Ss", qt, qt + 256)[1], 256, 0)
+                dma("s", T.osc[4 * k:4 * k + 4, :], src, "oz")
+        dma("y", T.y[:, 128 * h:128 * h + 128], V("ys", 128 * h, 128 * h + 128), "oy")
+    run()
     for sem, n in total.items():
         g.wait_ge(T.sem[sem], n)

@@ -5,8 +5,9 @@ N, C, A, R = 8, 256, 64, 3
 HOP = [1, 2, 3]
 LENT = HOP[1]
 X4, U8, BF, F32, I32, U16 = "float8_e4m3fn_x4", "uint8", "bfloat16", "float32", "int32", "uint16"
-BIG = float(2 ** 24)
-WAIT, FLIGHT, LOAD, SLACK = 0.2, 3.5, 2.5, 0.08
+BIG = float(2 ** 40)
+TINY = 1e-35
+WAIT, FLIGHT, LOAD, SLACK = 0.17, 2.4, 2.0, 0.05
 
 
 def _sb(n, d):
@@ -18,29 +19,27 @@ SCRATCH = {
     "uq": _sb(128, X4), "us": _sb(128, U8), "Uq": _sb(256, X4), "Us": _sb(256, U8),
     "vq": _sb(128, X4), "vs": _sb(128, U8),
     "Wq": _sb(512, X4), "Ws": _sb(512, U8), "Wl": _sb(512, X4), "Wm": _sb(512, U8),
-    "Sq": _sb(1792, X4), "Ss": _sb(1792, U8), "Lq": _sb(1536, X4), "Ls": _sb(1536, U8),
-    "Eq": _sb(512, X4), "Es": _sb(512, U8), "Z": _sb(528, BF), "ones": _sb(528, BF),
-    "Vh": _sb(1024, BF), "Vg": _sb(1024, BF), "G": _sb(1024, BF), "Ft": _sb(512, BF), "Ht": _sb(512, BF),
-    "Hd": _sb(320, BF), "ys": _sb(256, F32), "zt": _sb(512, BF),
+    "Sq": _sb(1920, X4), "Ss": _sb(1920, U8), "Lq": _sb(1280, X4), "Ls": _sb(1280, U8),
+    "Eq": _sb(512, X4), "Es": _sb(512, U8), "Z": _sb(528, BF), "ones": _sb(448, BF),
+    "Vh": _sb(1024, BF), "Vg": _sb(1024, BF), "G": _sb(1024, BF), "FH": _sb(768, BF),
+    "Hd": _sb(320, BF), "ys": _sb(256, F32),
     "pi": _sb(4, I32), "sc": _sb(32, F32), "pos": _sb(48, F32), "pos4": _sb(16, F32), "tmp": _sb(512, F32),
-    "PU": _sb(512, BF), "PA": _sb(256, BF), "PB": _sb(64, BF), "PC": _sb(256, BF), "PD": _sb(256, BF),
-    "Tab": _sb(1024, BF), "Flg": _sb(1024, BF), "c1": _sb(256, BF), "cE": _sb(48, BF), "cB": _sb(64, BF),
-    "rowa": _sb(16, F32), "rowb": _sb(16, F32), "rowc": _sb(16, F32), "lc": _sb(16, F32),
-    "ul": _sb(16, U16), "El": _sb(12, U16), "Fl": _sb(4, U16), "Pl": _sb(2, U16), "z0": _sb(2, U16),
-    "bits": _sb(512, BF), "su": _sb(512, F32), "cod": _sb(16, U16), "N1": _sb(256, BF), "X1": _sb(256, BF),
-    "s1": _sb(192, F32), "W1": _sb(12, U16), "Rb": _sb(192, BF), "s2": _sb(48, F32), "W2": _sb(6, U16),
-    "Qb": _sb(32, BF), "Pb": _sb(64, BF), "s3": _sb(16, F32), "W3": _sb(2, U16), "mp": _sb(48, F32),
-    "ML": _sb(96, F32), "ch": _sb(144, U16),
-    "AB": _sb(384, BF), "T12": _sb(64, BF), "BB": _sb(96, BF), "T2": _sb(16, BF), "Pp": _sb(16, BF),
-    "s4": _sb(16, F32), "D1": _sb(4, U16), "BC": _sb(64, BF), "s5": _sb(64, F32), "D2": _sb(16, U16),
-    "Pre": _sb(256, BF), "s6": _sb(256, F32), "nr": _sb(256, BF), "s7": _sb(256, F32), "s8": _sb(256, F32),
-    "ck": _sb(16, F32), "lf": _sb(16, F32), "ll": _sb(16, U16), "Kw": _sb(64, F32), "key": _sb(16, U16),
-    "m": _sb(256, BF), "K1": _sb(256, BF), "le": _sb(192, BF), "junk": _sb(368, BF), "sa": _sb(4, F32),
-    "sl": _sb(4, U16), "sf": _sb(4, F32), "s9": _sb(256, F32), "ka": _sb(16, I32), "kb": _sb(16, I32),
-    "kc": _sb(16, I32), "kl": _sb(16, U16),
+    "PU": _sb(256, BF), "PV": _sb(256, BF), "PA": _sb(256, BF), "PB": _sb(64, BF), "PC": _sb(256, BF),
+    "Tab": _sb(256, BF), "Flg": _sb(448, BF), "c1": _sb(256, BF), "rowa": _sb(16, F32), "lc": _sb(16, F32),
+    "ul": _sb(16, U16), "Fl": _sb(4, U16), "Kl": _sb(4, U16), "e0": _sb(2, U16),
+    "bits": _sb(512, BF), "su": _sb(512, BF), "sv": _sb(512, BF), "cod": _sb(16, U16), "N1": _sb(256, BF),
+    "s1": _sb(192, BF), "W1": _sb(12, U16), "RR": _sb(768, BF), "Rb": _sb(64, BF), "AB": _sb(256, BF),
+    "s2": _sb(48, BF), "W2": _sb(6, U16), "QQ": _sb(192, BF), "BB": _sb(64, BF), "Wc": _sb(16, U16),
+    "L3": _sb(560, BF), "s3": _sb(16, BF), "W0": _sb(2, U16), "Pp": _sb(64, BF), "s4": _sb(16, BF), "D1": _sb(4, U16),
+    "s5": _sb(64, BF), "D2": _sb(16, U16), "Pre": _sb(256, BF), "s6": _sb(256, BF),
+    "kd": _sb(48, I32), "ck": _sb(32, F32), "lf": _sb(16, F32), "ll": _sb(16, U16), "Kq": _sb(64, F32), "XX": _sb(256, F32),
+    "ml": _sb(48, U16), "me": _sb(48, U16), "mw": _sb(48, BF), "ML": _sb(192, U16), "MW": _sb(384, BF), "ch": _sb(64, U16),
+    "key": _sb(16, U16), "m": _sb(256, BF), "K1": _sb(256, BF), "le": _sb(192, BF), "ls": _sb(192, BF),
+    "junk": _sb(368, BF), "sa": _sb(4, F32), "sl": _sb(4, U16), "sf": _sb(4, F32), "s9": _sb(256, BF),
+    "ka": _sb(16, I32), "kb": _sb(16, I32), "kc": _sb(16, I32), "kl": _sb(16, U16),
     "ps": ("psum", [128, 4096], F32),
 }
-SEMAPHORES = ["ev", "es", "et", "eg", "dx", "du", "dv", "dwa", "dwb", "oy", "oz", "sent",
+SEMAPHORES = ["ev", "es", "et", "eg", "dx0", "dx1", "du", "dv", "dwa", "dwb", "dwc", "oy", "oz", "sent",
               "fa0", "fa1", "ha0", "ha1", "wa"] + ["map%d_%d" % (t, q) for t in range(R) for q in range(N - 1)]
 
 
@@ -53,15 +52,15 @@ def rank_program(g, core, T, topo):
     queue = {"v": g.vector, "s": g.scalar, "t": g.tensor, "g": g, "y": g.sync}
     own = {"v": "ev", "s": "es", "t": "et", "g": "eg"}
     total, seen, clock = {}, {}, {e: {} for e in queue}
-    ops, touched, landing, anchor, chain = [], {}, [], {}, {}
+    ops, touched, landing, anchor, chain, others = [], {}, [], {}, {}, {}
 
     def V(name, lo, hi, step=1):
         m = (1 << hi) - (1 << lo) if step == 1 else sum(1 << c for c in range(lo, hi, step))
         ap = T[name][:, lo:hi] if step == 1 else T[name][:, lo:hi:step]
         return (ap, [(name, m)], len(range(lo, hi, step)), 0)
 
-    def bank(k, n):
-        return (T.ps[:, 512 * k:512 * k + n], [("ps%d" % k, 1)], n, 0)
+    def bank(k, n, lo=0):
+        return (T.ps[:, 512 * k + lo:512 * k + lo + n], [("ps%d" % k, 1)], n, 0)
 
     def ind(win, off):
         return (win[0].indirect(off[0]), win[1] + off[1], 16 * off[2], 1)
@@ -111,7 +110,8 @@ def rank_program(g, core, T, topo):
             for name, m in regs:
                 for am, aw, j in touched.get(name, []):
                     if am & m and (aw or wr or name.startswith("ps")):
-                        pre[j] = WAIT + ops[j][6]
+                        near_ps = name.startswith("ps") and ops[j][0] == e
+                        pre[j] = max(pre.get(j, 0.0), 0.0 if near_ps else WAIT + ops[j][6])
         for name, m in reads:
             for ln, lm, key, lat in landing:
                 if ln == name and lm & m and key in anchor:
@@ -143,6 +143,8 @@ def rank_program(g, core, T, topo):
         rest, after, left = [0.0] * n, [[] for _ in ops], [len(o[7]) for o in ops]
         for i in range(n - 1, -1, -1):
             rest[i] += ops[i][5]
+            if i in others:
+                rest[others[i]] = max(rest[others[i]], rest[i] + FLIGHT + 1.0)
             for j, lat in ops[i][7].items():
                 after[j].append(i)
                 rest[j] = max(rest[j], rest[i] + lat)
@@ -153,11 +155,14 @@ def rank_program(g, core, T, topo):
             for e, l in ready.items():
                 if not l:
                     continue
-                top = max(l, key=lambda i: (rest[i], -i))
-                at = max(free[e], can[top])
-                fits = [i for i in l if max(free[e], can[i]) + ops[i][5] <= at + SLACK and can[i] < at]
-                i = max(fits, key=lambda i: (rest[i], -i)) if fits else top
-                s = max(free[e], can[i])
+                go = {i: max(free[e], can[i]) for i in l}
+                worst = max(go[i] + rest[i] for i in l)
+
+                def harm(i):
+                    done = go[i] + ops[i][5]
+                    return max([done + rest[j] for j in l if j != i and go[j] < done] + [worst]) - worst
+                i = min(l, key=lambda i: (max(harm(i) - SLACK, 0.0), go[i] if go[i] > free[e] + SLACK else 0.0, -rest[i], i))
+                s = go[i]
                 if pick is None or s < pick[0]:
                     pick = (s, i)
             s, i = pick
@@ -174,16 +179,15 @@ def rank_program(g, core, T, topo):
     def ap(a):
         return a[0] if isinstance(a, tuple) else a
 
-    def ts(out, in0, s1, op0, s2=None, op1=None):
+    def ts(out, in0, s1, op0, s2=None, op1=None, f=1.0):
         if op1 is None:
-            issue("v", lambda: g.vector.tensor_scalar(out[0], in0[0], ap(s1), None, op0), [out], [in0, s1])
-        else:
-            issue("v", lambda: g.vector.tensor_scalar(out[0], in0[0], ap(s1), ap(s2), op0, op1), [out], [in0, s1, s2])
+            return issue("v", lambda: g.vector.tensor_scalar(out[0], in0[0], ap(s1), None, op0), [out], [in0, s1], f=f)
+        return issue("v", lambda: g.vector.tensor_scalar(out[0], in0[0], ap(s1), ap(s2), op0, op1), [out], [in0, s1, s2], f=f)
 
-    def tt(out, a, b, op):
-        issue("v", lambda: g.vector.tensor_tensor(out[0], a[0], b[0], op), [out], [a, b], f=2.0)
+    def tt(out, a, b, op, line=None):
+        issue("v", lambda: g.vector.tensor_tensor(out[0], a[0], b[0], op), [out], [a, b], f=2.0, line=line)
 
-    def cp(out, a, e="v", scale=None):
+    def cp(out, a, e="v", scale=None, line=None):
         if e == "v" and scale is None:
             return issue("v", lambda: g.vector.tensor_copy(out[0], a[0]), [out], [a])
         elif e == "v":
@@ -191,10 +195,10 @@ def rank_program(g, core, T, topo):
         elif scale is None:
             issue("s", lambda: g.scalar.activation(out[0], a[0], AF.Copy), [out], [a])
         else:
-            issue("s", lambda: g.scalar.activation(out[0], a[0], AF.Copy, scale=scale), [out], [a])
+            issue("s", lambda: g.scalar.activation(out[0], a[0], AF.Copy, scale=scale), [out], [a], line=line)
 
-    def affine(out, a, scale, bias):
-        issue("s", lambda: g.scalar.activation(out[0], a[0], AF.Identity, bias=ap(bias), scale=scale), [out], [a, bias])
+    def affine(out, a, scale, bias, func=AF.Identity):
+        issue("s", lambda: g.scalar.activation(out[0], a[0], func, bias=ap(bias), scale=scale), [out], [a, bias])
 
     def fill(out, x):
         issue("v", lambda: g.vector.memset(out[0], x), [out], [], f=0.5)
@@ -202,8 +206,8 @@ def rank_program(g, core, T, topo):
     def sfill(name, lo, hi, step, x):
         cp(V(name, lo, hi, step), V("ones", 0, len(range(lo, hi, step))), "s", float(x))
 
-    def scan(out, d0, d1, op0, op1, f=1.0):
-        issue("v", lambda: g.vector.tensor_tensor_scan(out[0], d0[0], d1[0], 0.0, op0, op1), [out], [d0, d1], f=f)
+    def scan(out, d0, d1, op0, op1):
+        issue("v", lambda: g.vector.tensor_tensor_scan(out[0], d0[0], d1[0], 0.0, op0, op1), [out], [d0, d1], f=0.5)
 
     def pickup(out, pat, row):
         scan(out, pat, row, AL.add, AL.min)
@@ -215,7 +219,7 @@ def rank_program(g, core, T, topo):
     def mm(k, n, wq, ws, wlo, xq, xs, xlo):
         o, a, b = bank(k, n), V(wq, wlo, wlo + 128), V(ws, wlo, wlo + 128)
         c, d = V(xq, xlo, xlo + n), V(xs, xlo, xlo + n)
-        issue("t", lambda: g.tensor.matmul_mx(o[0], a[0], b[0], c[0], d[0], True, True), [o], [a, b, c, d], cost=0.0007 * (n + 16))
+        issue("t", lambda: g.tensor.matmul_mx(o[0], a[0], b[0], c[0], d[0], True, True), [o], [a, b, c, d], cost=0.0009 * (n + 16))
 
     def iota(out, pattern, base=0, cm=0, whole=False):
         cost = 0.13 + 0.0017 * out[2]
@@ -224,16 +228,16 @@ def rank_program(g, core, T, topo):
         else:
             issue("g", lambda: g.iota(out[0], pattern, base, cm, allow_small_or_imprecise_dtypes=True), [out], [], cost=cost)
 
-    def dma(e, out, in_, sem):
-        issue(e, lambda: queue[e].dma_start(ap(out), ap(in_)), [out] if isinstance(out, tuple) else [], [in_], sem,
-              cost=0.1, late=LOAD, line=e)
+    def dma(e, out, in_, sem, late=LOAD, behind=()):
+        issue(e, lambda: queue[e].dma_start(ap(out), ap(in_)), [out] if isinstance(out, tuple) else [], [in_] + list(behind), sem,
+              cost=0.1, late=late, line=e)
 
     def u8(a):
         return (a[0].bitcast(dt.uint8), a[1], a[2], 0)
 
-    def double(name, n, upto):
+    def double(name, n, upto, e="s"):
         while n < upto:
-            cp(V(name, n, 2 * n), V(name, 0, n), "s")
+            cp(V(name, n, 2 * n), V(name, 0, n), e)
             n *= 2
 
     def near(a, b):
@@ -259,15 +263,26 @@ def rank_program(g, core, T, topo):
                                                   dma_engine_mask=sum(1 << e for e in es),
                                                   remote_sem=T.sem[sem], src=src[0], dsts=[land[0] for q in to])
                                 for src, to, land, es, sem in parts], local_sem=T.sem.sent)
-        anchor[key] = issue("g", make, [], [p[0] for p in parts], "sent", cost=0.5, line="g")
+        anchor[key] = issue("g", make, [], [p[0] for p in parts], "sent", cost=0.4, line="g")
         total["sent"] = total.get("sent", 0) + sum(len(p[3]) for p in parts)
 
-    def map_plan(q, t):
-        later = list(range(q + 1, N))
-        here = [p for p in later if near(p, q)] if t else []
-        plan = [([p for p in later if p not in here], far_engines(q))]
-        plan += [([p], [e for e in lanes(q, p) if e not in far_engines(q)]) for p in here]
-        return [x for x in plan if x[0]]
+    def ahead(p):
+        return (p + 2) // 2
+
+    def form(q, p):
+        return ("me" if ahead(p) > 1 else "ml") if q == 0 else "mw" if q < ahead(p) else "ml"
+
+    def map_plan(q):
+        far = far_engines(q)
+        later = list(range(N - 1, q, -1))
+        sets = [(f, [p for p in later if not near(p, q) and form(q, p) == f]) for f in ("me", "mw", "ml")]
+        sets = [x for x in sets if x[1]]
+        n = len(far) // max(len(sets), 1)
+        plan = [(f, to, far[n * k:n * k + n]) for k, (f, to) in enumerate(sets)]
+        return plan + [(form(q, p), [p], [e for e in lanes(q, p) if e not in far]) for p in later if near(p, q)]
+
+    def slot(f, t, q):
+        return V("MW", 128 * t + 16 * q, 128 * t + 16 * q + 4) if f == "mw" else V("ML", 64 * t + 8 * q, 64 * t + 8 * q + 4)
 
     def holder(q, t):
         w = (q + HOP[t]) % N
@@ -281,309 +296,310 @@ def rank_program(g, core, T, topo):
         note(None, [], [x for a in views for x in a[1]], sem, n)
         landing.extend((name, m, key, lat) for a in views for name, m in a[1])
 
-    def send_tile(base, to, stage, sem):
-        x, es = 384 * stage + 192, lanes(r, to)
+    def send_tile(base, to, k, side, sem):
+        x, es, d = 640 * k + 192 + 192 * side, lanes(r, to), 192 * (1 - side)
         push([(u8(V("Sq", base, base + 64)), [to], u8(V("Lq", x, x + 64)), es[:len(es) // 2], sem),
-              (V("Ss", base - 192, base + 64), [to], V("Ls", x - 192, x + 64), es[len(es) // 2:], sem)], sem)
+              (V("Ss", base - d, base - d + 256), [to], V("Ls", x - d, x - d + 256), es[len(es) // 2:], sem)], sem)
 
-    def landed(sem, stage, frm):
-        x = 384 * stage + 192
-        arrives(sem, len(lanes(frm, r)), [V("Lq", x, x + 64), V("Ls", x - 192, x + 64)], sem, FLIGHT)
+    def landed(sem, k, side, frm):
+        x, d = 640 * k + 192 + 192 * side, 192 * (1 - side)
+        arrives(sem, len(lanes(frm, r)), [V("Lq", x, x + 64), V("Ls", x - d, x - d + 256)], sem, FLIGHT)
 
     for t in range(R):
         for q in range(r):
-            n = sum(len(es) for to, es in map_plan(q, t) if r in to)
-            arrives("map%d_%d" % (t, q), n, [V("ML", 32 * t + 4 * q, 32 * t + 4 * q + 4)], "map%d" % t,
-                    FLIGHT / 2 if t and q < r - 3 else FLIGHT)
+            f, n = [(f, len(es)) for f, to, es in map_plan(q) if r in to][0]
+            arrives("map%d_%d" % (t, q), n, [slot(f, t, q)], "map%d" % t, FLIGHT)
     away = [t for t in range(R) if holder(r, t) != r]
     guest = {t: [q for q in range(N) if holder(q, t) == r][0] for t in range(R)}
     for k, t in enumerate(away):
-        landed("fa%d" % k, 2 * k, guest[t])
-        landed("ha%d" % k, 2 * k + 1, holder(r, t))
-    arrives("wa", 2 * len(far_engines((r + LENT) % N)), [V("Wl", 0, 512), V("Wm", 0, 512)], "none", 0.0)
+        landed("fa%d" % k, k, 0, guest[t])
+        landed("ha%d" % k, k, 1, holder(r, t))
     wto, far = (r - LENT) % N, far_engines(r)
-    soon = (guest[0] + HOP[0]) % N == r and holder((r - HOP[0]) % N, 0) == r
 
-    dma("y", V("Tt", 0, 1024), T.x[:], "dx")
-    dma("s", V("ut", 0, 512), T.u[:], "du")
-    dma("y", V("Ws", 0, 512), T.ws[:], "dwa")
-    dma("y", u8(V("Wq", 0, 512)), T.wc[:], "dwb")
-    dma("y", V("vt", 0, 512), T.v[:], "dv")
+    def early(q):
+        return holder((q - HOP[0]) % N, 0) != q
+    arrives("wa", (3 if early((r + LENT) % N) else 2) * len(far_engines((r + LENT) % N)), [V("Wl", 0, 512), V("Wm", 0, 512)], "none", 0.0)
 
-    cI, cLO, cHI, cSW, cL8, cAA, cMU, cAU, cM3 = range(9)
-    cH4, cH1, cAC, cW, cA1, cA2, cAK, cSE, cS4, cK1, cK2, cK3, cT0, cT1, cT2 = range(9, 24)
+    dma("s", V("ut", 0, 512), T.u[:], "du", 1.5)
+    dma("y", V("Tt", 0, 512), T.x[:, 0:512], "dx0", 1.8)
+    dma("y", V("Tt", 512, 1024), T.x[:, 512:1024], "dx1", 2.2)
+    dma("y", V("Ws", 0, 512), T.ws[:], "dwa", 2.5)
+    dma("y", u8(V("Wq", 0, 256)), T.wc[:, 0:1024], "dwb", 3.0)
+    dma("y", u8(V("Wq", 256, 512)), T.wc[:, 1024:2048], "dwc", 3.5)
+    dma("y", V("vt", 0, 512), T.v[:], "dv", 4.0)
+
+    cI, cLO, cHI, cS4, cAA, cAC, cMU, cAU, cMV, cAV, cM3, cTI, cIL = range(13)
+    cSW, cU0, cU1, cV0, cV1, cH1, cD1, cD2, cK, cK1, cK2, cK3, cT0, cT1, cT2, cT3 = range(13, 29)
     iota(V("pi", 0, 1), [[0, 1]], 0, 1, True)
-    iota(V("pos", 0, 48), [[1, 48]], -8)
     iota(V("rowa", 0, 16), [[1, 2], [16, 8]])
-    iota(V("Tab", 768, 1024), [[0, 64], [4, 4]])
-    iota(V("Tab", 512, 768), [[0, 16], [4, 4], [0, 4]], -4)
+    iota(V("pos", 0, 48), [[1, 48]], -8)
+    iota(V("Tab", 128, 192), [[0, 16], [4, 4]])
+    iota(V("Tab", 4, 16), [[4, 3], [0, 4]])
+    iota(V("c1", 0, 256), [[16, 16], [0, 4], [1, 4]], 1)
+    iota(V("c1", 3, 256, 4), [[16, 4], [1, 4], [0, 4]], 1)
     iota(V("pos4", 0, 16), [[0, 4], [1, 4]])
-    iota(V("rowb", 0, 12), [[1, 3], [64, 4]])
-    fill(V("ones", 0, 528), 1.0)
+    iota(V("AB", 0, 64), [[64, 4], [4, 4], [16, 4]])
+    fill(V("ones", 0, 448), 1.0)
+    fill(V("ones", 320, 321), 0.0)
+    fill(col(cTI), -TINY)
+    fill(V("Z", 0, 528), 0.0)
+    issue("g", lambda: g.affine_select(T.Z[:, 3:515:4], T.ones[:, 0:128], [[1, 128]], AL.is_equal, 0.0, 0, -1),
+          [V("Z", 3, 515, 4)], [V("ones", 0, 128)], cost=0.39)
+    push([(V("Ws", 0, 512), [wto], V("Wm", 0, 512), far, "wa")], "w0")
+
+    def lend(lo, hi):
+        push([(u8(V("Wq", lo, hi)), [wto], u8(V("Wl", lo, hi)), far, "wa")], "w%d" % hi)
+    if early(r):
+        lend(0, 256)
+    cp(V("ul", 0, 16), V("rowa", 0, 16))
     ts(V("pi", 1, 2), V("pi", 0, 1), 15, AL.bitwise_and)
     ts(V("pi", 2, 3), V("pi", 0, 1), 3, AL.bitwise_and)
     ts(V("pi", 3, 4), V("pi", 0, 1), 2, AL.arith_shift_right, 3, AL.bitwise_and)
     cp(V("sc", 0, 3), V("pi", 1, 4))
-    iota(V("c1", 3, 256, 4), [[1, 4], [0, 16]])
-    iota(V("c1", 0, 256, 4), [[16, 4], [1, 4], [0, 4]])
-    iota(V("c1", 1, 256, 4), [[16, 4], [1, 4], [0, 4]])
-    iota(V("c1", 2, 256, 4), [[16, 16], [0, 4]], 3)
-    push([(V("Ws", 0, 512), [wto], V("Wm", 0, 512), far, "wa")], "w0")
-    iota(V("Pb", 0, 16), [[0, 4], [4, 4]])
-    iota(V("rowc", 0, 16), [[16, 16]], -1)
-    iota(V("BB", 0, 16), [[0, 4], [4, 4]])
-    iota(V("cE", 0, 16), [[1, 4], [0, 4]])
-    iota(V("cE", 16, 32), [[0, 4], [1, 4]])
-    iota(V("cE", 32, 48), [[0, 4], [16, 4]], 3)
-    iota(V("cB", 0, 64), [[0, 4], [16, 4], [1, 4]])
-    iota(V("AB", 0, 64), [[0, 4], [4, 4], [0, 4]])
-    issue("g", lambda: g.affine_select(T.Z[:, 0:516], T.ones[:, 0:516], [[1, 516]], AL.is_equal, 0.0, -3, -4),
-          [V("Z", 0, 516)], [V("ones", 0, 516)], cost=1.05)
-    ts(col(cL8), col(cLO), 8.0, AL.mult)
     ts(col(cSW), col(cLO), 4.0, AL.mult, col(cHI), AL.add)
+    ts(col(cU1), col(cLO), 8.0, AL.mult, 8.0, AL.add)
+    ts(col(cU0), col(cSW), 2.0, AL.mult)
+    ts(col(cV0), col(cHI), 8.0, AL.mult)
+    ts(col(cV1), col(cI), 2.0, AL.mult, 2.0, AL.add)
     ts(col(cH1), col(cHI), 1.0, AL.add)
     ts(col(cAA), col(cI), 15.0, AL.is_lt, 256.0, AL.mult)
     ts(col(cAC), col(cHI), 3.0, AL.is_lt, 256.0, AL.mult)
-    ts(col(cT0), col(cLO), 2.0, AL.is_ge, 2.0, AL.mult)
-    ts(col(cMU), col(cLO), 3.0, AL.is_equal, 1.0 / BIG, AL.max)
-    ts(col(cM3), col(cHI), 3.0, AL.is_lt, 0.25, AL.mult)
-    ts(col(cAU), col(cHI), 256.0, AL.mult, -85.0, AL.add)
-    cp(V("ul", 0, 16), V("rowa", 0, 16))
+    ts(col(cT0), col(cLO), 3.0, AL.is_equal, 1.0 / BIG, AL.max)
+    ts(col(cT1), col(cI), 15.0, AL.is_equal, 1.0 / BIG, AL.max)
+    ts(col(cM3), col(cHI), 0.0, AL.is_equal, 4.0, AL.mult)
+    cp(col(cMU), col(cT0), "s", 0.5)
+    cp(col(cMV), col(cT1), "s", 0.5)
     cp(col(cS4), col(cSW), "s", 4.0)
-    cp(col(cH4), col(cHI), "s", 4.0)
-    affine(col(cW), col(cLO), 1.0, col(cT0))
-    affine(col(cT1), col(cLO), 1.0, col(cAC))
-    affine(col(cT2), col(cI), 1.0, col(cAA))
-    affine(col(cA1), col(cW), 16.0, col(cAC))
-    affine(col(cA2), col(cW), 64.0, col(cAC))
+    affine(col(cD2), col(cLO), 64.0, col(cAC))
+    affine(col(cT2), col(cLO), 1.0, col(cAC))
+    ts(col(cD1), col(cT2), 12.0, AL.add)
+    ts(col(cT3), col(cLO), col(cHI), AL.subtract, 3.0, AL.mult)
+    ts(col(cK), col(cT3), col(cAC), AL.subtract, 12.0, AL.add)
+    ts(col(cIL), col(cI), -208.0, AL.add)
+    ts(col(cK1), col(cI), 16.0, AL.add)
+    ts(col(cK2), col(cI), 32.5, AL.add)
+    ts(col(cK3), col(cI), 48.5, AL.add)
 
-    def horner(name, n, start, fours, stop, o):
-        ts(V("tmp", o, o + 48), V("pos", 0, 48), start, AL.is_equal)
-        at = lambda k: V("tmp", o + 8 - k, o + 8 - k + n)
-        acc, top = V("tmp", o + 64, o + 64 + n), V("tmp", o + 96, o + 96 + n)
-        ts(top, at(stop), BIG, AL.mult)
-        tt(acc, at(fours[0]), at(fours[1]), AL.add)
-        for k in fours[2:]:
-            tt(acc, acc, at(k), AL.add)
-        ts(acc, acc, 3.0, AL.mult, 1.0, AL.add)
-        tt(acc, acc, at(0), AL.subtract)
-        tt(V(name, 0, n), acc, top, AL.max)
+    def horner(name, start, stop, o, mu, au):
+        p, a, b, c = V("pos", 8, 40), V("tmp", o, o + 32), V("tmp", o + 32, o + 64), V("tmp", o + 64, o + 96)
+        ts(a, p, stop, AL.is_lt, 1.0, AL.add)
+        ts(b, p, start, AL.not_equal)
+        ts(c, p, stop, AL.is_equal, BIG, AL.mult)
+        tt(a, a, b, AL.mult)
+        tt(V(name, 0, 32), a, c, AL.max)
+        tt(V(name, 32, 64), a, c, AL.max)
+        double(name, 64, 256)
+        scan(V("su", o, o + 32), V(name, 0, 32), V("ones", 0, 32), AL.mult, AL.add)
+        ts(au, V("su", o + 31, o + 32), mu, AL.mult)
 
-    def marks(name, a, sa, b, sb, at):
+    def marks(name, a, sa, b, sb, at, n):
         ts(V("tmp", at, at + 16), a, sa, AL.is_equal, 512.0, AL.mult)
         ts(V("tmp", at + 16, at + 32), b, sb, AL.is_equal, 256.0, AL.mult)
-        tt(V(name, 0, 16), V("tmp", at, at + 16), V("tmp", at + 16, at + 32), AL.subtract)
+        for k in range(2):
+            tt(V(name, 16 * k, 16 * k + 16), V("tmp", at, at + 16), V("tmp", at + 16, at + 32), AL.subtract)
+        double(name, 32, n)
 
-    horner("PU", 32, col(cL8), [2, 4, 6], 8, 0)
-    horner("PD", 16, col(cH4), [1, 2], 3, 128)
-    marks("PB", V("pos", 8, 24), col(cSW), V("pos", 7, 23), col(cSW), 256)
-    marks("PA", V("pos", 8, 24), col(cI), V("pos", 7, 23), col(cI), 288)
-    marks("PC", V("pos4", 0, 16), col(cHI), V("pos4", 0, 16), col(cH1), 320)
-    for name, n, upto in (("PU", 32, 512), ("PB", 16, 64), ("PA", 16, 256), ("PC", 16, 256), ("PD", 16, 256)):
-        double(name, n, upto)
-    sfill("Tab", 288, 304, 1, 0)
-    sfill("Tab", 304, 320, 1, 4)
+    horner("PU", col(cU0), col(cU1), 0, col(cMU), col(cAU))
+    marks("PA", V("pos", 8, 24), col(cI), V("pos", 7, 23), col(cI), 288, 256)
+    marks("PB", V("pos", 8, 24), col(cSW), V("pos", 7, 23), col(cSW), 256, 64)
+    marks("PC", V("pos4", 0, 16), col(cHI), V("pos4", 0, 16), col(cH1), 320, 256)
+    horner("PV", col(cV0), col(cV1), 128, col(cMV), col(cAV))
     sfill("Tab", 192, 256, 1, 0)
-    cp(V("Tab", 272, 288), V("Tab", 768, 784), "s")
-    cp(V("Tab", 128, 192), V("Tab", 768, 832), "s")
+    sfill("Tab", 32, 48, 1, 0)
+    sfill("Tab", 48, 64, 1, 4)
+    cp(V("Tab", 0, 4), V("Tab", 128, 132), "s")
+    cp(V("Tab", 16, 32), V("Tab", 128, 144), "s")
     for k in range(4):
-        sfill("Tab", 512 + k, 768, 16, 4 * k)
-    cp(V("Tab", 256, 272), V("Tab", 512, 528), "s")
-    cp(V("Tab", 64, 128), V("Tab", 512, 576), "s")
-    cp(V("Tab", 0, 64), V("Tab", 256, 320), "s")
-    cp(V("Tab", 320, 384), V("Tab", 256, 320), "s")
-    cp(V("Tab", 384, 512), V("Tab", 256, 384), "s")
-    for z in range(4):
-        sfill("c1", 64 * z + 35, 64 * z + 48, 4, 16 * z + 3)
-        sfill("c1", 64 * z + 51, 64 * z + 64, 4, 16 * (z + 1) if z < 3 else 16 * (r + 1))
+        cp(V("Tab", 64 + 16 * k, 80 + 16 * k), V("Tab", 0, 16), "s")
     quant("uq", "us", 0, 128, V("ut", 0, 512))
     pa, pb, po = V("Uq", 0, 256), V("uq", 0, 128), V("ul", 0, 16)
     issue("v", lambda: g.vector.tensor_copy(pa[0].bitcast(dt.uint32), pb[0].bitcast(dt.uint32).indirect(po[0])),
           [pa], [pb, po], cost=0.38)
     cp(V("Us", 0, 256), ind(V("us", 0, 128), V("ul", 0, 16)), "s")
-    ts(V("El", 0, 12), V("rowb", 0, 12), col(cS4), AL.add)
-    affine(V("lc", 0, 16), V("rowc", 0, 16), 1.0, col(cT2))
+    ts(V("Fl", 0, 4), V("pos", 8, 12), 64.0, AL.mult, col(cS4), AL.add)
+    ts(V("Kl", 0, 4), V("pos", 8, 12), 4.0, AL.mult, col(cLO), AL.add)
+    affine(V("lc", 0, 16), V("pos", 8, 24), 16.0, col(cI))
+    cp(V("BB", 0, 64, 4), V("pos", 8, 24), "s", 4.0)
+    fill(V("Pp", 0, 64), 0.0)
+    cp(V("Pp", 0, 16, 4), V("pos", 5, 9), "s", 4.0)
     for b in range(4):
         quant("Eq", "Es", 128 * b, 128, V("Z", 3 - b, 515 - b))
-    ts(V("Fl", 0, 1), col(cI), 4.0, AL.mult)
-    ts(V("Fl", 1, 2), col(cSW), 4.0, AL.mult, 1.0, AL.add)
-    ts(V("Fl", 2, 3), col(cSW), 4.0, AL.mult, 2.0, AL.add)
-    ts(V("Pl", 0, 1), col(cLO), 16.0, AL.mult, col(cHI), AL.add)
-    ts(col(cAK), col(cT1), -336.0, AL.add)
-    ts(col(cSE), col(cI), -64.0 * r, AL.add)
-    ts(col(cK1), col(cI), 16.0, AL.add)
-    ts(col(cK2), col(cI), 32.5, AL.add)
-    ts(col(cK3), col(cI), 48.5, AL.add)
-    fill(V("z0", 0, 2), 0)
-    fill(V("Ft", 256, 512), 0.0)
-    fill(V("Ht", 256, 512), 0.0)
-    fill(V("zt", 0, 512), 0.0)
+    for k in range(3):
+        sfill("RR", 256 * k, 256 * k + 256, 1, 0)
+    sfill("QQ", 0, 192, 1, 0)
+    sfill("L3", 0, 280, 1, 0)
+    sfill("L3", 280, 560, 1, 0)
+    fill(V("FH", 0, 512), 0.0)
     fill(V("Hd", 0, 320, 80), 0.0)
     if r == 0:
-        cp(V("ch", 128, 129), col(cI))
-    for st in range(4):
-        quant("Lq", "Ls", 384 * st + 256, 128, V("zt", 0, 512))
+        cp(V("e0", 0, 1), col(cI))
+    for k in range(len(away)):
+        quant("Lq", "Ls", 640 * k + 256, 128, V("FH", 0, 512))
     quant("vq", "vs", 0, 128, V("vt", 0, 512))
-
-    def one(e, t, lo, hi, step=1):
-        sfill("Flg", 16 * lo + 4 * e + t, 16 * (hi - 1) + 4 * e + t + 1, 16 * step, 1)
+    sfill("Flg", 0, 192, 1, 0)
+    sfill("Flg", 192, 256, 1, 1)
+    sfill("Flg", 256, 448, 1, 0)
+    for args in ((256, 320, 4), (320, 385, 16), (400, 416, 4), (416, 432, 1)):
+        sfill("Flg", *args, 1)
     for k in range(4):
-        sfill("Flg", 256 * k, 256 * k + 256, 1, 0)
-    for e in range(4):
-        one(e, e, 0, 64)
-    for args in ((0, 1, 0, 16), (2, 3, 0, 64, 4), (0, 2, 16, 32), (0, 2, 0, 4), (1, 3, 0, 64, 16), (0, 3, 32, 48),
-                 (0, 3, 16, 32, 4), (0, 3, 4, 8), (0, 3, 0, 1)):
-        one(*args)
-    for k in range(4):
-        one(1, 2, k, 64, 16)
-        one(1, 3, 4 + k, 64, 16)
-
-    def rest_of_w():
-        push([(u8(V("Wq", 0, 512)), [wto], u8(V("Wl", 0, 512)), far, "wa")], "w1")
+        sfill("Flg", 324 + k, 400, 16, 1)
 
     def count(c, lo, hi, at):
         o, s, k, bias = V("junk", at, at + hi - lo), V("sa", c, c + 1), V("K1", lo, hi), col(cK3 if c == 3 else cK2)
         issue("s", lambda: g.scalar.activation(o[0], k[0], AF.Sign, bias=bias[0], scale=-1.0, accum_out=s[0]), [o, s], [k, bias])
 
-    def reduce(c, lo, hi):
-        o, k = V("sa", c, c + 1), V("le", lo, hi)
-        issue("v", lambda: g.vector.tensor_reduce(o[0], k[0], AxisListType.X, AL.add), [o], [k])
-
     def update(lo, hi):
         for b in range(4):
             w = V("Tt", 64 * lo + b, 64 * hi, 4)
-            tt(w, ind(V("Hd", 80 * b, 80 * b + 65), V("kl", lo, hi)), w, AL.add)
+            tt(w, ind(V("Hd", 80 * b, 80 * b + 65), V("kl", lo, hi)), w, AL.add, "T")
 
     for t in range(R):
-        qt, qf, qh = 512 * t, 512 * t + 256, 512 * t + 384
+        qh, qt, qf = 512 * t, 512 * t + 128, 512 * t + 384
         for h in range(2):
             quant("Sq", "Ss", qt + 128 * h, 128, V("Tt", 512 * h, 512 * h + 512))
-            mm(6 * h + 1, 128, "Uq", "Us", 128, "Sq", "Ss", qt + 128 * h)
-            mm(6 * h, 128, "Uq", "Us", 0, "Sq", "Ss", qt + 128 * h)
-        for h in range(2):
-            ts(V("bits", 256 * h, 256 * h + 256, 2), bank(6 * h + 1, 128), 0.0, AL.is_gt, 2.0, AL.mult)
-            ts(V("bits", 256 * h + 1, 256 * h + 256, 2), bank(6 * h, 128), 0.0, AL.is_gt, 1.0, AL.add)
+            for b in (1, 0):
+                mm(6 * h + b, 128, "Uq", "Us", 128 * b, "Sq", "Ss", qt + 128 * h)
+                affine(V("bits", 256 * h + 1 - b, 256 * h + 256, 2), bank(6 * h + b, 128), 1.0, col(cTI), AF.Sign)
+            scan(V("su", 256 * h, 256 * h + 256), V("PU", 0, 256), V("bits", 256 * h, 256 * h + 256), AL.mult, AL.add)
+            ts(V("cod", 8 * h, 8 * h + 8), V("su", 256 * h + 31, 256 * h + 256, 32), col(cMU), AL.mult, col(cAU), AL.add)
+            tt(V("N1", 128 * h, 128 * h + 128), ind(V("Tab", 0, 256), V("cod", 8 * h, 8 * h + 8)), V("c1", 128 * h, 128 * h + 128), AL.add)
         for b in range(4):
             mm(2 + b, 256, "Eq", "Es", 128 * b, "Sq", "Ss", qt)
-            cp(V("Vh", 256 * b, 256 * b + 256), bank(2 + b, 256), "s", 0.5)
-            cp(V("Vg", 256 * b, 256 * b + 256), bank(2 + b, 256), "s", 0.5)
-        scan(V("su", 0, 512), V("PU", 0, 512), V("bits", 0, 512), AL.mult, AL.add)
-        ts(V("cod", 0, 16), V("su", 31, 512, 32), col(cMU), AL.mult, col(cAU), AL.add)
-        tt(V("N1", 0, 256), ind(V("Tab", 0, 1024), V("cod", 0, 16)), V("c1", 0, 256), AL.add)
-        cp(V("X1", 0, 256), ind(V("Tab", 0, 1024), V("cod", 0, 16)), "s")
-        cp(V("AB", 64, 256), ind(V("X1", 0, 256), V("El", 0, 12)), "s")
+            cp(V("Vh", 256 * b, 256 * b + 256), bank(2 + b, 256), "s", 0.5, "V")
+            cp(V("Vg", 256 * b, 256 * b + 256), bank(2 + b, 256), "s", 0.5, "V")
         for u in (2, 1, 0):
-            pickup(V("s1", 64 * u, 64 * u + 64), V("PB", 0, 64), V("N1", u, 256, 4))
-        ts(V("W1", 0, 12), V("s1", 15, 192, 16), col(cAA), AL.add)
-        cp(V("Rb", 0, 64), ind(V("N1", 0, 256), V("W1", 8, 12)))
-        cp(V("Rb", 64, 128), ind(V("Rb", 0, 64), V("W1", 4, 8)))
-        cp(V("Rb", 128, 192), ind(V("Rb", 64, 128), V("W1", 0, 4)))
-        cp(V("T12", 0, 64), ind(V("AB", 192, 256), V("W1", 4, 8)), "s")
-        cp(V("AB", 256, 320), ind(V("AB", 128, 192), V("W1", 0, 4)), "s")
-        cp(V("AB", 320, 384), ind(V("T12", 0, 64), V("W1", 0, 4)), "s")
+            pickup(V("s1", 64 * u, 64 * u + 64), V("PA" if u else "PB", 0, 64), V("N1", u, 256, 4))
+        ts(V("W1", 8, 12), V("s1", 143, 192, 16), col(cAA), AL.add)
+        ts(V("W1", 0, 8), V("s1", 15, 128, 16), col(cAA), AL.add)
+        cp(V("RR", 2, 256, 4), ind(V("N1", 0, 256), V("W1", 8, 12)))
+        cp(V("RR", 257, 512, 4), ind(V("RR", 0, 256), V("W1", 4, 8)))
+        cp(V("Rb", 0, 64), ind(V("RR", 256, 512), V("W1", 0, 4)))
+        cp(V("RR", 513, 768, 4), ind(V("N1", 0, 256), V("W1", 4, 8)), "s")
+        cp(V("AB", 64, 128), ind(V("N1", 0, 256), V("Fl", 0, 4)), "s")
+        cp(V("AB", 128, 192), ind(V("N1", 0, 256), V("W1", 0, 4)), "s")
+        cp(V("AB", 192, 256), ind(V("RR", 512, 768), V("W1", 0, 4)), "s")
         for v in (2, 1, 0):
-            pickup(V("s2", 16 * v, 16 * v + 16), V("PB" if v else "PA", 0, 16), V("Rb", 128 + v, 192, 4))
-        ts(V("W2", 0, 6, 2), V("s2", 15, 48, 16), col(cAA), AL.add)
-        cp(V("Qb", 0, 16), ind(V("Rb", 128, 192), V("W2", 4, 5)))
-        cp(V("Qb", 16, 32), ind(V("Qb", 0, 16), V("W2", 2, 3)))
-        cp(V("Pb", 16, 32), ind(V("Qb", 16, 32), V("W2", 0, 1)))
-        pickup(V("s3", 0, 16), V("PA", 0, 16), V("Pb", 16, 32))
-        ts(V("W3", 0, 1), V("s3", 15, 16), col(cAA), AL.add, col(cM3), AL.mult)
-        cp(V("Pb", 32, 48), ind(V("Pb", 16, 32), V("W3", 0, 1)))
-        anchor["map%d" % t] = cp(V("Pb", 48, 64), ind(V("Pb", 32, 48), V("W3", 0, 1)))
+            pickup(V("s2", 16 * v, 16 * v + 16), V("PA", 0, 16), V("Rb", v, 64, 4))
+        ts(V("W2", 4, 5), V("s2", 47, 48), col(cAA), AL.add)
+        ts(V("W2", 0, 4, 2), V("s2", 15, 32, 16), col(cAA), AL.add)
+        cp(V("QQ", 2, 64, 4), ind(V("Rb", 0, 64), V("W2", 4, 5)))
+        cp(V("QQ", 65, 128, 4), ind(V("QQ", 0, 64), V("W2", 2, 3)))
+        ts(V("Wc", 0, 16), ind(V("QQ", 64, 128), V("W2", 0, 1)), 4.0, AL.mult)
+        cp(V("L3", 0, 256, 16), ind(V("QQ", 64, 128), V("W2", 0, 1)), "s")
+        cp(V("QQ", 129, 192, 4), ind(V("Rb", 0, 64), V("W2", 2, 3)), "s")
+        cp(V("BB", 1, 64, 4), V("Rb", 0, 64, 4), "s")
+        cp(V("BB", 2, 64, 4), ind(V("Rb", 0, 64), V("W2", 0, 1)), "s")
+        cp(V("BB", 3, 64, 4), ind(V("QQ", 128, 192), V("W2", 0, 1)), "s")
+        cp(V("L3", 336, 400), ind(V("L3", 48, 256), V("Wc", 8, 12)))
+        cp(V("L3", 496, 560), ind(V("L3", 48, 256), V("Wc", 4, 8)), "s")
+        pickup(V("s3", 0, 16), V("PA", 0, 16), V("L3", 0, 256, 16))
+        cp(V("L3", 416, 480), ind(V("L3", 256, 400), V("Wc", 4, 8)))
+        anchor["map%d" % t] = ts(V("W0", 0, 1), V("s3", 15, 16), col(cAA), AL.add, col(cM3), AL.mult)
+        last = ind(V("L3", 400, 480), V("W0", 0, 1))
+        for f in sorted({f for f, to, es in map_plan(r)}):
+            o = V(f, 16 * t, 16 * t + 16)
+            if f == "ml":
+                ts(o, last, 4.0, AL.mult, col(cIL), AL.add)
+            elif f == "me":
+                ts(o, last, 0.25, AL.mult, -13.0, AL.add)
+            else:
+                cp(o, last, "s")
         if r < N - 1:
-            cp(V("mp", 16 * t, 16 * t + 16), ind(V("Pb", 48, 64), V("W3", 0, 1)))
-            push([(V("mp", 16 * t, 16 * t + 4), to, V("ML", 32 * t + 4 * r, 32 * t + 4 * r + 4), es, "map%d_%d" % (t, r))
-                  for to, es in map_plan(r, t)], "map%d" % t)
-        if t == 0 and not soon:
-            rest_of_w()
+            push([(V(f, 16 * t, 16 * t + 4), to, slot(f, t, r), es, "map%d_%d" % (t, r)) for f, to, es in map_plan(r)], "map%d" % t)
+        if t == 0 and early(r):
+            lend(256, 512)
         for h in range(2):
-            tt(V("nr", 128 * h, 128 * h + 128), V("bits", 256 * h, 256 * h + 256, 2), V("bits", 256 * h + 1, 256 * h + 256, 2), AL.add)
-        tt(V("BB", 16, 64), ind(V("Rb", 128, 192), V("Fl", 0, 3)), V("cE", 0, 48), AL.subtract)
-        ts(V("Pp", 0, 16), ind(V("Pb", 0, 64), V("Pl", 0, 1)), 0.25, AL.mult)
-        pickup(V("s7", 0, 256), V("PA", 0, 256), V("nr", 0, 256))
-        cp(V("T2", 0, 16), ind(V("BB", 48, 64), V("W2", 2, 3)))
-        cp(V("BB", 64, 80), ind(V("BB", 32, 48), V("W2", 0, 1)))
-        pickup(V("s4", 0, 16), V("PC", 0, 16), V("Pp", 0, 16))
-        tt(V("lf", 0, 16), V("s7", 15, 256, 16), V("lc", 0, 16), AL.add)
-        cp(V("BB", 80, 96), ind(V("T2", 0, 16), V("W2", 0, 1)))
-        ts(V("D1", 0, 4), V("s4", 3, 16, 4), col(cA1), AL.add)
+            scan(V("sv", 256 * h, 256 * h + 256), V("PV", 0, 256), V("bits", 256 * h, 256 * h + 256), AL.mult, AL.add)
+        ts(V("kd", 0, 16), V("sv", 31, 512, 32), col(cMV), AL.mult, col(cAV), AL.add)
+        ts(V("kd", 16, 32), V("kd", 0, 16), 3, AL.bitwise_and)
+        ts(V("kd", 32, 48), V("kd", 0, 16), 252, AL.bitwise_and)
+        tt(V("lf", 0, 16), V("kd", 16, 32), V("lc", 0, 16), AL.add)
         ts(V("ll", 0, 16), V("lf", 0, 16), 255.0, AL.min)
-        tt(V("BC", 0, 64), ind(V("BB", 0, 96), V("D1", 0, 4)), V("cB", 0, 64), AL.add)
-        scan(V("s8", 0, 256), V("PD", 0, 256), V("nr", 0, 256), AL.mult, AL.add)
-        pickup(V("s5", 0, 64), V("PC", 0, 64), V("BC", 0, 64))
-        ts(V("ck", 0, 16), V("s8", 15, 256, 16), 16.0 / BIG, AL.mult, col(cAK), AL.add)
-        ts(V("D2", 0, 16), V("s5", 3, 64, 4), col(cA2), AL.add)
-        cp(V("Pre", 0, 256), ind(V("AB", 0, 384), V("D2", 0, 16)), "s")
+        ts(V("ck", 16, 32), V("kd", 32, 48), 1.0 / 64, AL.mult, col(cK), AL.add)
+        tt(V("ck", 0, 16), V("ck", 16, 32), V("lc", 0, 16), AL.add)
+        pickup(V("s5", 0, 64), V("PC", 0, 64), V("BB", 0, 64))
+        ts(V("D2", 0, 16), V("s5", 3, 64, 4), col(cD2), AL.add)
+        cp(V("Pre", 0, 256), ind(V("AB", 0, 256), V("D2", 0, 16)), "s")
+        pickup(V("s6", 0, 256), V("PC", 0, 256), V("Pre", 0, 256))
+        tt(V("Kq", 0, 64), ind(V("ck", 0, 16), V("Kl", 0, 4)), V("s6", 3, 256, 4), AL.subtract)
+        cp(V("Pp", 1, 16, 4), V("L3", 0, 64, 16), "s")
+        cp(V("Pp", 2, 64, 4), ind(V("L3", 48, 256), V("W0", 0, 1)), "s")
+        cp(V("Pp", 3, 64, 4), ind(V("L3", 480, 560), V("W0", 0, 1)), "s")
+        pickup(V("s4", 0, 16), V("PC", 0, 16), V("Pp", 0, 16))
+        ts(V("D1", 0, 4), V("s4", 3, 16, 4), col(cD1), AL.add)
+        cp(V("XX", 0, 64), ind(V("Kq", 0, 64), V("D1", 0, 4)))
         for b in range(4):
             for h in range(2):
                 lo = 256 * b + 128 * h
-                tt(V("G", lo, lo + 128), ind(V("Vh", 256 * b, 256 * b + 256), V("ll", 8 * h, 8 * h + 8)), V("Vg", lo, lo + 128), AL.add)
-        pickup(V("s6", 0, 256), V("PC", 0, 256), V("Pre", 0, 256))
-        for e in range(4):
-            tt(V("Kw", 16 * e, 16 * e + 16), V("s6", 64 * e + 3, 64 * e + 64, 4), V("ck", 0, 16), AL.add)
-        for q in range(r):
-            src = ind(V("ML", 32 * t, 32 * t + 4 * q + 4), V("ch", 16 * q - 16, 16 * q - 15) if q else V("z0", 0, 1))
-            if q < r - 1:
-                ts(V("ch", 16 * q, 16 * q + 16), src, 0.25, AL.mult)
+                tt(V("G", lo, lo + 128), ind(V("Vh", 256 * b, 256 * b + 256), V("ll", 8 * h, 8 * h + 8)), V("Vg", lo, lo + 128), AL.add, "G")
+        x = 0
+        for q in range(r - 1, ahead(r) - 1, -1):
+            cp(V("XX", x + 64, x + 128), ind(V("XX", x, x + 64), slot("ml", t, q)), "s")
+            x += 64
+        at = V("ML", 64 * t, 64 * t + 1) if r else V("e0", 0, 1)
+        for q in range(1, min(ahead(r), r)):
+            src, o = ind(slot("mw", t, q), at), V("ch", 16 * q, 16 * q + 16)
+            if q < ahead(r) - 1:
+                ts(o, src, 0.25, AL.mult, -13.0, AL.add)
             else:
-                ts(V("ch", 128, 144), src, 4.0, AL.mult, col(cSE), AL.add)
-        cp(V("key", 0, 16), ind(V("Kw", 0, 64), V("ch", 128, 129)))
-        cp(V("m", 0, 256), ind(V("Flg", 0, 1024), V("key", 0, 16)))
-        scan(V("K1", 0, 256), V("ones", 0, 256), V("m", 0, 256), AL.mult, AL.add, 0.5)
+                ts(o, src, 4.0, AL.mult, col(cIL), AL.add)
+            at = V("ch", 16 * q, 16 * q + 1)
+        others[ts(V("key", 0, 16), ind(V("XX", x, x + 64), at), 16.0, AL.mult)] = anchor["map%d" % t]
+        for h in range(2):
+            cp(V("m", 128 * h, 128 * h + 128), ind(V("Flg", 0, 448), V("key", 8 * h, 8 * h + 8)), "vs"[h])
+        scan(V("K1", 0, 256), V("ones", 0, 256), V("m", 0, 256), AL.mult, AL.add)
         count(3, 48, 256, 0)
         count(2, 32, 192, 208)
-        ts(V("le", 64, 192), V("K1", 0, 128), col(cK1), AL.is_le)
+        ts(V("le", 64, 192), V("K1", 0, 128), col(cK1), AL.is_le, f=0.5)
         ts(V("le", 0, 64), V("K1", 0, 64), col(cI), AL.is_le)
-        reduce(1, 64, 192)
-        reduce(0, 0, 64)
+        scan(V("ls", 0, 192), V("ones", 256, 448), V("le", 0, 192), AL.mult, AL.add)
         ts(V("sl", 3, 4), V("sa", 3, 4), 0.5, AL.mult, 152.0, AL.add)
-        cp(V("sl", 0, 2), V("sa", 0, 2))
+        cp(V("sl", 0, 2), V("ls", 63, 192, 128))
         ts(V("sl", 2, 3), V("sa", 2, 3), 0.5, AL.mult, 112.0, AL.add)
         for b in range(4):
-            cp(V("Ft", b, 256, 4), ind(V("G", 256 * b, 256 * b + 256), V("sl", 0, 4)), "vs"[b % 2])
-        quant("Sq", "Ss", qf, 128, V("Ft", 0, 512))
+            cp(V("FH", b, 256, 4), ind(V("G", 256 * b, 256 * b + 256), V("sl", 0, 4)), "vs"[b % 2])
+        quant("Sq", "Ss", qf, 128, V("FH", 0, 512))
         k = away.index(t) if t in away else None
         if k is not None:
-            send_tile(qf, holder(r, t), 2 * k, "fa%d" % k)
-        if t == R - 1:
-            cp(V("sf", 0, 4), V("sl", 0, 4))
-            for c in range(4):
-                dma("y", T.ol[:, 16 * c:16 * c + 16], V("sf", c, c + 1), "oy")
+            send_tile(qf, holder(r, t), k, 0, "fa%d" % k)
         wq, ws = ("Wq", "Ws") if (guest[t] + HOP[t]) % N == r else ("Wl", "Wm")
         for b in range(4):
             if k is None:
                 mm(2 + b, 128, wq, ws, 128 * b, "Sq", "Ss", qf)
             else:
-                mm(2 + b, 128, wq, ws, 128 * b, "Lq", "Ls", 768 * k + 192)
+                mm(2 + b, 128, wq, ws, 128 * b, "Lq", "Ls", 640 * k + 192)
         pickup(V("s9", 0, 256), V("PA", 0, 256), V("K1", 0, 256))
         ts(V("ka", 0, 16), V("s9", 15, 256, 16), col(cAA), AL.add, -1.0, AL.add)
         ts(V("kb", 0, 16), V("ka", 0, 16), 63, AL.bitwise_and)
         tt(V("kc", 0, 16), V("ka", 0, 16), V("kb", 0, 16), AL.min)
         ts(V("kl", 0, 16), V("kc", 0, 16), 1.0, AL.add)
         for b in range(4):
-            cp(V("Ht", b, 256, 4), bank(2 + b, 64), "sv"[b % 2], 0.03125)
-        quant("Sq", "Ss", qh, 128, V("Ht", 0, 512))
+            cp(V("FH", 512 + b, 768, 4), bank(2 + b, 64), "sv"[b % 2], 0.03125)
+        quant("Sq", "Ss", qh, 128, V("FH", 256, 768))
         if k is not None:
-            send_tile(qh, guest[t], 2 * k + 1, "ha%d" % k)
-        if t == 0 and soon:
-            rest_of_w()
+            send_tile(qh + 64, guest[t], k, 1, "ha%d" % k)
+        if t == 0 and not early(r):
+            lend(0, 512)
         banks = (0, 1, 6, 7)
         for b in range(4):
             if k is None:
                 mm(banks[b], 128, "Eq", "Es", 128 * b, "Sq", "Ss", qh)
             else:
-                mm(banks[b], 128, "Eq", "Es", 128 * b, "Lq", "Ls", 768 * k + 576)
-            cp(V("Hd", 80 * b + 1, 80 * b + 65), bank(banks[b], 64), "s" if b else "v")
+                mm(banks[b], 128, "Eq", "Es", 128 * b, "Lq", "Ls", 640 * k + 320)
+            cp(V("Hd", 80 * b + 1, 80 * b + 65), bank(banks[b], 64, 64), "s" if b else "v")
+        if t == R - 1:
+            cp(V("sf", 0, 4), V("sl", 0, 4))
+            for c in range(4):
+                dma("y", T.ol[:, 16 * c:16 * c + 16], V("sf", c, c + 1), "oy", behind=[V("Hd", 1, 2)])
         update(0, 8)
         update(8, 16)
-    qt = 512 * R
+    qt = 512 * R + 128
     for h in range(2):
         lo = qt + 128 * h
         quant("Sq", "Ss", lo, 128, V("Tt", 512 * h, 512 * h + 512))
         mm(2 + h, 128, "vq", "vs", 0, "Sq", "Ss", lo)
         dma("y", T.oc[:, 512 * h:512 * h + 512], u8(V("Sq", lo, lo + 128)), "oy")
-        cp(V("ys", 128 * h, 128 * h + 128), bank(2 + h, 128), "sv"[h])
+        cp(V("ys", 128 * h, 128 * h + 128), bank(2 + h, 128), "s")
         if h:
             for k in range(4):
                 src = (T.Ss[32 * k:32 * k + 4, qt:qt + 256], V("Ss", qt, qt + 256)[1], 256, 0)

@@ -4,10 +4,11 @@ from concourse.mybir import dt, AluOpType, AxisListType, ActivationFunctionType
 N, C, A, R = 8, 256, 64, 3
 HOP = [1, 2, 3]
 LENT = HOP[1]
+WHOLE = 2
 X4, U8, BF, F32, I32, U16 = "float8_e4m3fn_x4", "uint8", "bfloat16", "float32", "int32", "uint16"
 BIG = float(2 ** 40)
 TINY = 1e-35
-WAIT, FLIGHT, LOAD, SLACK = 0.17, 2.4, 2.0, 0.05
+WAIT, LOAD, SLACK, CALL, FIRST, START, ROW, BYTE, WAKE, DOUBT = 0.17, 1.5, 0.05, 0.3, 2.0, 0.8, 0.015, 7e-5, 0.25, 1.2
 
 
 def _sb(n, d):
@@ -21,38 +22,159 @@ SCRATCH = {
     "Wq": _sb(512, X4), "Ws": _sb(512, U8), "Wl": _sb(512, X4), "Wm": _sb(512, U8),
     "Sq": _sb(1920, X4), "Ss": _sb(1920, U8), "Lq": _sb(1280, X4), "Ls": _sb(1280, U8),
     "Eq": _sb(512, X4), "Es": _sb(512, U8), "Z": _sb(528, BF), "ones": _sb(448, BF),
-    "Vh": _sb(1024, BF), "Vg": _sb(1024, BF), "G": _sb(1024, BF), "FH": _sb(768, BF),
+    "Vh": _sb(1024, BF), "Vg": _sb(1024, BF), "G": _sb(1024, F32), "FH": _sb(768, BF),
     "Hd": _sb(320, BF), "ys": _sb(256, F32),
-    "pi": _sb(4, I32), "sc": _sb(32, F32), "pos": _sb(48, F32), "pos4": _sb(16, F32), "tmp": _sb(512, F32),
+    "pi": _sb(4, I32), "sc": _sb(40, F32), "pos": _sb(48, F32), "pos4": _sb(16, F32), "tmp": _sb(512, F32),
     "PU": _sb(256, BF), "PV": _sb(256, BF), "PA": _sb(256, BF), "PB": _sb(64, BF), "PC": _sb(256, BF),
     "Tab": _sb(256, BF), "Flg": _sb(448, BF), "c1": _sb(256, BF), "rowa": _sb(16, F32), "lc": _sb(16, F32),
     "ul": _sb(16, U16), "Fl": _sb(4, U16), "Kl": _sb(4, U16), "e0": _sb(2, U16),
     "bits": _sb(512, BF), "su": _sb(512, BF), "sv": _sb(512, BF), "cod": _sb(16, U16), "N1": _sb(256, BF),
     "s1": _sb(192, BF), "W1": _sb(12, U16), "RR": _sb(768, BF), "Rb": _sb(64, BF), "AB": _sb(256, BF),
     "s2": _sb(48, BF), "W2": _sb(6, U16), "QQ": _sb(192, BF), "BB": _sb(64, BF), "Wc": _sb(16, U16),
-    "L3": _sb(560, BF), "s3": _sb(16, BF), "W0": _sb(2, U16), "Pp": _sb(64, BF), "s4": _sb(16, BF), "D1": _sb(4, U16),
-    "s5": _sb(64, BF), "D2": _sb(16, U16), "Pre": _sb(256, BF), "s6": _sb(256, BF),
-    "kd": _sb(48, I32), "ck": _sb(32, F32), "lf": _sb(16, F32), "ll": _sb(16, U16), "Kq": _sb(64, F32), "XX": _sb(256, F32),
-    "ml": _sb(48, U16), "me": _sb(48, U16), "mw": _sb(48, BF), "ML": _sb(192, U16), "MW": _sb(384, BF), "ch": _sb(64, U16),
+    "L3": _sb(480, BF), "s3": _sb(16, BF), "W0": _sb(2, U16), "L4": _sb(416, BF), "MM": _sb(144, BF), "D1": _sb(4, U16),
+    "s5": _sb(64, BF), "D2": _sb(4, U16), "cx": _sb(64, F32), "s6": _sb(256, BF),
+    "kd": _sb(48, I32), "ck": _sb(32, F32), "lf": _sb(16, F32), "ll": _sb(16, U16), "Kq": _sb(64, BF), "XX": _sb(384, BF),
+    "XI": _sb(256, BF), "Tq": _sb(256, X4), "Tp": _sb(256, U8), "gl": _sb(16, U16), "gK": _sb(64, BF), "cw": _sb(64, F32),
+    "ce": _sb(144, U16),
+    "ml": _sb(48, U16), "me": _sb(48, U16), "mw": _sb(48, BF), "ML": _sb(192, U16), "MW": _sb(384, BF), "ch": _sb(96, U16),
     "key": _sb(16, U16), "m": _sb(256, BF), "K1": _sb(256, BF), "le": _sb(192, BF), "ls": _sb(192, BF),
     "junk": _sb(368, BF), "sa": _sb(4, F32), "sl": _sb(4, U16), "sf": _sb(4, F32), "s9": _sb(256, BF),
     "ka": _sb(16, I32), "kb": _sb(16, I32), "kc": _sb(16, I32), "kl": _sb(16, U16),
     "ps": ("psum", [128, 4096], F32),
 }
-SEMAPHORES = ["ev", "es", "et", "eg", "dx0", "dx1", "du", "dv", "dwa", "dwb", "dwc", "oy", "oz", "sent",
-              "fa0", "fa1", "ha0", "ha1", "wa"] + ["map%d_%d" % (t, q) for t in range(R) for q in range(N - 1)]
+SEMAPHORES = ["ev", "es", "et", "eg", "dx0", "dx1", "du", "dv", "dwa", "dwb", "dwc", "oy", "sent",
+              "fa0", "fa1", "ha0", "ha1", "wa", "ta", "gl", "gk", "on0", "on1", "on2", "on3"] + ["map%d_%d" % (t, q) for t in range(R) for q in range(N - 1)]
+
+
+ORDER = {}
+
+
+def order_calls(lists):
+    ops = [(r, k) + o for r, l in enumerate(lists) for k, o in enumerate(l)]
+    base = [sum(len(l) for l in lists[:r]) for r in range(N)]
+    n = len(ops)
+    pre = [{base[o[0]] + j: lat for j, lat in o[9].items()} for o in ops]
+    sender, waits = {}, {}
+    for i, o in enumerate(ops):
+        for to, es, size, sem, doubt in o[11]:
+            for k, p in enumerate(to):
+                sender.setdefault((p, sem), []).append((i, START + (k + 1) * 128 / len(es) * (ROW + size * BYTE) + WAKE + doubt))
+    for i, o in enumerate(ops):
+        for sem in o[10]:
+            for j, lat in sender[o[0], sem]:
+                pre[i][j] = lat
+                waits.setdefault((j, o[0], sem), []).append(i)
+    after, left = [[] for _ in ops], [len(p) for p in pre]
+    for i in range(n):
+        for j in pre[i]:
+            after[j].append(i)
+    rest, todo, undone = [0.0] * n, [i for i in range(n) if not after[i]], [len(a) for a in after]
+    while todo:
+        i = todo.pop()
+        rest[i] = max(rest[i], ops[i][8]) + ops[i][7]
+        for j, lat in pre[i].items():
+            rest[j] = max(rest[j], rest[i] + lat)
+            undone[j] -= 1
+            if not undone[j]:
+                todo.append(j)
+    ready, free, can, best = {}, {}, [0.0] * n, {}
+    for i, o in enumerate(ops):
+        free[o[0], o[2]] = 0.0
+        ready.setdefault((o[0], o[2]), [])
+        if not left[i]:
+            ready[o[0], o[2]].append(i)
+    engine, order = [[0.0] * 16 for _ in range(N)], {r: [] for r in range(N)}
+
+    def choose(e):
+        l = ready[e]
+        go = {i: max(free[e], can[i]) for i in l}
+        worst = max(go[i] + rest[i] for i in l)
+        for i in sorted(l, key=lambda i: (go[i], -rest[i], i)):
+            if all(go[i] + ops[i][7] + rest[j] <= worst + SLACK for j in l if rest[j] > rest[i] and go[j] < go[i] + ops[i][7]):
+                return go[i], i
+    for _ in range(n):
+        for e, l in ready.items():
+            if l and e not in best:
+                best[e] = choose(e)
+        e = min(best, key=best.get)
+        s, i = best.pop(e)
+        ready[e].remove(i)
+        free[e] = end = s + ops[i][7]
+        order[e[0]].append(ops[i][1])
+        for to, es, size, sem, doubt in ops[i][11]:
+            for p in to:
+                for x in es:
+                    engine[e[0]][x] = max(engine[e[0]][x], end + START) + 128 / len(es) * (ROW + size * BYTE)
+                for k in waits.get((i, p, sem), []):
+                    can[k] = max(can[k], max(engine[e[0]][x] for x in es) + WAKE + doubt)
+        for k in after[i]:
+            can[k] = max(can[k], end + pre[k][i])
+            left[k] -= 1
+            if not left[k]:
+                ready[ops[k][0], ops[k][2]].append(k)
+                best.pop((ops[k][0], ops[k][2]), None)
+    return order
+
+
+def host(T, topo, q, t):
+    w = (q + HOP[t]) % N
+    for p in ((w - LENT) % N, w):
+        if t != WHOLE and topo.chip(T.cores[p]) == topo.chip(T.cores[q]):
+            return p
+    return w
+
+
+def early(T, topo, q):
+    return host(T, topo, (q - HOP[0]) % N, 0) != q
+
+
+def relay(T, topo, q):
+    c = T.cores[q]
+    free = [x for x in topo.cores_of(c) if x not in T.cores and all(topo.may_write(x, y) for y in T.cores)]
+    free.sort(key=lambda x: topo.die(x) == topo.die(c))
+    return free[[x for x in T.cores if topo.chip(x) == topo.chip(c)].index(c)]
+
+
+def hand_on(g, core, to, helper, T, topo, pieces):
+    rid, pid, _ = topo.addr(to)
+    n = 0
+    for k, (src, dst) in enumerate(((T.Ws[:], T.Wm[:]), (T.Wq[:, 0:256].bitcast(dt.uint8), T.Wl[:, 0:256].bitcast(dt.uint8)),
+                                    (T.Wq[:, 256:512].bitcast(dt.uint8), T.Wl[:, 256:512].bitcast(dt.uint8)))[:pieces]):
+        g.wait_ge(T.sem["on%d" % k], len(topo.engines(topo.cores_of(core)[0], topo.cores_of(core)[1])))
+        g.remote_dma_fused([RemoteDMATransfer(dst_ids=[DstId(rid=rid, pnc=pid)], dma_engine_mask=topo.mask(core, to),
+                                              remote_sem=T.sem.wa, src=src, dsts=[dst])], local_sem=T.sem.sent)
+        n += len(topo.engines(core, to))
+    rid, pid, _ = topo.addr(helper)
+    half = T.Tq[:, 0:128].bitcast(dt.uint8)
+    g.wait_ge(T.sem.on3, len(topo.engines(topo.cores_of(core)[0], topo.cores_of(core)[1])) - len(topo.engines(core, helper)))
+    g.remote_dma_fused([RemoteDMATransfer(dst_ids=[DstId(rid=rid, pnc=pid)], dma_engine_mask=topo.mask(core, helper),
+                                          remote_sem=T.sem.ta, src=half, dsts=[half])], local_sem=T.sem.sent)
+    g.wait_ge(T.sem.sent, n + len(topo.engines(core, helper)))
 
 
 def rank_program(g, core, T, topo):
     r = T.rank_of(core)
     if r is None:
+        for q in range(N):
+            if relay(T, topo, q) == core:
+                hand_on(g, core, T.cores[(q - LENT) % N], T.cores[host(T, topo, q, WHOLE)], T, topo, 1 if early(T, topo, q) else 3)
         return
+    if not ORDER:
+        ORDER.update(order_calls([listing(g, T, topo, q)[0] for q in range(N)]))
+    ops, emit, total = listing(g, T, topo, r)
+    for i in ORDER[r]:
+        emit(i)
+    for sem, n in total.items():
+        g.wait_ge(T.sem[sem], n)
+
+
+def listing(g, T, topo, r):
     AL, AF = AluOpType, ActivationFunctionType
     cores = T.cores
     queue = {"v": g.vector, "s": g.scalar, "t": g.tensor, "g": g, "y": g.sync}
     own = {"v": "ev", "s": "es", "t": "et", "g": "eg"}
     total, seen, clock = {}, {}, {e: {} for e in queue}
-    ops, touched, landing, anchor, chain, others = [], {}, [], {}, {}, {}
+    ops, touched, landing, chain, hold = [], {}, [], {}, []
 
     def V(name, lo, hi, step=1):
         m = (1 << hi) - (1 << lo) if step == 1 else sum(1 << c for c in range(lo, hi, step))
@@ -99,12 +221,12 @@ def rank_program(g, core, T, topo):
         for name, m in reads:
             seen.setdefault(name, []).append((m, False, sem, val, snap, e))
 
-    def issue(e, make, outs, ins, sem=None, cost=None, f=1.0, late=0.0, line=None):
+    def issue(e, make, outs, ins, sem=None, cost=None, f=1.0, late=0.0, line=None, sends=()):
         ins = [a for a in ins if isinstance(a, tuple)]
         reads, writes = [x for a in ins for x in a[1]], [x for a in outs for x in a[1]]
         if cost is None:
             n = max(a[2] for a in outs + ins[:1])
-            cost = 0.05 + 0.0013 * n if any(a[3] for a in ins) else max(64, n * f) * 0.00083
+            cost = (0.065 if e == "s" else 0.05) + 0.0013 * n if any(a[3] for a in ins) else max(64, n * f) * 0.00083
         me, pre = len(ops), {}
         for regs, wr in ((reads, False), (writes, True)):
             for name, m in regs:
@@ -112,15 +234,14 @@ def rank_program(g, core, T, topo):
                     if am & m and (aw or wr or name.startswith("ps")):
                         near_ps = name.startswith("ps") and ops[j][0] == e
                         pre[j] = max(pre.get(j, 0.0), 0.0 if near_ps else WAIT + ops[j][6])
-        for name, m in reads:
-            for ln, lm, key, lat in landing:
-                if ln == name and lm & m and key in anchor:
-                    pre[anchor[key]] = max(pre.get(anchor[key], 0), lat)
+        needs = {ls for name, m in reads for ln, lm, ls in landing if ln == name and lm & m}
+        for j in hold:
+            pre.setdefault(j, 0.0)
         if line:
             if line in chain:
                 pre.setdefault(chain[line], 0.0)
             chain[line] = me
-        ops.append((e, make, reads, writes, sem, cost, late, pre))
+        ops.append((e, make, reads, writes, sem, cost, late, pre, needs, sends))
         for name, m in writes:
             touched[name] = [a for a in touched.get(name, []) if a[0] & ~m] + [(m, True, me)]
         for name, m in reads:
@@ -138,44 +259,6 @@ def rank_program(g, core, T, topo):
         make().then_inc(T.sem[sem], inc)
         note(e, reads, writes, sem, total[sem])
 
-    def run():
-        n = len(ops)
-        rest, after, left = [0.0] * n, [[] for _ in ops], [len(o[7]) for o in ops]
-        for i in range(n - 1, -1, -1):
-            rest[i] += ops[i][5]
-            if i in others:
-                rest[others[i]] = max(rest[others[i]], rest[i] + FLIGHT + 1.0)
-            for j, lat in ops[i][7].items():
-                after[j].append(i)
-                rest[j] = max(rest[j], rest[i] + lat)
-        free, end, can = {e: 0.0 for e in queue}, [0.0] * n, [0.0] * n
-        ready = {e: [i for i in range(n) if ops[i][0] == e and not left[i]] for e in queue}
-        for _ in range(n):
-            pick = None
-            for e, l in ready.items():
-                if not l:
-                    continue
-                go = {i: max(free[e], can[i]) for i in l}
-                worst = max(go[i] + rest[i] for i in l)
-
-                def harm(i):
-                    done = go[i] + ops[i][5]
-                    return max([done + rest[j] for j in l if j != i and go[j] < done] + [worst]) - worst
-                i = min(l, key=lambda i: (max(harm(i) - SLACK, 0.0), go[i] if go[i] > free[e] + SLACK else 0.0, -rest[i], i))
-                s = go[i]
-                if pick is None or s < pick[0]:
-                    pick = (s, i)
-            s, i = pick
-            e = ops[i][0]
-            ready[e].remove(i)
-            free[e] = end[i] = s + ops[i][5]
-            emit(i)
-            for k in after[i]:
-                can[k] = max(can[k], end[i] + ops[k][7][i])
-                left[k] -= 1
-                if not left[k]:
-                    ready[ops[k][0]].append(k)
-
     def ap(a):
         return a[0] if isinstance(a, tuple) else a
 
@@ -184,8 +267,8 @@ def rank_program(g, core, T, topo):
             return issue("v", lambda: g.vector.tensor_scalar(out[0], in0[0], ap(s1), None, op0), [out], [in0, s1], f=f)
         return issue("v", lambda: g.vector.tensor_scalar(out[0], in0[0], ap(s1), ap(s2), op0, op1), [out], [in0, s1, s2], f=f)
 
-    def tt(out, a, b, op, line=None):
-        issue("v", lambda: g.vector.tensor_tensor(out[0], a[0], b[0], op), [out], [a, b], f=2.0, line=line)
+    def tt(out, a, b, op, line=None, f=2.0):
+        issue("v", lambda: g.vector.tensor_tensor(out[0], a[0], b[0], op), [out], [a, b], f=f, line=line)
 
     def cp(out, a, e="v", scale=None, line=None):
         if e == "v" and scale is None:
@@ -198,7 +281,8 @@ def rank_program(g, core, T, topo):
             issue("s", lambda: g.scalar.activation(out[0], a[0], AF.Copy, scale=scale), [out], [a], line=line)
 
     def affine(out, a, scale, bias, func=AF.Identity):
-        issue("s", lambda: g.scalar.activation(out[0], a[0], func, bias=ap(bias), scale=scale), [out], [a, bias])
+        func = AF.Copy if isinstance(bias, float) else func
+        issue("s", lambda: g.scalar.activation(out[0], a[0], func, bias=ap(bias), scale=ap(scale)), [out], [a, bias, scale])
 
     def fill(out, x):
         issue("v", lambda: g.vector.memset(out[0], x), [out], [], f=0.5)
@@ -212,9 +296,9 @@ def rank_program(g, core, T, topo):
     def pickup(out, pat, row):
         scan(out, pat, row, AL.add, AL.min)
 
-    def quant(q, s, lo, n, tile):
+    def quant(q, s, lo, n, tile, line=None):
         a, b = V(q, lo, lo + n), V(s, lo, lo + n)
-        issue("v", lambda: g.vector.quantize_mx(a[0], b[0], tile[0]), [a, b], [tile], cost=0.012 + 0.00088 * n)
+        issue("v", lambda: g.vector.quantize_mx(a[0], b[0], tile[0]), [a, b], [tile], cost=0.012 + 0.00088 * n, line=line)
 
     def mm(k, n, wq, ws, wlo, xq, xs, xlo):
         o, a, b = bank(k, n), V(wq, wlo, wlo + 128), V(ws, wlo, wlo + 128)
@@ -257,68 +341,94 @@ def rank_program(g, core, T, topo):
         rid, pid, _ = topo.addr(c)
         return DstId(rid=rid, pnc=pid)
 
-    def push(parts, key):
+    def push(parts, size, doubt=0.0):
         def make():
             g.remote_dma_fused([RemoteDMATransfer(dst_ids=[dst_id(cores[q]) for q in to],
                                                   dma_engine_mask=sum(1 << e for e in es),
                                                   remote_sem=T.sem[sem], src=src[0], dsts=[land[0] for q in to])
                                 for src, to, land, es, sem in parts], local_sem=T.sem.sent)
-        anchor[key] = issue("g", make, [], [p[0] for p in parts], "sent", cost=0.4, line="g")
+        issue("g", make, [], [p[0] for p in parts], "sent", cost=CALL if "sent" in total else FIRST, line="g",
+              sends=[(to, es, size, sem, doubt) for src, to, land, es, sem in parts])
         total["sent"] = total.get("sent", 0) + sum(len(p[3]) for p in parts)
 
-    def ahead(p):
-        return (p + 2) // 2
+    def ahead(p, t):
+        return min(p, max(2, p // 2 + t))
 
-    def form(q, p):
-        return ("me" if ahead(p) > 1 else "ml") if q == 0 else "mw" if q < ahead(p) else "ml"
+    def maker(p, t):
+        return (p - HOP[t]) % N if t == WHOLE else p
 
-    def map_plan(q):
+    def form(q, c, t):
+        return ("me" if ahead(c, t) > 1 or t == WHOLE else "ml") if q == 0 else "mw" if q < ahead(c, t) else "ml"
+
+    def map_plan(q, t):
         far = far_engines(q)
-        later = list(range(N - 1, q, -1))
-        sets = [(f, [p for p in later if not near(p, q) and form(q, p) == f]) for f in ("me", "mw", "ml")]
-        sets = [x for x in sets if x[1]]
-        n = len(far) // max(len(sets), 1)
-        plan = [(f, to, far[n * k:n * k + n]) for k, (f, to) in enumerate(sets)]
-        return plan + [(form(q, p), [p], [e for e in lanes(q, p) if e not in far]) for p in later if near(p, q)]
 
-    def slot(f, t, q):
-        return V("MW", 128 * t + 16 * q, 128 * t + 16 * q + 4) if f == "mw" else V("ML", 64 * t + 8 * q, 64 * t + 8 * q + 4)
+        def turn(p):
+            c, a = maker(p, t), ahead(maker(p, t), t)
+            return c - 2 * (a - q if q < a else q - a + 2)
+        first = sorted((p for p in range(N) if p != q and q < maker(p, t)), key=turn)
+        sets = {}
+        for p in first:
+            sets.setdefault((near(p, q), form(q, maker(p, t), t)), []).append(p)
+        for p in range(q + 1, N):
+            if p not in first:
+                room = sorted((len(to), f) for (here, f), to in sets.items() if not here)
+                sets.setdefault((near(p, q), room[0][1] if room else ("mw" if q else "me")), []).append(p)
+        out = [(f, to) for (here, f), to in sets.items() if not here]
+        n = len(far) // max(len(out), 1)
+        return [(f, to, far[n * k:n * k + n]) for k, (f, to) in enumerate(out)] + \
+               [(f, to, [e for e in lanes(q, to[0]) if e not in far]) for (here, f), to in sets.items() if here]
+
+    def slot(f, t, q, mine=False, n=4):
+        if mine:
+            return V(f, 16 * t, 16 * t + n)
+        return V("MW", 128 * t + 16 * q, 128 * t + 16 * q + n) if f == "mw" else V("ML", 64 * t + 8 * q, 64 * t + 8 * q + n)
 
     def holder(q, t):
-        w = (q + HOP[t]) % N
-        for p in ((w - LENT) % N, w):
-            if p == q or near(p, q):
-                return p
-        return w
+        return host(T, topo, q, t)
 
-    def arrives(sem, n, views, key, lat):
+    def arrives(sem, n, views):
         total[sem] = n
         note(None, [], [x for a in views for x in a[1]], sem, n)
-        landing.extend((name, m, key, lat) for a in views for name, m in a[1])
+        landing.extend((name, m, sem) for a in views for name, m in a[1])
 
     def send_tile(base, to, k, side, sem):
         x, es, d = 640 * k + 192 + 192 * side, lanes(r, to), 192 * (1 - side)
+        if not near(r, to):
+            push([(u8(V("Sq", base, base + 64)), [to], u8(V("Lq", x, x + 64)), es, sem)], 256)
+            push([(V("Ss", base, base + 64), [to], V("Ls", x, x + 64), es, sem)], 64)
+            return
         push([(u8(V("Sq", base, base + 64)), [to], u8(V("Lq", x, x + 64)), es[:len(es) // 2], sem),
-              (V("Ss", base - d, base - d + 256), [to], V("Ls", x - d, x - d + 256), es[len(es) // 2:], sem)], sem)
+              (V("Ss", base - d, base - d + 256), [to], V("Ls", x - d, x - d + 256), es[len(es) // 2:], sem)], 256)
 
     def landed(sem, k, side, frm):
         x, d = 640 * k + 192 + 192 * side, 192 * (1 - side)
-        arrives(sem, len(lanes(frm, r)), [V("Lq", x, x + 64), V("Ls", x - d, x - d + 256)], sem, FLIGHT)
+        arrives(sem, len(lanes(frm, r)) * (1 if near(frm, r) else 2), [V("Lq", x, x + 64), V("Ls", x - d, x - d + 256)])
 
+    came = {}
     for t in range(R):
-        for q in range(r):
-            f, n = [(f, len(es)) for f, to, es in map_plan(q) if r in to][0]
-            arrives("map%d_%d" % (t, q), n, [slot(f, t, q)], "map%d" % t, FLIGHT)
+        for q in range(N - 1):
+            for f, to, es in map_plan(q, t):
+                if r in to:
+                    came[t, q] = f
+                    arrives("map%d_%d" % (t, q), len(es), [slot(f, t, q)])
     away = [t for t in range(R) if holder(r, t) != r]
     guest = {t: [q for q in range(N) if holder(q, t) == r][0] for t in range(R)}
     for k, t in enumerate(away):
-        landed("fa%d" % k, k, 0, guest[t])
+        if t != WHOLE:
+            landed("fa%d" % k, k, 0, guest[t])
         landed("ha%d" % k, k, 1, holder(r, t))
     wto, far = (r - LENT) % N, far_engines(r)
+    if WHOLE in guest:
+        n = len(lanes(guest[WHOLE], r))
+        arrives("ta", 3 * n, [V("Tq", 0, 256), V("Tp", 0, 256)])
+        arrives("gl", n, [V("gl", 0, 16)])
+        arrives("gk", n, [V("gK", 0, 64)])
 
-    def early(q):
-        return holder((q - HOP[0]) % N, 0) != q
-    arrives("wa", (3 if early((r + LENT) % N) else 2) * len(far_engines((r + LENT) % N)), [V("Wl", 0, 512), V("Wm", 0, 512)], "none", 0.0)
+    def tell(src, land, t, sem, size, doubt=0.0):
+        push([(src, [holder(r, t)], land, lanes(r, holder(r, t)), sem)], size, doubt)
+
+    arrives("wa", 3 * len(topo.engines(relay(T, topo, (r + LENT) % N), cores[r])), [V("Wl", 0, 512), V("Wm", 0, 512)])
 
     dma("s", V("ut", 0, 512), T.u[:], "du", 1.5)
     dma("y", V("Tt", 0, 512), T.x[:, 0:512], "dx0", 1.8)
@@ -328,8 +438,9 @@ def rank_program(g, core, T, topo):
     dma("y", u8(V("Wq", 256, 512)), T.wc[:, 1024:2048], "dwc", 3.5)
     dma("y", V("vt", 0, 512), T.v[:], "dv", 4.0)
 
-    cI, cLO, cHI, cS4, cAA, cAC, cMU, cAU, cMV, cAV, cM3, cTI, cIL = range(13)
-    cSW, cU0, cU1, cV0, cV1, cH1, cD1, cD2, cK, cK1, cK2, cK3, cT0, cT1, cT2, cT3 = range(13, 29)
+    cI, cLO, cHI, cS4, cAA, cMU, cAU, cMV, cAV, cM3, cTI, cIL = range(12)
+    cSW, cU0, cU1, cV0, cV1, cH1, cD1, cD2, cK, cK1, cK2, cK3, cT0, cT1, cE = range(12, 27)
+    cM = cE + 4
     iota(V("pi", 0, 1), [[0, 1]], 0, 1, True)
     iota(V("rowa", 0, 16), [[1, 2], [16, 8]])
     iota(V("pos", 0, 48), [[1, 48]], -8)
@@ -338,47 +449,52 @@ def rank_program(g, core, T, topo):
     iota(V("c1", 0, 256), [[16, 16], [0, 4], [1, 4]], 1)
     iota(V("c1", 3, 256, 4), [[16, 4], [1, 4], [0, 4]], 1)
     iota(V("pos4", 0, 16), [[0, 4], [1, 4]])
-    iota(V("AB", 0, 64), [[64, 4], [4, 4], [16, 4]])
+    iota(V("AB", 0, 256, 4), [[64, 4], [4, 4], [16, 4]])
     fill(V("ones", 0, 448), 1.0)
     fill(V("ones", 320, 321), 0.0)
     fill(col(cTI), -TINY)
     fill(V("Z", 0, 528), 0.0)
     issue("g", lambda: g.affine_select(T.Z[:, 3:515:4], T.ones[:, 0:128], [[1, 128]], AL.is_equal, 0.0, 0, -1),
-          [V("Z", 3, 515, 4)], [V("ones", 0, 128)], cost=0.39)
-    push([(V("Ws", 0, 512), [wto], V("Wm", 0, 512), far, "wa")], "w0")
+          [V("Z", 3, 515, 4)], [V("ones", 0, 128)], cost=0.39, line="g")
 
-    def lend(lo, hi):
-        push([(u8(V("Wq", lo, hi)), [wto], u8(V("Wl", lo, hi)), far, "wa")], "w%d" % hi)
-    if early(r):
-        lend(0, 256)
+    def lend(k):
+        src = u8(V("Wq", 256 * k - 256, 256 * k)) if k else V("Ws", 0, 512)
+        x = relay(T, topo, r)
+        es = topo.engines(cores[r], x)
+        issue("g", lambda: g.remote_dma_fused([RemoteDMATransfer(dst_ids=[dst_id(x)], dma_engine_mask=topo.mask(cores[r], x),
+                                                                 remote_sem=T.sem["on%d" % k], src=src[0], dsts=[src[0]])],
+                                              local_sem=T.sem.sent),
+              [], [src], "sent", cost=CALL if k else FIRST, line="g", sends=[([wto], es, 1024 if k else 512, "wa", 3 * DOUBT)])
+        total["sent"] = total.get("sent", 0) + len(es)
+
+    def direct(k):
+        push([(u8(V("Wq", 256 * k - 256, 256 * k)), [wto], u8(V("Wl", 256 * k - 256, 256 * k)), far, "wa")], 1024)
+    lend(0)
+    if early(T, topo, r):
+        direct(1)
     cp(V("ul", 0, 16), V("rowa", 0, 16))
     ts(V("pi", 1, 2), V("pi", 0, 1), 15, AL.bitwise_and)
     ts(V("pi", 2, 3), V("pi", 0, 1), 3, AL.bitwise_and)
     ts(V("pi", 3, 4), V("pi", 0, 1), 2, AL.arith_shift_right, 3, AL.bitwise_and)
     cp(V("sc", 0, 3), V("pi", 1, 4))
     ts(col(cSW), col(cLO), 4.0, AL.mult, col(cHI), AL.add)
-    ts(col(cU1), col(cLO), 8.0, AL.mult, 8.0, AL.add)
-    ts(col(cU0), col(cSW), 2.0, AL.mult)
-    ts(col(cV0), col(cHI), 8.0, AL.mult)
-    ts(col(cV1), col(cI), 2.0, AL.mult, 2.0, AL.add)
-    ts(col(cH1), col(cHI), 1.0, AL.add)
-    ts(col(cAA), col(cI), 15.0, AL.is_lt, 256.0, AL.mult)
-    ts(col(cAC), col(cHI), 3.0, AL.is_lt, 256.0, AL.mult)
-    ts(col(cT0), col(cLO), 3.0, AL.is_equal, 1.0 / BIG, AL.max)
-    ts(col(cT1), col(cI), 15.0, AL.is_equal, 1.0 / BIG, AL.max)
-    ts(col(cM3), col(cHI), 0.0, AL.is_equal, 4.0, AL.mult)
-    cp(col(cMU), col(cT0), "s", 0.5)
-    cp(col(cMV), col(cT1), "s", 0.5)
-    cp(col(cS4), col(cSW), "s", 4.0)
-    affine(col(cD2), col(cLO), 64.0, col(cAC))
-    affine(col(cT2), col(cLO), 1.0, col(cAC))
-    ts(col(cD1), col(cT2), 12.0, AL.add)
-    ts(col(cT3), col(cLO), col(cHI), AL.subtract, 3.0, AL.mult)
-    ts(col(cK), col(cT3), col(cAC), AL.subtract, 12.0, AL.add)
-    ts(col(cIL), col(cI), -208.0, AL.add)
-    ts(col(cK1), col(cI), 16.0, AL.add)
-    ts(col(cK2), col(cI), 32.5, AL.add)
-    ts(col(cK3), col(cI), 48.5, AL.add)
+    ts(V("sc", cE, cE + 4), V("pos", 8, 12), col(cHI), AL.is_equal)
+    ts(col(cMU), col(cLO), 3.0, AL.is_equal, 0.5, AL.mult)
+    ts(col(cMV), col(cI), 15.0, AL.is_equal, 0.5, AL.mult)
+    for out, a, scale, bias in (
+            (cU1, cLO, 8.0, 8.0), (cU0, cSW, 2.0, 0.0), (cAA, cMV, -512.0, 256.0), (cD2, cMV, -512.0, 256.75),
+            (cMU, cMU, 1.0, 0.5 / BIG), (cMV, cMV, 1.0, 0.5 / BIG), (cV0, cHI, 8.0, 0.0), (cV1, cI, 2.0, 2.0),
+            (cH1, cHI, 1.0, 1.0), (cM3, cE, 4.0, 0.0), (cS4, cSW, 4.0, 0.0), (cIL, cI, 1.0, -208.0),
+            (cT0, cE + 3, 92.0, -128.0), (cT0, cHI, 16.0, cT0), (cD1, cLO, 1.0, cT0),
+            (cT1, cE + 3, 256.0, -256.0), (cT1, cHI, -3.0, cT1), (cK, cLO, 3.0, cT1),
+            (cK1, cI, 1.0, 16.0), (cK2, cI, 1.0, 32.5), (cK3, cI, 1.0, 48.5),
+            (cM, cE, 0.25, 0.0), (cM + 1, cE, -127.0, 255.0), (cM + 2, cE + 1, 0.25, 0.0), (cM + 3, cE + 1, -127.0, 255.0),
+            (cM + 4, cE + 2, 4.0, 0.0), (cM + 5, cE + 3, -192.0, 192.0), (cM + 5, cE + 2, -64.0, cM + 5)):
+        affine(col(out), col(a), scale, bias if isinstance(bias, float) else col(bias))
+    iota(V("XI", 0, 64), [[16, 4], [0, 16]])
+    for k in range(3):
+        row = V("XI", 0, 64) if k < 2 else V("pos4", 0, 16)
+        affine(V("MM", 64 * k, 64 * k + row[2]), row, col(cM + 2 * k), col(cM + 2 * k + 1))
 
     def horner(name, start, stop, o, mu, au):
         p, a, b, c = V("pos", 8, 40), V("tmp", o, o + 32), V("tmp", o + 32, o + 64), V("tmp", o + 64, o + 96)
@@ -420,26 +536,17 @@ def rank_program(g, core, T, topo):
     ts(V("Kl", 0, 4), V("pos", 8, 12), 4.0, AL.mult, col(cLO), AL.add)
     affine(V("lc", 0, 16), V("pos", 8, 24), 16.0, col(cI))
     cp(V("BB", 0, 64, 4), V("pos", 8, 24), "s", 4.0)
-    fill(V("Pp", 0, 64), 0.0)
-    cp(V("Pp", 0, 16, 4), V("pos", 5, 9), "s", 4.0)
     for b in range(4):
         quant("Eq", "Es", 128 * b, 128, V("Z", 3 - b, 515 - b))
-    for k in range(3):
-        sfill("RR", 256 * k, 256 * k + 256, 1, 0)
-    sfill("QQ", 0, 192, 1, 0)
-    sfill("L3", 0, 280, 1, 0)
-    sfill("L3", 280, 560, 1, 0)
-    fill(V("FH", 0, 512), 0.0)
+    for name, lo, hi in (("RR", 0, 384), ("RR", 384, 768), ("QQ", 0, 192), ("L3", 0, 240), ("L3", 240, 480), ("L4", 0, 272),
+                         ("FH", 0, 256), ("FH", 256, 512), ("Flg", 0, 192), ("Flg", 256, 448)):
+        fill(V(name, lo, hi), 0.0)
     fill(V("Hd", 0, 320, 80), 0.0)
-    if r == 0:
-        cp(V("e0", 0, 1), col(cI))
+    cp(V("e0", 0, 1), col(cI))
     for k in range(len(away)):
         quant("Lq", "Ls", 640 * k + 256, 128, V("FH", 0, 512))
     quant("vq", "vs", 0, 128, V("vt", 0, 512))
-    sfill("Flg", 0, 192, 1, 0)
-    sfill("Flg", 192, 256, 1, 1)
-    sfill("Flg", 256, 448, 1, 0)
-    for args in ((256, 320, 4), (320, 385, 16), (400, 416, 4), (416, 432, 1)):
+    for args in ((192, 256, 1), (256, 320, 4), (320, 385, 16), (400, 416, 4), (416, 432, 1)):
         sfill("Flg", *args, 1)
     for k in range(4):
         sfill("Flg", 324 + k, 400, 16, 1)
@@ -448,66 +555,64 @@ def rank_program(g, core, T, topo):
         o, s, k, bias = V("junk", at, at + hi - lo), V("sa", c, c + 1), V("K1", lo, hi), col(cK3 if c == 3 else cK2)
         issue("s", lambda: g.scalar.activation(o[0], k[0], AF.Sign, bias=bias[0], scale=-1.0, accum_out=s[0]), [o, s], [k, bias])
 
-    def update(lo, hi):
+    def starts(keys, at):
+        me = ts(V("key", 0, 16), ind(keys, at), -16.0, AL.mult, 192.0, AL.add)
+        for h in range(2):
+            cp(V("m", 128 * h, 128 * h + 128), ind(V("Flg", 0, 448), V("key", 8 * h, 8 * h + 8)), "vs"[h])
+        scan(V("K1", 0, 256), V("ones", 0, 256), V("m", 0, 256), AL.mult, AL.add)
+        return me
+
+    def firsts(out):
+        count(3, 48, 256, 0)
+        count(2, 32, 192, 208)
+        ts(V("le", 64, 192), V("K1", 0, 128), col(cK1), AL.is_le, f=0.5)
+        ts(V("le", 0, 64), V("K1", 0, 64), col(cI), AL.is_le)
+        scan(V("ls", 0, 192), V("ones", 256, 448), V("le", 0, 192), AL.mult, AL.add)
+        ts(V(out, 3, 4), V("sa", 3, 4), 0.5, AL.mult, 152.0, AL.add)
+        cp(V(out, 0, 2), V("ls", 63, 192, 128))
+        ts(V(out, 2, 3), V("sa", 2, 3), 0.5, AL.mult, 112.0, AL.add)
+
+    def send_map(t, soon):
+        plan = [(f, [p for p in to if (r < maker(p, t)) == soon], es) for f, to, es in map_plan(r, t)]
+        parts = [(V(f, 16 * t, 16 * t + 4), to, slot(f, t, r), es, "map%d_%d" % (t, r)) for f, to, es in plan if to]
+        if parts:
+            push(parts, 8, 0.0 if soon else DOUBT)
+
+    def unpack(q, s, lo):
         for b in range(4):
+            mm(2 + b, 256, "Eq", "Es", 128 * b, q, s, lo)
+            for x in (0, 128):
+                cp(V("Vh", 256 * b + x, 256 * b + x + 128), bank(2 + b, 128, x), "s", 1.0, "V")
+
+    def update(lo, hi, bs):
+        for b in bs:
             w = V("Tt", 64 * lo + b, 64 * hi, 4)
             tt(w, ind(V("Hd", 80 * b, 80 * b + 65), V("kl", lo, hi)), w, AL.add, "T")
 
     for t in range(R):
         qh, qt, qf = 512 * t, 512 * t + 128, 512 * t + 384
         for h in range(2):
-            quant("Sq", "Ss", qt + 128 * h, 128, V("Tt", 512 * h, 512 * h + 512))
+            if t and h:
+                update(8, 16, [3])
+            quant("Sq", "Ss", qt + 128 * h, 128, V("Tt", 512 * h, 512 * h + 512), "T")
             for b in (1, 0):
                 mm(6 * h + b, 128, "Uq", "Us", 128 * b, "Sq", "Ss", qt + 128 * h)
                 affine(V("bits", 256 * h + 1 - b, 256 * h + 256, 2), bank(6 * h + b, 128), 1.0, col(cTI), AF.Sign)
             scan(V("su", 256 * h, 256 * h + 256), V("PU", 0, 256), V("bits", 256 * h, 256 * h + 256), AL.mult, AL.add)
             ts(V("cod", 8 * h, 8 * h + 8), V("su", 256 * h + 31, 256 * h + 256, 32), col(cMU), AL.mult, col(cAU), AL.add)
             tt(V("N1", 128 * h, 128 * h + 128), ind(V("Tab", 0, 256), V("cod", 8 * h, 8 * h + 8)), V("c1", 128 * h, 128 * h + 128), AL.add)
-        for b in range(4):
-            mm(2 + b, 256, "Eq", "Es", 128 * b, "Sq", "Ss", qt)
-            cp(V("Vh", 256 * b, 256 * b + 256), bank(2 + b, 256), "s", 0.5, "V")
-            cp(V("Vg", 256 * b, 256 * b + 256), bank(2 + b, 256), "s", 0.5, "V")
-        for u in (2, 1, 0):
-            pickup(V("s1", 64 * u, 64 * u + 64), V("PA" if u else "PB", 0, 64), V("N1", u, 256, 4))
-        ts(V("W1", 8, 12), V("s1", 143, 192, 16), col(cAA), AL.add)
-        ts(V("W1", 0, 8), V("s1", 15, 128, 16), col(cAA), AL.add)
-        cp(V("RR", 2, 256, 4), ind(V("N1", 0, 256), V("W1", 8, 12)))
-        cp(V("RR", 257, 512, 4), ind(V("RR", 0, 256), V("W1", 4, 8)))
-        cp(V("Rb", 0, 64), ind(V("RR", 256, 512), V("W1", 0, 4)))
-        cp(V("RR", 513, 768, 4), ind(V("N1", 0, 256), V("W1", 4, 8)), "s")
-        cp(V("AB", 64, 128), ind(V("N1", 0, 256), V("Fl", 0, 4)), "s")
-        cp(V("AB", 128, 192), ind(V("N1", 0, 256), V("W1", 0, 4)), "s")
-        cp(V("AB", 192, 256), ind(V("RR", 512, 768), V("W1", 0, 4)), "s")
-        for v in (2, 1, 0):
-            pickup(V("s2", 16 * v, 16 * v + 16), V("PA", 0, 16), V("Rb", v, 64, 4))
-        ts(V("W2", 4, 5), V("s2", 47, 48), col(cAA), AL.add)
-        ts(V("W2", 0, 4, 2), V("s2", 15, 32, 16), col(cAA), AL.add)
-        cp(V("QQ", 2, 64, 4), ind(V("Rb", 0, 64), V("W2", 4, 5)))
-        cp(V("QQ", 65, 128, 4), ind(V("QQ", 0, 64), V("W2", 2, 3)))
-        ts(V("Wc", 0, 16), ind(V("QQ", 64, 128), V("W2", 0, 1)), 4.0, AL.mult)
-        cp(V("L3", 0, 256, 16), ind(V("QQ", 64, 128), V("W2", 0, 1)), "s")
-        cp(V("QQ", 129, 192, 4), ind(V("Rb", 0, 64), V("W2", 2, 3)), "s")
-        cp(V("BB", 1, 64, 4), V("Rb", 0, 64, 4), "s")
-        cp(V("BB", 2, 64, 4), ind(V("Rb", 0, 64), V("W2", 0, 1)), "s")
-        cp(V("BB", 3, 64, 4), ind(V("QQ", 128, 192), V("W2", 0, 1)), "s")
-        cp(V("L3", 336, 400), ind(V("L3", 48, 256), V("Wc", 8, 12)))
-        cp(V("L3", 496, 560), ind(V("L3", 48, 256), V("Wc", 4, 8)), "s")
-        pickup(V("s3", 0, 16), V("PA", 0, 16), V("L3", 0, 256, 16))
-        cp(V("L3", 416, 480), ind(V("L3", 256, 400), V("Wc", 4, 8)))
-        anchor["map%d" % t] = ts(V("W0", 0, 1), V("s3", 15, 16), col(cAA), AL.add, col(cM3), AL.mult)
-        last = ind(V("L3", 400, 480), V("W0", 0, 1))
-        for f in sorted({f for f, to, es in map_plan(r)}):
-            o = V(f, 16 * t, 16 * t + 16)
-            if f == "ml":
-                ts(o, last, 4.0, AL.mult, col(cIL), AL.add)
-            elif f == "me":
-                ts(o, last, 0.25, AL.mult, -13.0, AL.add)
-            else:
-                cp(o, last, "s")
-        if r < N - 1:
-            push([(V(f, 16 * t, 16 * t + 4), to, slot(f, t, r), es, "map%d_%d" % (t, r)) for f, to, es in map_plan(r)], "map%d" % t)
-        if t == 0 and early(r):
-            lend(256, 512)
+        if t == WHOLE:
+            x, a, b = relay(T, topo, r), u8(V("Sq", qt, qt + 128)), u8(V("Sq", qt + 128, qt + 256))
+            rest = [e for e in topo.engines(cores[r], x) if e not in far]
+            issue("g", lambda x=x, a=a, b=b, rest=rest, to=holder(r, t): g.remote_dma_fused([
+                RemoteDMATransfer(dst_ids=[dst_id(c)], dma_engine_mask=sum(1 << e for e in es), remote_sem=T.sem[sem], src=src[0],
+                                  dsts=[u8(V("Tq", lo, lo + 128))[0]])
+                for c, es, sem, src, lo in ((x, rest, "on3", a, 0), (cores[to], far, "ta", b, 128))], local_sem=T.sem.sent),
+                [], [a, b], "sent", cost=CALL, line="g",
+                sends=[([holder(r, t)], rest, 512, "ta", 2 * DOUBT), ([holder(r, t)], far, 512, "ta", 0.0)])
+            total["sent"] += len(rest) + len(far)
+            tell(V("Ss", qt, qt + 256), V("Tp", 0, 256), t, "ta", 256, DOUBT)
+        unpack(*(("Tq", "Tp", 0) if t == WHOLE else ("Sq", "Ss", qt)))
         for h in range(2):
             scan(V("sv", 256 * h, 256 * h + 256), V("PV", 0, 256), V("bits", 256 * h, 256 * h + 256), AL.mult, AL.add)
         ts(V("kd", 0, 16), V("sv", 31, 512, 32), col(cMV), AL.mult, col(cAV), AL.add)
@@ -517,57 +622,122 @@ def rank_program(g, core, T, topo):
         ts(V("ll", 0, 16), V("lf", 0, 16), 255.0, AL.min)
         ts(V("ck", 16, 32), V("kd", 32, 48), 1.0 / 64, AL.mult, col(cK), AL.add)
         tt(V("ck", 0, 16), V("ck", 16, 32), V("lc", 0, 16), AL.add)
-        pickup(V("s5", 0, 64), V("PC", 0, 64), V("BB", 0, 64))
-        ts(V("D2", 0, 16), V("s5", 3, 64, 4), col(cD2), AL.add)
-        cp(V("Pre", 0, 256), ind(V("AB", 0, 256), V("D2", 0, 16)), "s")
-        pickup(V("s6", 0, 256), V("PC", 0, 256), V("Pre", 0, 256))
-        tt(V("Kq", 0, 64), ind(V("ck", 0, 16), V("Kl", 0, 4)), V("s6", 3, 256, 4), AL.subtract)
-        cp(V("Pp", 1, 16, 4), V("L3", 0, 64, 16), "s")
-        cp(V("Pp", 2, 64, 4), ind(V("L3", 48, 256), V("W0", 0, 1)), "s")
-        cp(V("Pp", 3, 64, 4), ind(V("L3", 480, 560), V("W0", 0, 1)), "s")
-        pickup(V("s4", 0, 16), V("PC", 0, 16), V("Pp", 0, 16))
-        ts(V("D1", 0, 4), V("s4", 3, 16, 4), col(cD1), AL.add)
+        if t == WHOLE:
+            tell(V("ll", 0, 16), V("gl", 0, 16), t, "gl", 32)
+        for u in (2, 1, 0):
+            pickup(V("s1", 64 * u, 64 * u + 64), V("PA" if u else "PB", 0, 64), V("N1", u, 256, 4))
+        ts(V("W1", 8, 12), V("s1", 143, 192, 16), col(cAA), AL.add)
+        ts(V("W1", 0, 8), V("s1", 15, 128, 16), col(cAA), AL.add)
+        cp(V("RR", 2, 256, 4), ind(V("N1", 0, 256), V("W1", 8, 12)))
+        cp(V("RR", 257, 512, 4), ind(V("RR", 0, 256), V("W1", 4, 8)))
+        cp(V("Rb", 0, 64), ind(V("RR", 256, 512), V("W1", 0, 4)))
+        cp(V("RR", 513, 768, 4), ind(V("N1", 0, 256), V("W1", 4, 8)), "s")
+        cp(V("AB", 1, 256, 4), ind(V("N1", 0, 256), V("Fl", 0, 4)), "s")
+        cp(V("AB", 2, 256, 4), ind(V("N1", 0, 256), V("W1", 0, 4)), "s")
+        cp(V("AB", 3, 256, 4), ind(V("RR", 512, 768), V("W1", 0, 4)), "s")
+        for v in (2, 1, 0):
+            pickup(V("s2", 16 * v, 16 * v + 16), V("PA", 0, 16), V("Rb", v, 64, 4))
+        ts(V("W2", 4, 5), V("s2", 47, 48), col(cAA), AL.add)
+        ts(V("W2", 0, 4, 2), V("s2", 15, 32, 16), col(cAA), AL.add)
+        cp(V("QQ", 2, 64, 4), ind(V("Rb", 0, 64), V("W2", 4, 5)))
+        cp(V("QQ", 65, 128, 4), ind(V("QQ", 0, 64), V("W2", 2, 3)))
+        ts(V("Wc", 0, 16), ind(V("QQ", 64, 128), V("W2", 0, 1)), 4.0, AL.mult)
+        if r < N - 1:
+            cp(V("L3", 0, 256, 16), ind(V("QQ", 64, 128), V("W2", 0, 1)), "s")
+        cp(V("QQ", 129, 192, 4), ind(V("Rb", 0, 64), V("W2", 2, 3)), "s")
+        cp(V("BB", 1, 64, 4), V("Rb", 0, 64, 4), "s")
+        cp(V("BB", 2, 64, 4), ind(V("Rb", 0, 64), V("W2", 0, 1)), "s")
+        cp(V("BB", 3, 64, 4), ind(V("QQ", 128, 192), V("W2", 0, 1)), "s")
+        if r < N - 1:
+            cp(V("L3", 336, 400), ind(V("L3", 48, 256), V("Wc", 8, 12)))
+            pickup(V("s3", 0, 16), V("PA", 0, 16), V("L3", 0, 256, 16))
+            cp(V("L3", 416, 480), ind(V("L3", 256, 400), V("Wc", 4, 8)))
+            ts(V("W0", 0, 1), V("s3", 15, 16), col(cAA), AL.add, col(cM3), AL.mult)
+        last = ind(V("L3", 400, 480), V("W0", 0, 1))
+        c = maker(r, t)
+        for f in sorted({f for f, to, es in map_plan(r, t)} | ({form(r, c, t)} if r < c else set())):
+            o = V(f, 16 * t, 16 * t + 16)
+            if f == "ml":
+                ts(o, last, 4.0, AL.mult, col(cIL), AL.add)
+            elif f == "me":
+                ts(o, last, 0.25, AL.mult, -13.0, AL.add)
+            else:
+                cp(o, last, "s")
+        send_map(t, True)
+        if t == 0 and early(T, topo, r):
+            direct(2)
+        elif t == 0:
+            lend(1)
+            lend(2)
+        pickup(V("s6", 0, 256), V("PC", 0, 256), V("AB", 0, 256))
+        cp(V("cx", 0, 64), ind(V("ck", 0, 16), V("Kl", 0, 4)), "s")
+        pickup(V("s5", 0, 64), V("PA", 0, 64), V("BB", 0, 64))
+        ts(V("D2", 0, 4), V("s5", 15, 64, 16), col(cD2), AL.add, 4.0, AL.mult)
+        tt(V("Kq", 0, 64), ind(V("s6", 0, 256), V("D2", 0, 4)), V("cx", 0, 64), AL.subtract)
+        tt(V("L4", 0, 256, 16), ind(V("QQ", 64, 128), V("W2", 0, 1)), V("MM", 128, 144), AL.max)
+        tt(V("L4", 272, 336), ind(V("L4", 48, 256), V("Wc", 4, 8)), V("MM", 64, 128), AL.min)
+        tt(V("L4", 352, 416), ind(V("L4", 256, 336), V("Wc", 0, 4)), V("MM", 0, 64), AL.min)
+        ts(V("D1", 0, 4), V("L4", 352, 416, 16), col(cD1), AL.add)
         cp(V("XX", 0, 64), ind(V("Kq", 0, 64), V("D1", 0, 4)))
+        if t == WHOLE:
+            tell(V("XX", 0, 64), V("gK", 0, 64), t, "gk", 128)
+            send_map(t, False)
         for b in range(4):
             for h in range(2):
                 lo = 256 * b + 128 * h
-                tt(V("G", lo, lo + 128), ind(V("Vh", 256 * b, 256 * b + 256), V("ll", 8 * h, 8 * h + 8)), V("Vg", lo, lo + 128), AL.add, "G")
-        x = 0
-        for q in range(r - 1, ahead(r) - 1, -1):
-            cp(V("XX", x + 64, x + 128), ind(V("XX", x, x + 64), slot("ml", t, q)), "s")
+                cp(V("Vg", lo, lo + 128), ind(V("Vh", 256 * b, 256 * b + 256), V("gl" if t == WHOLE else "ll", 8 * h, 8 * h + 8)), "s", 1.0, "L")
+                tt(V("G", lo, lo + 128), bank(2 + b, 128, 128 * h), V("Vg", lo, lo + 128), AL.add, "G", 1.0)
+        x, xx = 0, "XI" if t == WHOLE else "XX"
+        for q in range(c - 1, ahead(c, t) - 1, -1):
+            cp(V(xx, x + 64, x + 128), ind(V(xx, x, x + 64), slot("ml", t, q, q == r)), "s")
             x += 64
-        at = V("ML", 64 * t, 64 * t + 1) if r else V("e0", 0, 1)
-        for q in range(1, min(ahead(r), r)):
-            src, o = ind(slot("mw", t, q), at), V("ch", 16 * q, 16 * q + 16)
-            if q < ahead(r) - 1:
+        at = slot(form(0, c, t), t, 0, r == 0, 1) if c else V("e0", 0, 1)
+        for q in range(1, min(ahead(c, t), c)):
+            src, o = ind(slot("mw", t, q, q == r), at), V("ch", 16 * q, 16 * q + 16)
+            if q < ahead(c, t) - 1:
                 ts(o, src, 0.25, AL.mult, -13.0, AL.add)
             else:
                 ts(o, src, 4.0, AL.mult, col(cIL), AL.add)
             at = V("ch", 16 * q, 16 * q + 1)
-        others[ts(V("key", 0, 16), ind(V("XX", x, x + 64), at), 16.0, AL.mult)] = anchor["map%d" % t]
-        for h in range(2):
-            cp(V("m", 128 * h, 128 * h + 128), ind(V("Flg", 0, 448), V("key", 8 * h, 8 * h + 8)), "vs"[h])
-        scan(V("K1", 0, 256), V("ones", 0, 256), V("m", 0, 256), AL.mult, AL.add)
-        count(3, 48, 256, 0)
-        count(2, 32, 192, 208)
-        ts(V("le", 64, 192), V("K1", 0, 128), col(cK1), AL.is_le, f=0.5)
-        ts(V("le", 0, 64), V("K1", 0, 64), col(cI), AL.is_le)
-        scan(V("ls", 0, 192), V("ones", 256, 448), V("le", 0, 192), AL.mult, AL.add)
-        ts(V("sl", 3, 4), V("sa", 3, 4), 0.5, AL.mult, 152.0, AL.add)
-        cp(V("sl", 0, 2), V("ls", 63, 192, 128))
-        ts(V("sl", 2, 3), V("sa", 2, 3), 0.5, AL.mult, 112.0, AL.add)
+        keys = V("XX", x, x + 64)
+        if t == WHOLE:
+            keys = V("gK", 0, 64)
+            if c == 1:
+                ts(V("ch", 0, 1), at, 16.0, AL.mult, col(cI), AL.add)
+            elif x:
+                ts(V("ch", 0, 16), ind(V("XI", x, x + 64), at), col(cI), AL.add)
+            at = V("ch", 0, 1) if c == 1 or x else at
+        keyed = starts(keys, at)
+        firsts("sl")
         for b in range(4):
-            cp(V("FH", b, 256, 4), ind(V("G", 256 * b, 256 * b + 256), V("sl", 0, 4)), "vs"[b % 2])
+            cp(V("FH", b, 256, 4), ind(V("G", 256 * b, 256 * b + 256), V("sl", 0, 4)), "vs"[b % 2], 0.5)
+        made = len(ops) - 1
         quant("Sq", "Ss", qf, 128, V("FH", 0, 512))
         k = away.index(t) if t in away else None
-        if k is not None:
+        if k is not None and t != WHOLE:
             send_tile(qf, holder(r, t), k, 0, "fa%d" % k)
         wq, ws = ("Wq", "Ws") if (guest[t] + HOP[t]) % N == r else ("Wl", "Wm")
         for b in range(4):
-            if k is None:
+            if k is None or t == WHOLE:
                 mm(2 + b, 128, wq, ws, 128 * b, "Sq", "Ss", qf)
             else:
                 mm(2 + b, 128, wq, ws, 128 * b, "Lq", "Ls", 640 * k + 192)
+        if t == WHOLE:
+            at = V("ML", 64 * t, 64 * t + 1)
+            hold.append(keyed)
+            for q in range(1, r):
+                o = V("ce", 16 * q, 16 * q + 16)
+                if came[t, q] == "mw":
+                    ts(o, ind(slot("mw", t, q), at), 0.25, AL.mult, -13.0, AL.add)
+                else:
+                    cp(V("cw", 8 * q, 8 * q + 4), slot("ml", t, q))
+                    ts(o, ind(V("cw", 8 * q, 8 * q + 4), at), col(cI), AL.subtract, 1.0 / 16, AL.mult)
+                at = V("ce", 16 * q, 16 * q + 1)
+            if r:
+                ts(V("ce", 0, 1), at, 16.0, AL.mult, col(cI), AL.add)
+            hold.append(made)
+            starts(V("XX", 0, 64), V("ce" if r else "e0", 0, 1))
+            hold.clear()
         pickup(V("s9", 0, 256), V("PA", 0, 256), V("K1", 0, 256))
         ts(V("ka", 0, 16), V("s9", 15, 256, 16), col(cAA), AL.add, -1.0, AL.add)
         ts(V("kb", 0, 16), V("ka", 0, 16), 63, AL.bitwise_and)
@@ -576,10 +746,12 @@ def rank_program(g, core, T, topo):
         for b in range(4):
             cp(V("FH", 512 + b, 768, 4), bank(2 + b, 64), "sv"[b % 2], 0.03125)
         quant("Sq", "Ss", qh, 128, V("FH", 256, 768))
+        if t == WHOLE:
+            hold.append(len(ops) - 1)
+            firsts("sf")
+            hold.clear()
         if k is not None:
             send_tile(qh + 64, guest[t], k, 1, "ha%d" % k)
-        if t == 0 and not early(r):
-            lend(0, 512)
         banks = (0, 1, 6, 7)
         for b in range(4):
             if k is None:
@@ -588,23 +760,28 @@ def rank_program(g, core, T, topo):
                 mm(banks[b], 128, "Eq", "Es", 128 * b, "Lq", "Ls", 640 * k + 320)
             cp(V("Hd", 80 * b + 1, 80 * b + 65), bank(banks[b], 64, 64), "s" if b else "v")
         if t == R - 1:
-            cp(V("sf", 0, 4), V("sl", 0, 4))
-            for c in range(4):
-                dma("y", T.ol[:, 16 * c:16 * c + 16], V("sf", c, c + 1), "oy", behind=[V("Hd", 1, 2)])
-        update(0, 8)
-        update(8, 16)
+            if t != WHOLE:
+                cp(V("sf", 0, 4), V("sl", 0, 4))
+            for j in range(4):
+                dma("y", T.ol[:, 16 * j:16 * j + 16], V("sf", j, j + 1), "oy", behind=[V("Hd", 1, 2)])
+        else:
+            update(0, 16, [0, 1])
+            update(0, 8, [2, 3])
+            update(8, 16, [2])
     qt = 512 * R + 128
+    update(0, 8, range(4))
+    update(8, 16, [0])
     for h in range(2):
         lo = qt + 128 * h
-        quant("Sq", "Ss", lo, 128, V("Tt", 512 * h, 512 * h + 512))
+        if h:
+            update(8, 16, [1, 2, 3])
+        quant("Sq", "Ss", lo, 128, V("Tt", 512 * h, 512 * h + 512), "T")
         mm(2 + h, 128, "vq", "vs", 0, "Sq", "Ss", lo)
         dma("y", T.oc[:, 512 * h:512 * h + 512], u8(V("Sq", lo, lo + 128)), "oy")
         cp(V("ys", 128 * h, 128 * h + 128), bank(2 + h, 128), "s")
         if h:
             for k in range(4):
                 src = (T.Ss[32 * k:32 * k + 4, qt:qt + 256], V("Ss", qt, qt + 256)[1], 256, 0)
-                dma("s", T.osc[4 * k:4 * k + 4, :], src, "oz")
+                dma("y", T.osc[4 * k:4 * k + 4, :], src, "oy")
         dma("y", T.y[:, 128 * h:128 * h + 128], V("ys", 128 * h, 128 * h + 128), "oy")
-    run()
-    for sem, n in total.items():
-        g.wait_ge(T.sem[sem], n)
+    return ops, emit, total

from concourse.bass import DstId, RemoteDMATransfer
from concourse.mybir import dt, AluOpType, AxisListType, ActivationFunctionType

N, C, A, R = 8, 256, 64, 3
HOP = [1, 2, 3]
LENT = HOP[1]
WHOLE = 2
X4, U8, BF, F32, I32, U16 = "float8_e4m3fn_x4", "uint8", "bfloat16", "float32", "int32", "uint16"
BIG = float(2 ** 40)
TINY = 1e-35
WAIT, LOAD, SLACK, CALL, FIRST, START, ROW, BYTE, WAKE, DOUBT = 0.17, 1.5, 0.05, 0.3, 2.0, 0.8, 0.015, 7e-5, 0.25, 1.2


def _sb(n, d):
    return ("sbuf", [128, n], d)


SCRATCH = {
    "Tt": _sb(1024, BF), "ut": _sb(512, BF), "vt": _sb(512, BF),
    "uq": _sb(128, X4), "us": _sb(128, U8), "Uq": _sb(256, X4), "Us": _sb(256, U8),
    "vq": _sb(128, X4), "vs": _sb(128, U8),
    "Wq": _sb(512, X4), "Ws": _sb(512, U8), "Wl": _sb(512, X4), "Wm": _sb(512, U8),
    "Sq": _sb(1920, X4), "Ss": _sb(1920, U8), "Lq": _sb(1280, X4), "Ls": _sb(1280, U8),
    "Eq": _sb(512, X4), "Es": _sb(512, U8), "Z": _sb(528, BF), "ones": _sb(448, BF),
    "Vh": _sb(1024, BF), "Vg": _sb(1024, BF), "G": _sb(1024, F32), "FH": _sb(768, BF),
    "Hd": _sb(320, BF), "ys": _sb(256, F32),
    "pi": _sb(4, I32), "sc": _sb(40, F32), "pos": _sb(48, F32), "pos4": _sb(16, F32), "tmp": _sb(512, F32),
    "PU": _sb(256, BF), "PV": _sb(256, BF), "PA": _sb(256, BF), "PB": _sb(64, BF), "PC": _sb(256, BF),
    "Tab": _sb(256, BF), "Flg": _sb(448, BF), "c1": _sb(256, BF), "rowa": _sb(16, F32), "lc": _sb(16, F32),
    "ul": _sb(16, U16), "Fl": _sb(4, U16), "Kl": _sb(4, U16), "e0": _sb(2, U16),
    "bits": _sb(512, BF), "su": _sb(512, BF), "sv": _sb(512, BF), "cod": _sb(16, U16), "N1": _sb(256, BF),
    "s1": _sb(192, BF), "W1": _sb(12, U16), "RR": _sb(768, BF), "Rb": _sb(64, BF), "AB": _sb(256, BF),
    "s2": _sb(48, BF), "W2": _sb(6, U16), "QQ": _sb(192, BF), "BB": _sb(64, BF), "Wc": _sb(16, U16),
    "L3": _sb(480, BF), "s3": _sb(16, BF), "W0": _sb(2, U16), "L4": _sb(416, BF), "MM": _sb(144, BF), "D1": _sb(4, U16),
    "s5": _sb(64, BF), "D2": _sb(4, U16), "cx": _sb(64, F32), "s6": _sb(256, BF),
    "kd": _sb(48, I32), "ck": _sb(32, F32), "lf": _sb(16, F32), "ll": _sb(16, U16), "Kq": _sb(64, BF), "XX": _sb(384, BF),
    "XI": _sb(256, BF), "Tq": _sb(256, X4), "Tp": _sb(256, U8), "gl": _sb(16, U16), "gK": _sb(64, BF), "cw": _sb(64, F32),
    "ce": _sb(144, U16),
    "ml": _sb(48, U16), "me": _sb(48, U16), "mw": _sb(48, BF), "ML": _sb(192, U16), "MW": _sb(384, BF), "ch": _sb(96, U16),
    "key": _sb(16, U16), "m": _sb(256, BF), "K1": _sb(256, BF), "le": _sb(192, BF), "ls": _sb(192, BF),
    "junk": _sb(368, BF), "sa": _sb(4, F32), "sl": _sb(4, U16), "sf": _sb(4, F32), "s9": _sb(256, BF),
    "ka": _sb(16, I32), "kb": _sb(16, I32), "kc": _sb(16, I32), "kl": _sb(16, U16),
    "ps": ("psum", [128, 4096], F32),
}
SEMAPHORES = ["ev", "es", "et", "eg", "dx0", "dx1", "du", "dv", "dwa", "dwb", "dwc", "oy", "sent",
              "fa0", "fa1", "ha0", "ha1", "wa", "ta", "gl", "gk", "on0", "on1", "on2", "on3"] + ["map%d_%d" % (t, q) for t in range(R) for q in range(N - 1)]


ORDER = {}


def order_calls(lists):
    ops = [(r, k) + o for r, l in enumerate(lists) for k, o in enumerate(l)]
    base = [sum(len(l) for l in lists[:r]) for r in range(N)]
    n = len(ops)
    pre = [{base[o[0]] + j: lat for j, lat in o[9].items()} for o in ops]
    sender, waits = {}, {}
    for i, o in enumerate(ops):
        for to, es, size, sem, doubt in o[11]:
            for k, p in enumerate(to):
                sender.setdefault((p, sem), []).append((i, START + (k + 1) * 128 / len(es) * (ROW + size * BYTE) + WAKE + doubt))
    for i, o in enumerate(ops):
        for sem in o[10]:
            for j, lat in sender[o[0], sem]:
                pre[i][j] = lat
                waits.setdefault((j, o[0], sem), []).append(i)
    after, left = [[] for _ in ops], [len(p) for p in pre]
    for i in range(n):
        for j in pre[i]:
            after[j].append(i)
    rest, todo, undone = [0.0] * n, [i for i in range(n) if not after[i]], [len(a) for a in after]
    while todo:
        i = todo.pop()
        rest[i] = max(rest[i], ops[i][8]) + ops[i][7]
        for j, lat in pre[i].items():
            rest[j] = max(rest[j], rest[i] + lat)
            undone[j] -= 1
            if not undone[j]:
                todo.append(j)
    ready, free, can, best = {}, {}, [0.0] * n, {}
    for i, o in enumerate(ops):
        free[o[0], o[2]] = 0.0
        ready.setdefault((o[0], o[2]), [])
        if not left[i]:
            ready[o[0], o[2]].append(i)
    engine, order = [[0.0] * 16 for _ in range(N)], {r: [] for r in range(N)}

    def choose(e):
        l = ready[e]
        go = {i: max(free[e], can[i]) for i in l}
        worst = max(go[i] + rest[i] for i in l)
        for i in sorted(l, key=lambda i: (go[i], -rest[i], i)):
            if all(go[i] + ops[i][7] + rest[j] <= worst + SLACK for j in l if rest[j] > rest[i] and go[j] < go[i] + ops[i][7]):
                return go[i], i
    for _ in range(n):
        for e, l in ready.items():
            if l and e not in best:
                best[e] = choose(e)
        e = min(best, key=best.get)
        s, i = best.pop(e)
        ready[e].remove(i)
        free[e] = end = s + ops[i][7]
        order[e[0]].append(ops[i][1])
        for to, es, size, sem, doubt in ops[i][11]:
            for p in to:
                for x in es:
                    engine[e[0]][x] = max(engine[e[0]][x], end + START) + 128 / len(es) * (ROW + size * BYTE)
                for k in waits.get((i, p, sem), []):
                    can[k] = max(can[k], max(engine[e[0]][x] for x in es) + WAKE + doubt)
        for k in after[i]:
            can[k] = max(can[k], end + pre[k][i])
            left[k] -= 1
            if not left[k]:
                ready[ops[k][0], ops[k][2]].append(k)
                best.pop((ops[k][0], ops[k][2]), None)
    return order


def host(T, topo, q, t):
    w = (q + HOP[t]) % N
    for p in ((w - LENT) % N, w):
        if t != WHOLE and topo.chip(T.cores[p]) == topo.chip(T.cores[q]):
            return p
    return w


def early(T, topo, q):
    return host(T, topo, (q - HOP[0]) % N, 0) != q


def relay(T, topo, q):
    c = T.cores[q]
    free = [x for x in topo.cores_of(c) if x not in T.cores and all(topo.may_write(x, y) for y in T.cores)]
    free.sort(key=lambda x: topo.die(x) == topo.die(c))
    return free[[x for x in T.cores if topo.chip(x) == topo.chip(c)].index(c)]


def hand_on(g, core, to, helper, T, topo, pieces):
    rid, pid, _ = topo.addr(to)
    n = 0
    for k, (src, dst) in enumerate(((T.Ws[:], T.Wm[:]), (T.Wq[:, 0:256].bitcast(dt.uint8), T.Wl[:, 0:256].bitcast(dt.uint8)),
                                    (T.Wq[:, 256:512].bitcast(dt.uint8), T.Wl[:, 256:512].bitcast(dt.uint8)))[:pieces]):
        g.wait_ge(T.sem["on%d" % k], len(topo.engines(topo.cores_of(core)[0], topo.cores_of(core)[1])))
        g.remote_dma_fused([RemoteDMATransfer(dst_ids=[DstId(rid=rid, pnc=pid)], dma_engine_mask=topo.mask(core, to),
                                              remote_sem=T.sem.wa, src=src, dsts=[dst])], local_sem=T.sem.sent)
        n += len(topo.engines(core, to))
    rid, pid, _ = topo.addr(helper)
    half = T.Tq[:, 0:128].bitcast(dt.uint8)
    g.wait_ge(T.sem.on3, len(topo.engines(topo.cores_of(core)[0], topo.cores_of(core)[1])) - len(topo.engines(core, helper)))
    g.remote_dma_fused([RemoteDMATransfer(dst_ids=[DstId(rid=rid, pnc=pid)], dma_engine_mask=topo.mask(core, helper),
                                          remote_sem=T.sem.ta, src=half, dsts=[half])], local_sem=T.sem.sent)
    g.wait_ge(T.sem.sent, n + len(topo.engines(core, helper)))


def rank_program(g, core, T, topo):
    r = T.rank_of(core)
    if r is None:
        for q in range(N):
            if relay(T, topo, q) == core:
                hand_on(g, core, T.cores[(q - LENT) % N], T.cores[host(T, topo, q, WHOLE)], T, topo, 1 if early(T, topo, q) else 3)
        return
    if not ORDER:
        ORDER.update(order_calls([listing(g, T, topo, q)[0] for q in range(N)]))
    ops, emit, total = listing(g, T, topo, r)
    for i in ORDER[r]:
        emit(i)
    for sem, n in total.items():
        g.wait_ge(T.sem[sem], n)


def listing(g, T, topo, r):
    AL, AF = AluOpType, ActivationFunctionType
    cores = T.cores
    queue = {"v": g.vector, "s": g.scalar, "t": g.tensor, "g": g, "y": g.sync}
    own = {"v": "ev", "s": "es", "t": "et", "g": "eg"}
    total, seen, clock = {}, {}, {e: {} for e in queue}
    ops, touched, landing, chain, hold = [], {}, [], {}, []

    def V(name, lo, hi, step=1):
        m = (1 << hi) - (1 << lo) if step == 1 else sum(1 << c for c in range(lo, hi, step))
        ap = T[name][:, lo:hi] if step == 1 else T[name][:, lo:hi:step]
        return (ap, [(name, m)], len(range(lo, hi, step)), 0)

    def bank(k, n, lo=0):
        return (T.ps[:, 512 * k + lo:512 * k + lo + n], [("ps%d" % k, 1)], n, 0)

    def ind(win, off):
        return (win[0].indirect(off[0]), win[1] + off[1], 16 * off[2], 1)

    def col(k):
        return V("sc", k, k + 1)

    def wait_for(e, reads, writes):
        need = {}
        for regs, wr in ((reads, False), (writes, True)):
            for name, m in regs:
                for am, aw, sem, val, snap, ae in seen.get(name, []):
                    if not am & m:
                        continue
                    if name.startswith("ps"):
                        if ae == e:
                            continue
                    elif not (aw or wr):
                        continue
                    if val > need.get(sem, (0, None))[0]:
                        need[sem] = (val, snap)
        for sem in list(need):
            if any(o != sem and need[o][1].get(sem, 0) >= need[sem][0] for o in need):
                del need[sem]
        for sem, (val, snap) in need.items():
            if clock[e].get(sem, 0) < val:
                queue[e].wait_ge(T.sem[sem], val)
            for k, x in snap.items():
                clock[e][k] = max(clock[e].get(k, 0), x)

    def note(e, reads, writes, sem, val):
        snap = dict(clock[e]) if e else {}
        snap[sem] = val
        for name, m in writes:
            seen[name] = [a for a in seen.get(name, []) if a[0] & ~m] + [(m, True, sem, val, snap, e)]
        for name, m in reads:
            seen.setdefault(name, []).append((m, False, sem, val, snap, e))

    def issue(e, make, outs, ins, sem=None, cost=None, f=1.0, late=0.0, line=None, sends=()):
        ins = [a for a in ins if isinstance(a, tuple)]
        reads, writes = [x for a in ins for x in a[1]], [x for a in outs for x in a[1]]
        if cost is None:
            n = max(a[2] for a in outs + ins[:1])
            cost = (0.065 if e == "s" else 0.05) + 0.0013 * n if any(a[3] for a in ins) else max(64, n * f) * 0.00083
        me, pre = len(ops), {}
        for regs, wr in ((reads, False), (writes, True)):
            for name, m in regs:
                for am, aw, j in touched.get(name, []):
                    if am & m and (aw or wr or name.startswith("ps")):
                        near_ps = name.startswith("ps") and ops[j][0] == e
                        pre[j] = max(pre.get(j, 0.0), 0.0 if near_ps else WAIT + ops[j][6])
        needs = {ls for name, m in reads for ln, lm, ls in landing if ln == name and lm & m}
        for j in hold:
            pre.setdefault(j, 0.0)
        if line:
            if line in chain:
                pre.setdefault(chain[line], 0.0)
            chain[line] = me
        ops.append((e, make, reads, writes, sem, cost, late, pre, needs, sends))
        for name, m in writes:
            touched[name] = [a for a in touched.get(name, []) if a[0] & ~m] + [(m, True, me)]
        for name, m in reads:
            touched.setdefault(name, []).append((m, False, me))
        return me

    def emit(i):
        e, make, reads, writes, sem = ops[i][:5]
        wait_for(e, reads, writes)
        if sem == "sent":
            return make()
        inc = 16 if sem else 1
        sem = sem or own[e]
        total[sem] = total.get(sem, 0) + inc
        make().then_inc(T.sem[sem], inc)
        note(e, reads, writes, sem, total[sem])

    def ap(a):
        return a[0] if isinstance(a, tuple) else a

    def ts(out, in0, s1, op0, s2=None, op1=None, f=1.0):
        if op1 is None:
            return issue("v", lambda: g.vector.tensor_scalar(out[0], in0[0], ap(s1), None, op0), [out], [in0, s1], f=f)
        return issue("v", lambda: g.vector.tensor_scalar(out[0], in0[0], ap(s1), ap(s2), op0, op1), [out], [in0, s1, s2], f=f)

    def tt(out, a, b, op, line=None, f=2.0):
        issue("v", lambda: g.vector.tensor_tensor(out[0], a[0], b[0], op), [out], [a, b], f=f, line=line)

    def cp(out, a, e="v", scale=None, line=None):
        if e == "v" and scale is None:
            return issue("v", lambda: g.vector.tensor_copy(out[0], a[0]), [out], [a])
        elif e == "v":
            ts(out, a, scale, AL.mult)
        elif scale is None:
            issue("s", lambda: g.scalar.activation(out[0], a[0], AF.Copy), [out], [a])
        else:
            issue("s", lambda: g.scalar.activation(out[0], a[0], AF.Copy, scale=scale), [out], [a], line=line)

    def affine(out, a, scale, bias, func=AF.Identity):
        func = AF.Copy if isinstance(bias, float) else func
        issue("s", lambda: g.scalar.activation(out[0], a[0], func, bias=ap(bias), scale=ap(scale)), [out], [a, bias, scale])

    def fill(out, x):
        issue("v", lambda: g.vector.memset(out[0], x), [out], [], f=0.5)

    def sfill(name, lo, hi, step, x):
        cp(V(name, lo, hi, step), V("ones", 0, len(range(lo, hi, step))), "s", float(x))

    def scan(out, d0, d1, op0, op1):
        issue("v", lambda: g.vector.tensor_tensor_scan(out[0], d0[0], d1[0], 0.0, op0, op1), [out], [d0, d1], f=0.5)

    def pickup(out, pat, row):
        scan(out, pat, row, AL.add, AL.min)

    def quant(q, s, lo, n, tile, line=None):
        a, b = V(q, lo, lo + n), V(s, lo, lo + n)
        issue("v", lambda: g.vector.quantize_mx(a[0], b[0], tile[0]), [a, b], [tile], cost=0.012 + 0.00088 * n, line=line)

    def mm(k, n, wq, ws, wlo, xq, xs, xlo):
        o, a, b = bank(k, n), V(wq, wlo, wlo + 128), V(ws, wlo, wlo + 128)
        c, d = V(xq, xlo, xlo + n), V(xs, xlo, xlo + n)
        issue("t", lambda: g.tensor.matmul_mx(o[0], a[0], b[0], c[0], d[0], True, True), [o], [a, b, c, d], cost=0.0009 * (n + 16))

    def iota(out, pattern, base=0, cm=0, whole=False):
        cost = 0.13 + 0.0017 * out[2]
        if whole:
            issue("g", lambda: g.iota(out[0], pattern, base, cm), [out], [], cost=cost)
        else:
            issue("g", lambda: g.iota(out[0], pattern, base, cm, allow_small_or_imprecise_dtypes=True), [out], [], cost=cost)

    def dma(e, out, in_, sem, late=LOAD, behind=()):
        issue(e, lambda: queue[e].dma_start(ap(out), ap(in_)), [out] if isinstance(out, tuple) else [], [in_] + list(behind), sem,
              cost=0.1, late=late, line=e)

    def u8(a):
        return (a[0].bitcast(dt.uint8), a[1], a[2], 0)

    def double(name, n, upto, e="s"):
        while n < upto:
            cp(V(name, n, 2 * n), V(name, 0, n), e)
            n *= 2

    def near(a, b):
        return topo.chip(cores[a]) == topo.chip(cores[b])

    def far_engines(a):
        es = None
        for b in range(N):
            if b != a:
                es = [e for e in topo.engines(cores[a], cores[b]) if es is None or e in es]
        return es

    def lanes(a, b):
        return topo.engines(cores[a], cores[b])

    def dst_id(c):
        rid, pid, _ = topo.addr(c)
        return DstId(rid=rid, pnc=pid)

    def push(parts, size, doubt=0.0):
        def make():
            g.remote_dma_fused([RemoteDMATransfer(dst_ids=[dst_id(cores[q]) for q in to],
                                                  dma_engine_mask=sum(1 << e for e in es),
                                                  remote_sem=T.sem[sem], src=src[0], dsts=[land[0] for q in to])
                                for src, to, land, es, sem in parts], local_sem=T.sem.sent)
        issue("g", make, [], [p[0] for p in parts], "sent", cost=CALL if "sent" in total else FIRST, line="g",
              sends=[(to, es, size, sem, doubt) for src, to, land, es, sem in parts])
        total["sent"] = total.get("sent", 0) + sum(len(p[3]) for p in parts)

    def ahead(p, t):
        return min(p, max(2, p // 2 + t))

    def maker(p, t):
        return (p - HOP[t]) % N if t == WHOLE else p

    def form(q, c, t):
        return ("me" if ahead(c, t) > 1 or t == WHOLE else "ml") if q == 0 else "mw" if q < ahead(c, t) else "ml"

    def map_plan(q, t):
        far = far_engines(q)

        def turn(p):
            c, a = maker(p, t), ahead(maker(p, t), t)
            return c - 2 * (a - q if q < a else q - a + 2)
        first = sorted((p for p in range(N) if p != q and q < maker(p, t)), key=turn)
        sets = {}
        for p in first:
            sets.setdefault((near(p, q), form(q, maker(p, t), t)), []).append(p)
        for p in range(q + 1, N):
            if p not in first:
                room = sorted((len(to), f) for (here, f), to in sets.items() if not here)
                sets.setdefault((near(p, q), room[0][1] if room else ("mw" if q else "me")), []).append(p)
        out = [(f, to) for (here, f), to in sets.items() if not here]
        n = len(far) // max(len(out), 1)
        return [(f, to, far[n * k:n * k + n]) for k, (f, to) in enumerate(out)] + \
               [(f, to, [e for e in lanes(q, to[0]) if e not in far]) for (here, f), to in sets.items() if here]

    def slot(f, t, q, mine=False, n=4):
        if mine:
            return V(f, 16 * t, 16 * t + n)
        return V("MW", 128 * t + 16 * q, 128 * t + 16 * q + n) if f == "mw" else V("ML", 64 * t + 8 * q, 64 * t + 8 * q + n)

    def holder(q, t):
        return host(T, topo, q, t)

    def arrives(sem, n, views):
        total[sem] = n
        note(None, [], [x for a in views for x in a[1]], sem, n)
        landing.extend((name, m, sem) for a in views for name, m in a[1])

    def send_tile(base, to, k, side, sem):
        x, es, d = 640 * k + 192 + 192 * side, lanes(r, to), 192 * (1 - side)
        if not near(r, to):
            push([(u8(V("Sq", base, base + 64)), [to], u8(V("Lq", x, x + 64)), es, sem)], 256)
            push([(V("Ss", base, base + 64), [to], V("Ls", x, x + 64), es, sem)], 64)
            return
        push([(u8(V("Sq", base, base + 64)), [to], u8(V("Lq", x, x + 64)), es[:len(es) // 2], sem),
              (V("Ss", base - d, base - d + 256), [to], V("Ls", x - d, x - d + 256), es[len(es) // 2:], sem)], 256)

    def landed(sem, k, side, frm):
        x, d = 640 * k + 192 + 192 * side, 192 * (1 - side)
        arrives(sem, len(lanes(frm, r)) * (1 if near(frm, r) else 2), [V("Lq", x, x + 64), V("Ls", x - d, x - d + 256)])

    came = {}
    for t in range(R):
        for q in range(N - 1):
            for f, to, es in map_plan(q, t):
                if r in to:
                    came[t, q] = f
                    arrives("map%d_%d" % (t, q), len(es), [slot(f, t, q)])
    away = [t for t in range(R) if holder(r, t) != r]
    guest = {t: [q for q in range(N) if holder(q, t) == r][0] for t in range(R)}
    for k, t in enumerate(away):
        if t != WHOLE:
            landed("fa%d" % k, k, 0, guest[t])
        landed("ha%d" % k, k, 1, holder(r, t))
    wto, far = (r - LENT) % N, far_engines(r)
    if WHOLE in guest:
        n = len(lanes(guest[WHOLE], r))
        arrives("ta", 3 * n, [V("Tq", 0, 256), V("Tp", 0, 256)])
        arrives("gl", n, [V("gl", 0, 16)])
        arrives("gk", n, [V("gK", 0, 64)])

    def tell(src, land, t, sem, size, doubt=0.0):
        push([(src, [holder(r, t)], land, lanes(r, holder(r, t)), sem)], size, doubt)

    arrives("wa", 3 * len(topo.engines(relay(T, topo, (r + LENT) % N), cores[r])), [V("Wl", 0, 512), V("Wm", 0, 512)])

    dma("s", V("ut", 0, 512), T.u[:], "du", 1.5)
    dma("y", V("Tt", 0, 512), T.x[:, 0:512], "dx0", 1.8)
    dma("y", V("Tt", 512, 1024), T.x[:, 512:1024], "dx1", 2.2)
    dma("y", V("Ws", 0, 512), T.ws[:], "dwa", 2.5)
    dma("y", u8(V("Wq", 0, 256)), T.wc[:, 0:1024], "dwb", 3.0)
    dma("y", u8(V("Wq", 256, 512)), T.wc[:, 1024:2048], "dwc", 3.5)
    dma("y", V("vt", 0, 512), T.v[:], "dv", 4.0)

    cI, cLO, cHI, cS4, cAA, cMU, cAU, cMV, cAV, cM3, cTI, cIL = range(12)
    cSW, cU0, cU1, cV0, cV1, cH1, cD1, cD2, cK, cK1, cK2, cK3, cT0, cT1, cE = range(12, 27)
    cM = cE + 4
    iota(V("pi", 0, 1), [[0, 1]], 0, 1, True)
    iota(V("rowa", 0, 16), [[1, 2], [16, 8]])
    iota(V("pos", 0, 48), [[1, 48]], -8)
    iota(V("Tab", 128, 192), [[0, 16], [4, 4]])
    iota(V("Tab", 4, 16), [[4, 3], [0, 4]])
    iota(V("c1", 0, 256), [[16, 16], [0, 4], [1, 4]], 1)
    iota(V("c1", 3, 256, 4), [[16, 4], [1, 4], [0, 4]], 1)
    iota(V("pos4", 0, 16), [[0, 4], [1, 4]])
    iota(V("AB", 0, 256, 4), [[64, 4], [4, 4], [16, 4]])
    fill(V("ones", 0, 448), 1.0)
    fill(V("ones", 320, 321), 0.0)
    fill(col(cTI), -TINY)
    fill(V("Z", 0, 528), 0.0)
    issue("g", lambda: g.affine_select(T.Z[:, 3:515:4], T.ones[:, 0:128], [[1, 128]], AL.is_equal, 0.0, 0, -1),
          [V("Z", 3, 515, 4)], [V("ones", 0, 128)], cost=0.39, line="g")

    def lend(k):
        src = u8(V("Wq", 256 * k - 256, 256 * k)) if k else V("Ws", 0, 512)
        x = relay(T, topo, r)
        es = topo.engines(cores[r], x)
        issue("g", lambda: g.remote_dma_fused([RemoteDMATransfer(dst_ids=[dst_id(x)], dma_engine_mask=topo.mask(cores[r], x),
                                                                 remote_sem=T.sem["on%d" % k], src=src[0], dsts=[src[0]])],
                                              local_sem=T.sem.sent),
              [], [src], "sent", cost=CALL if k else FIRST, line="g", sends=[([wto], es, 1024 if k else 512, "wa", 3 * DOUBT)])
        total["sent"] = total.get("sent", 0) + len(es)

    def direct(k):
        push([(u8(V("Wq", 256 * k - 256, 256 * k)), [wto], u8(V("Wl", 256 * k - 256, 256 * k)), far, "wa")], 1024)
    lend(0)
    if early(T, topo, r):
        direct(1)
    cp(V("ul", 0, 16), V("rowa", 0, 16))
    ts(V("pi", 1, 2), V("pi", 0, 1), 15, AL.bitwise_and)
    ts(V("pi", 2, 3), V("pi", 0, 1), 3, AL.bitwise_and)
    ts(V("pi", 3, 4), V("pi", 0, 1), 2, AL.arith_shift_right, 3, AL.bitwise_and)
    cp(V("sc", 0, 3), V("pi", 1, 4))
    ts(col(cSW), col(cLO), 4.0, AL.mult, col(cHI), AL.add)
    ts(V("sc", cE, cE + 4), V("pos", 8, 12), col(cHI), AL.is_equal)
    ts(col(cMU), col(cLO), 3.0, AL.is_equal, 0.5, AL.mult)
    ts(col(cMV), col(cI), 15.0, AL.is_equal, 0.5, AL.mult)
    for out, a, scale, bias in (
            (cU1, cLO, 8.0, 8.0), (cU0, cSW, 2.0, 0.0), (cAA, cMV, -512.0, 256.0), (cD2, cMV, -512.0, 256.75),
            (cMU, cMU, 1.0, 0.5 / BIG), (cMV, cMV, 1.0, 0.5 / BIG), (cV0, cHI, 8.0, 0.0), (cV1, cI, 2.0, 2.0),
            (cH1, cHI, 1.0, 1.0), (cM3, cE, 4.0, 0.0), (cS4, cSW, 4.0, 0.0), (cIL, cI, 1.0, -208.0),
            (cT0, cE + 3, 92.0, -128.0), (cT0, cHI, 16.0, cT0), (cD1, cLO, 1.0, cT0),
            (cT1, cE + 3, 256.0, -256.0), (cT1, cHI, -3.0, cT1), (cK, cLO, 3.0, cT1),
            (cK1, cI, 1.0, 16.0), (cK2, cI, 1.0, 32.5), (cK3, cI, 1.0, 48.5),
            (cM, cE, 0.25, 0.0), (cM + 1, cE, -127.0, 255.0), (cM + 2, cE + 1, 0.25, 0.0), (cM + 3, cE + 1, -127.0, 255.0),
            (cM + 4, cE + 2, 4.0, 0.0), (cM + 5, cE + 3, -192.0, 192.0), (cM + 5, cE + 2, -64.0, cM + 5)):
        affine(col(out), col(a), scale, bias if isinstance(bias, float) else col(bias))
    iota(V("XI", 0, 64), [[16, 4], [0, 16]])
    for k in range(3):
        row = V("XI", 0, 64) if k < 2 else V("pos4", 0, 16)
        affine(V("MM", 64 * k, 64 * k + row[2]), row, col(cM + 2 * k), col(cM + 2 * k + 1))

    def horner(name, start, stop, o, mu, au):
        p, a, b, c = V("pos", 8, 40), V("tmp", o, o + 32), V("tmp", o + 32, o + 64), V("tmp", o + 64, o + 96)
        ts(a, p, stop, AL.is_lt, 1.0, AL.add)
        ts(b, p, start, AL.not_equal)
        ts(c, p, stop, AL.is_equal, BIG, AL.mult)
        tt(a, a, b, AL.mult)
        tt(V(name, 0, 32), a, c, AL.max)
        tt(V(name, 32, 64), a, c, AL.max)
        double(name, 64, 256)
        scan(V("su", o, o + 32), V(name, 0, 32), V("ones", 0, 32), AL.mult, AL.add)
        ts(au, V("su", o + 31, o + 32), mu, AL.mult)

    def marks(name, a, sa, b, sb, at, n):
        ts(V("tmp", at, at + 16), a, sa, AL.is_equal, 512.0, AL.mult)
        ts(V("tmp", at + 16, at + 32), b, sb, AL.is_equal, 256.0, AL.mult)
        for k in range(2):
            tt(V(name, 16 * k, 16 * k + 16), V("tmp", at, at + 16), V("tmp", at + 16, at + 32), AL.subtract)
        double(name, 32, n)

    horner("PU", col(cU0), col(cU1), 0, col(cMU), col(cAU))
    marks("PA", V("pos", 8, 24), col(cI), V("pos", 7, 23), col(cI), 288, 256)
    marks("PB", V("pos", 8, 24), col(cSW), V("pos", 7, 23), col(cSW), 256, 64)
    marks("PC", V("pos4", 0, 16), col(cHI), V("pos4", 0, 16), col(cH1), 320, 256)
    horner("PV", col(cV0), col(cV1), 128, col(cMV), col(cAV))
    sfill("Tab", 192, 256, 1, 0)
    sfill("Tab", 32, 48, 1, 0)
    sfill("Tab", 48, 64, 1, 4)
    cp(V("Tab", 0, 4), V("Tab", 128, 132), "s")
    cp(V("Tab", 16, 32), V("Tab", 128, 144), "s")
    for k in range(4):
        cp(V("Tab", 64 + 16 * k, 80 + 16 * k), V("Tab", 0, 16), "s")
    quant("uq", "us", 0, 128, V("ut", 0, 512))
    pa, pb, po = V("Uq", 0, 256), V("uq", 0, 128), V("ul", 0, 16)
    issue("v", lambda: g.vector.tensor_copy(pa[0].bitcast(dt.uint32), pb[0].bitcast(dt.uint32).indirect(po[0])),
          [pa], [pb, po], cost=0.38)
    cp(V("Us", 0, 256), ind(V("us", 0, 128), V("ul", 0, 16)), "s")
    ts(V("Fl", 0, 4), V("pos", 8, 12), 64.0, AL.mult, col(cS4), AL.add)
    ts(V("Kl", 0, 4), V("pos", 8, 12), 4.0, AL.mult, col(cLO), AL.add)
    affine(V("lc", 0, 16), V("pos", 8, 24), 16.0, col(cI))
    cp(V("BB", 0, 64, 4), V("pos", 8, 24), "s", 4.0)
    for b in range(4):
        quant("Eq", "Es", 128 * b, 128, V("Z", 3 - b, 515 - b))
    for name, lo, hi in (("RR", 0, 384), ("RR", 384, 768), ("QQ", 0, 192), ("L3", 0, 240), ("L3", 240, 480), ("L4", 0, 272),
                         ("FH", 0, 256), ("FH", 256, 512), ("Flg", 0, 192), ("Flg", 256, 448)):
        fill(V(name, lo, hi), 0.0)
    fill(V("Hd", 0, 320, 80), 0.0)
    cp(V("e0", 0, 1), col(cI))
    for k in range(len(away)):
        quant("Lq", "Ls", 640 * k + 256, 128, V("FH", 0, 512))
    quant("vq", "vs", 0, 128, V("vt", 0, 512))
    for args in ((192, 256, 1), (256, 320, 4), (320, 385, 16), (400, 416, 4), (416, 432, 1)):
        sfill("Flg", *args, 1)
    for k in range(4):
        sfill("Flg", 324 + k, 400, 16, 1)

    def count(c, lo, hi, at):
        o, s, k, bias = V("junk", at, at + hi - lo), V("sa", c, c + 1), V("K1", lo, hi), col(cK3 if c == 3 else cK2)
        issue("s", lambda: g.scalar.activation(o[0], k[0], AF.Sign, bias=bias[0], scale=-1.0, accum_out=s[0]), [o, s], [k, bias])

    def starts(keys, at):
        me = ts(V("key", 0, 16), ind(keys, at), -16.0, AL.mult, 192.0, AL.add)
        for h in range(2):
            cp(V("m", 128 * h, 128 * h + 128), ind(V("Flg", 0, 448), V("key", 8 * h, 8 * h + 8)), "vs"[h])
        scan(V("K1", 0, 256), V("ones", 0, 256), V("m", 0, 256), AL.mult, AL.add)
        return me

    def firsts(out):
        count(3, 48, 256, 0)
        count(2, 32, 192, 208)
        ts(V("le", 64, 192), V("K1", 0, 128), col(cK1), AL.is_le, f=0.5)
        ts(V("le", 0, 64), V("K1", 0, 64), col(cI), AL.is_le)
        scan(V("ls", 0, 192), V("ones", 256, 448), V("le", 0, 192), AL.mult, AL.add)
        ts(V(out, 3, 4), V("sa", 3, 4), 0.5, AL.mult, 152.0, AL.add)
        cp(V(out, 0, 2), V("ls", 63, 192, 128))
        ts(V(out, 2, 3), V("sa", 2, 3), 0.5, AL.mult, 112.0, AL.add)

    def send_map(t, soon):
        plan = [(f, [p for p in to if (r < maker(p, t)) == soon], es) for f, to, es in map_plan(r, t)]
        parts = [(V(f, 16 * t, 16 * t + 4), to, slot(f, t, r), es, "map%d_%d" % (t, r)) for f, to, es in plan if to]
        if parts:
            push(parts, 8, 0.0 if soon else DOUBT)

    def unpack(q, s, lo):
        for b in range(4):
            mm(2 + b, 256, "Eq", "Es", 128 * b, q, s, lo)
            for x in (0, 128):
                cp(V("Vh", 256 * b + x, 256 * b + x + 128), bank(2 + b, 128, x), "s", 1.0, "V")

    def update(lo, hi, bs):
        for b in bs:
            w = V("Tt", 64 * lo + b, 64 * hi, 4)
            tt(w, ind(V("Hd", 80 * b, 80 * b + 65), V("kl", lo, hi)), w, AL.add, "T")

    for t in range(R):
        qh, qt, qf = 512 * t, 512 * t + 128, 512 * t + 384
        for h in range(2):
            if t and h:
                update(8, 16, [3])
            quant("Sq", "Ss", qt + 128 * h, 128, V("Tt", 512 * h, 512 * h + 512), "T")
            for b in (1, 0):
                mm(6 * h + b, 128, "Uq", "Us", 128 * b, "Sq", "Ss", qt + 128 * h)
                affine(V("bits", 256 * h + 1 - b, 256 * h + 256, 2), bank(6 * h + b, 128), 1.0, col(cTI), AF.Sign)
            scan(V("su", 256 * h, 256 * h + 256), V("PU", 0, 256), V("bits", 256 * h, 256 * h + 256), AL.mult, AL.add)
            ts(V("cod", 8 * h, 8 * h + 8), V("su", 256 * h + 31, 256 * h + 256, 32), col(cMU), AL.mult, col(cAU), AL.add)
            tt(V("N1", 128 * h, 128 * h + 128), ind(V("Tab", 0, 256), V("cod", 8 * h, 8 * h + 8)), V("c1", 128 * h, 128 * h + 128), AL.add)
        if t == WHOLE:
            x, a, b = relay(T, topo, r), u8(V("Sq", qt, qt + 128)), u8(V("Sq", qt + 128, qt + 256))
            rest = [e for e in topo.engines(cores[r], x) if e not in far]
            issue("g", lambda x=x, a=a, b=b, rest=rest, to=holder(r, t): g.remote_dma_fused([
                RemoteDMATransfer(dst_ids=[dst_id(c)], dma_engine_mask=sum(1 << e for e in es), remote_sem=T.sem[sem], src=src[0],
                                  dsts=[u8(V("Tq", lo, lo + 128))[0]])
                for c, es, sem, src, lo in ((x, rest, "on3", a, 0), (cores[to], far, "ta", b, 128))], local_sem=T.sem.sent),
                [], [a, b], "sent", cost=CALL, line="g",
                sends=[([holder(r, t)], rest, 512, "ta", 2 * DOUBT), ([holder(r, t)], far, 512, "ta", 0.0)])
            total["sent"] += len(rest) + len(far)
            tell(V("Ss", qt, qt + 256), V("Tp", 0, 256), t, "ta", 256, DOUBT)
        unpack(*(("Tq", "Tp", 0) if t == WHOLE else ("Sq", "Ss", qt)))
        for h in range(2):
            scan(V("sv", 256 * h, 256 * h + 256), V("PV", 0, 256), V("bits", 256 * h, 256 * h + 256), AL.mult, AL.add)
        ts(V("kd", 0, 16), V("sv", 31, 512, 32), col(cMV), AL.mult, col(cAV), AL.add)
        ts(V("kd", 16, 32), V("kd", 0, 16), 3, AL.bitwise_and)
        ts(V("kd", 32, 48), V("kd", 0, 16), 252, AL.bitwise_and)
        tt(V("lf", 0, 16), V("kd", 16, 32), V("lc", 0, 16), AL.add)
        ts(V("ll", 0, 16), V("lf", 0, 16), 255.0, AL.min)
        ts(V("ck", 16, 32), V("kd", 32, 48), 1.0 / 64, AL.mult, col(cK), AL.add)
        tt(V("ck", 0, 16), V("ck", 16, 32), V("lc", 0, 16), AL.add)
        if t == WHOLE:
            tell(V("ll", 0, 16), V("gl", 0, 16), t, "gl", 32)
        for u in (2, 1, 0):
            pickup(V("s1", 64 * u, 64 * u + 64), V("PA" if u else "PB", 0, 64), V("N1", u, 256, 4))
        ts(V("W1", 8, 12), V("s1", 143, 192, 16), col(cAA), AL.add)
        ts(V("W1", 0, 8), V("s1", 15, 128, 16), col(cAA), AL.add)
        cp(V("RR", 2, 256, 4), ind(V("N1", 0, 256), V("W1", 8, 12)))
        cp(V("RR", 257, 512, 4), ind(V("RR", 0, 256), V("W1", 4, 8)))
        cp(V("Rb", 0, 64), ind(V("RR", 256, 512), V("W1", 0, 4)))
        cp(V("RR", 513, 768, 4), ind(V("N1", 0, 256), V("W1", 4, 8)), "s")
        cp(V("AB", 1, 256, 4), ind(V("N1", 0, 256), V("Fl", 0, 4)), "s")
        cp(V("AB", 2, 256, 4), ind(V("N1", 0, 256), V("W1", 0, 4)), "s")
        cp(V("AB", 3, 256, 4), ind(V("RR", 512, 768), V("W1", 0, 4)), "s")
        for v in (2, 1, 0):
            pickup(V("s2", 16 * v, 16 * v + 16), V("PA", 0, 16), V("Rb", v, 64, 4))
        ts(V("W2", 4, 5), V("s2", 47, 48), col(cAA), AL.add)
        ts(V("W2", 0, 4, 2), V("s2", 15, 32, 16), col(cAA), AL.add)
        cp(V("QQ", 2, 64, 4), ind(V("Rb", 0, 64), V("W2", 4, 5)))
        cp(V("QQ", 65, 128, 4), ind(V("QQ", 0, 64), V("W2", 2, 3)))
        ts(V("Wc", 0, 16), ind(V("QQ", 64, 128), V("W2", 0, 1)), 4.0, AL.mult)
        if r < N - 1:
            cp(V("L3", 0, 256, 16), ind(V("QQ", 64, 128), V("W2", 0, 1)), "s")
        cp(V("QQ", 129, 192, 4), ind(V("Rb", 0, 64), V("W2", 2, 3)), "s")
        cp(V("BB", 1, 64, 4), V("Rb", 0, 64, 4), "s")
        cp(V("BB", 2, 64, 4), ind(V("Rb", 0, 64), V("W2", 0, 1)), "s")
        cp(V("BB", 3, 64, 4), ind(V("QQ", 128, 192), V("W2", 0, 1)), "s")
        if r < N - 1:
            cp(V("L3", 336, 400), ind(V("L3", 48, 256), V("Wc", 8, 12)))
            pickup(V("s3", 0, 16), V("PA", 0, 16), V("L3", 0, 256, 16))
            cp(V("L3", 416, 480), ind(V("L3", 256, 400), V("Wc", 4, 8)))
            ts(V("W0", 0, 1), V("s3", 15, 16), col(cAA), AL.add, col(cM3), AL.mult)
        last = ind(V("L3", 400, 480), V("W0", 0, 1))
        c = maker(r, t)
        for f in sorted({f for f, to, es in map_plan(r, t)} | ({form(r, c, t)} if r < c else set())):
            o = V(f, 16 * t, 16 * t + 16)
            if f == "ml":
                ts(o, last, 4.0, AL.mult, col(cIL), AL.add)
            elif f == "me":
                ts(o, last, 0.25, AL.mult, -13.0, AL.add)
            else:
                cp(o, last, "s")
        send_map(t, True)
        if t == 0 and early(T, topo, r):
            direct(2)
        elif t == 0:
            lend(1)
            lend(2)
        pickup(V("s6", 0, 256), V("PC", 0, 256), V("AB", 0, 256))
        cp(V("cx", 0, 64), ind(V("ck", 0, 16), V("Kl", 0, 4)), "s")
        pickup(V("s5", 0, 64), V("PA", 0, 64), V("BB", 0, 64))
        ts(V("D2", 0, 4), V("s5", 15, 64, 16), col(cD2), AL.add, 4.0, AL.mult)
        tt(V("Kq", 0, 64), ind(V("s6", 0, 256), V("D2", 0, 4)), V("cx", 0, 64), AL.subtract)
        tt(V("L4", 0, 256, 16), ind(V("QQ", 64, 128), V("W2", 0, 1)), V("MM", 128, 144), AL.max)
        tt(V("L4", 272, 336), ind(V("L4", 48, 256), V("Wc", 4, 8)), V("MM", 64, 128), AL.min)
        tt(V("L4", 352, 416), ind(V("L4", 256, 336), V("Wc", 0, 4)), V("MM", 0, 64), AL.min)
        ts(V("D1", 0, 4), V("L4", 352, 416, 16), col(cD1), AL.add)
        cp(V("XX", 0, 64), ind(V("Kq", 0, 64), V("D1", 0, 4)))
        if t == WHOLE:
            tell(V("XX", 0, 64), V("gK", 0, 64), t, "gk", 128)
            send_map(t, False)
        for b in range(4):
            for h in range(2):
                lo = 256 * b + 128 * h
                cp(V("Vg", lo, lo + 128), ind(V("Vh", 256 * b, 256 * b + 256), V("gl" if t == WHOLE else "ll", 8 * h, 8 * h + 8)), "s", 1.0, "L")
                tt(V("G", lo, lo + 128), bank(2 + b, 128, 128 * h), V("Vg", lo, lo + 128), AL.add, "G", 1.0)
        x, xx = 0, "XI" if t == WHOLE else "XX"
        for q in range(c - 1, ahead(c, t) - 1, -1):
            cp(V(xx, x + 64, x + 128), ind(V(xx, x, x + 64), slot("ml", t, q, q == r)), "s")
            x += 64
        at = slot(form(0, c, t), t, 0, r == 0, 1) if c else V("e0", 0, 1)
        for q in range(1, min(ahead(c, t), c)):
            src, o = ind(slot("mw", t, q, q == r), at), V("ch", 16 * q, 16 * q + 16)
            if q < ahead(c, t) - 1:
                ts(o, src, 0.25, AL.mult, -13.0, AL.add)
            else:
                ts(o, src, 4.0, AL.mult, col(cIL), AL.add)
            at = V("ch", 16 * q, 16 * q + 1)
        keys = V("XX", x, x + 64)
        if t == WHOLE:
            keys = V("gK", 0, 64)
            if c == 1:
                ts(V("ch", 0, 1), at, 16.0, AL.mult, col(cI), AL.add)
            elif x:
                ts(V("ch", 0, 16), ind(V("XI", x, x + 64), at), col(cI), AL.add)
            at = V("ch", 0, 1) if c == 1 or x else at
        keyed = starts(keys, at)
        firsts("sl")
        for b in range(4):
            cp(V("FH", b, 256, 4), ind(V("G", 256 * b, 256 * b + 256), V("sl", 0, 4)), "vs"[b % 2], 0.5)
        made = len(ops) - 1
        quant("Sq", "Ss", qf, 128, V("FH", 0, 512))
        k = away.index(t) if t in away else None
        if k is not None and t != WHOLE:
            send_tile(qf, holder(r, t), k, 0, "fa%d" % k)
        wq, ws = ("Wq", "Ws") if (guest[t] + HOP[t]) % N == r else ("Wl", "Wm")
        for b in range(4):
            if k is None or t == WHOLE:
                mm(2 + b, 128, wq, ws, 128 * b, "Sq", "Ss", qf)
            else:
                mm(2 + b, 128, wq, ws, 128 * b, "Lq", "Ls", 640 * k + 192)
        if t == WHOLE:
            at = V("ML", 64 * t, 64 * t + 1)
            hold.append(keyed)
            for q in range(1, r):
                o = V("ce", 16 * q, 16 * q + 16)
                if came[t, q] == "mw":
                    ts(o, ind(slot("mw", t, q), at), 0.25, AL.mult, -13.0, AL.add)
                else:
                    cp(V("cw", 8 * q, 8 * q + 4), slot("ml", t, q))
                    ts(o, ind(V("cw", 8 * q, 8 * q + 4), at), col(cI), AL.subtract, 1.0 / 16, AL.mult)
                at = V("ce", 16 * q, 16 * q + 1)
            if r:
                ts(V("ce", 0, 1), at, 16.0, AL.mult, col(cI), AL.add)
            hold.append(made)
            starts(V("XX", 0, 64), V("ce" if r else "e0", 0, 1))
            hold.clear()
        pickup(V("s9", 0, 256), V("PA", 0, 256), V("K1", 0, 256))
        ts(V("ka", 0, 16), V("s9", 15, 256, 16), col(cAA), AL.add, -1.0, AL.add)
        ts(V("kb", 0, 16), V("ka", 0, 16), 63, AL.bitwise_and)
        tt(V("kc", 0, 16), V("ka", 0, 16), V("kb", 0, 16), AL.min)
        ts(V("kl", 0, 16), V("kc", 0, 16), 1.0, AL.add)
        for b in range(4):
            cp(V("FH", 512 + b, 768, 4), bank(2 + b, 64), "sv"[b % 2], 0.03125)
        quant("Sq", "Ss", qh, 128, V("FH", 256, 768))
        if t == WHOLE:
            hold.append(len(ops) - 1)
            firsts("sf")
            hold.clear()
        if k is not None:
            send_tile(qh + 64, guest[t], k, 1, "ha%d" % k)
        banks = (0, 1, 6, 7)
        for b in range(4):
            if k is None:
                mm(banks[b], 128, "Eq", "Es", 128 * b, "Sq", "Ss", qh)
            else:
                mm(banks[b], 128, "Eq", "Es", 128 * b, "Lq", "Ls", 640 * k + 320)
            cp(V("Hd", 80 * b + 1, 80 * b + 65), bank(banks[b], 64, 64), "s" if b else "v")
        if t == R - 1:
            if t != WHOLE:
                cp(V("sf", 0, 4), V("sl", 0, 4))
            for j in range(4):
                dma("y", T.ol[:, 16 * j:16 * j + 16], V("sf", j, j + 1), "oy", behind=[V("Hd", 1, 2)])
        else:
            update(0, 16, [0, 1])
            update(0, 8, [2, 3])
            update(8, 16, [2])
    qt = 512 * R + 128
    update(0, 8, range(4))
    update(8, 16, [0])
    for h in range(2):
        lo = qt + 128 * h
        if h:
            update(8, 16, [1, 2, 3])
        quant("Sq", "Ss", lo, 128, V("Tt", 512 * h, 512 * h + 512), "T")
        mm(2 + h, 128, "vq", "vs", 0, "Sq", "Ss", lo)
        dma("y", T.oc[:, 512 * h:512 * h + 512], u8(V("Sq", lo, lo + 128)), "oy")
        cp(V("ys", 128 * h, 128 * h + 128), bank(2 + h, 128), "s")
        if h:
            for k in range(4):
                src = (T.Ss[32 * k:32 * k + 4, qt:qt + 256], V("Ss", qt, qt + 256)[1], 256, 0)
                dma("y", T.osc[4 * k:4 * k + 4, :], src, "oy")
        dma("y", T.y[:, 128 * h:128 * h + 128], V("ys", 128 * h, 128 * h + 128), "oy")
    return ops, emit, total
